import numpy as np, ml_dtypes
CORES = [13,21,141,149]
N = 4
BF = ml_dtypes.bfloat16
def gentries(a):
    return np.ascontiguousarray(a.reshape(8, 16, -1).transpose(0, 2, 1)).reshape(8, -1)
def gtable(e):
    e = np.asarray(e); return np.ascontiguousarray(e.reshape(8, -1, 16).transpose(0, 2, 1)).reshape(128, -1).astype(np.int32)
S, G, CAP, WN, M, Q, RO, H, T0 = 1792, 384, 32, 160, 512, 2048, 4, 3, 192
W, L = S + (N - 1) * G, (N - 1) * CAP + WN
def lines(rng, n):
    base = rng.integers(0, 256, (N, 8, 1, n)); amp = rng.choice(np.array([0.0, 2.0, 12.0, 50.0]), (N, 8, 1, n))
    return np.clip(np.rint(base + amp * rng.standard_normal((N, 8, 15, n))), 0, 255).astype(np.int64)
def parts(rng):
    st = np.where(rng.random((N, 8, S)) < rng.choice(np.array([0.3, 0.45, 0.6]), (N, 8, 1)), -1, rng.integers(0, T0, (N, 8, S)))
    x = np.concatenate([lines(rng, S), st[:, :, None, :]], axis=2)
    order = np.argsort(st, axis=-1, kind="stable"); pos = np.argsort(order, axis=-1)
    span = rng.choice(np.array([4, 32, 300]), (N, 8, 1, S))
    at = np.clip(pos[:, :, None, :] + (span * (rng.random((N, 8, 16, S)) * 4 - 3)).astype(np.int64), 0, S - 1)
    nb = np.take_along_axis(order[:, :, None, :], at, 3)
    gh = rng.random((N, 8, 16, S)) < rng.choice(np.array([0.01, 0.03, 0.08]), (N, 8, 1, 1))
    nb = np.where(gh, rng.integers(S, W, (N, 8, 16, S)), nb)
    pl = np.concatenate([lines(rng, M), rng.integers(0, 256, (N, 8, 1, M))], axis=2); w = rng.integers(0, 256, (N, 8, 16, 1))
    none = np.sum(st < 0, axis=-1)[:, :, None]; k = np.minimum(none + (rng.random((N, 8, RO * WN)) * (S - none)).astype(np.int64), S - 1)
    wl = np.take_along_axis(order, k, 2); wl = np.where(rng.random(wl.shape) < 0.1, rng.integers(0, S, wl.shape), wl).reshape(N, 8, RO, WN)
    return x, nb, pl, w, wl, rng.integers(0, S, (N, 8, N - 1, G))
def pack(x, nb, pl, w, wl, sl):
    return {"x0": x.reshape(N, 128, S).astype(np.float32).astype(BF), "nb": np.ascontiguousarray(nb.reshape(N, 128, S)).astype(np.int32),
            "pull": pl.reshape(N, 128, M).astype(np.float32).astype(BF), "wt": w.reshape(N, 128, 1).astype(np.int32),
            "wants": np.stack([gtable(a.reshape(8, -1)) for a in wl]), "snd": np.stack([gtable(a.reshape(8, -1)) for a in sl])}
def aim(bl, lo):
    place = np.array([np.sum(bl[:i] == bl[i]) for i in range(len(bl))])
    return S + bl * G + lo + place % CAP
def brim(rng, x, nb, w, wl, sl, g):
    K = (N - 1) * CAP; w[:, g] = 0; w[:, g, 0] = 16; w[:, g, 1] = 1
    for r in range(N):
        zs = rng.permutation(Q); h = ((zs * zs >> 5) + 194) & (Q - 1)
        u, i = np.unique(np.where(h >= S, h - S, h), return_index=True)
        p = rng.permutation(np.nonzero(u)[0])[:L]; z = zs[i[p]]
        o = rng.permutation(np.setdiff1d(np.arange(1, S), u[p]))[:3 * WN + 2 * K]
        o[2 * WN + K + int(rng.integers(0, K))] = 0
        one, two, asked, late, last = np.split(o, [WN, 2 * WN, 2 * WN + K, 2 * WN + 2 * K])
        x[r, g, 15, u[p]] = -1
        for q, k in ((one, 0), (two, 0), (asked, 1), (late, 2)):
            x[r, g, 2, q] = 100 * k + rng.integers(0, 50, len(q)); x[r, g, 3, q] = 250 - 100 * k - rng.integers(0, 50, len(q))
            x[r, g, 15, q] = 60 * k + rng.integers(0, 50, len(q))
        end = np.concatenate([late, last]); x[r, g, 0, end] = z >> 4; x[r, g, 1, end] = z & 15
        x[r, g, 15, last] = rng.integers(0, T0, WN)
        nb[r, g][:, o] = o
        sl[r, g, :, :CAP] = asked.reshape(N - 1, CAP); sl[r, g, :, G - CAP:] = late.reshape(N - 1, CAP)
        bl = np.concatenate([rng.permutation(np.repeat(np.arange(N - 1), CAP)), rng.integers(0, N - 1, WN - K)])
        nb[r, g][rng.integers(0, 16, WN), one] = aim(bl, 0)
        b = int(rng.integers(0, N - 1)); bl = rng.permutation(np.arange(L - CAP) % (N - 2))
        bl = np.concatenate([bl + (bl >= b), np.full(CAP, b)])
        nb[r, g][rng.integers(0, 16, L), np.concatenate([asked, two])] = aim(bl, G - CAP)
        wl[r, g, 0] = one; wl[r, g, 1] = two; wl[r, g, 2] = last
def setup_inputs(rng):
    return pack(*parts(rng))
def setup_inputs_room(rng):
    x, nb, pl, w, wl, sl = parts(rng); k = S // 8
    for r in range(N):
        for g in range(8):
            o = rng.permutation(S); a, b, c, e = o[:k], o[k:2 * k], o[2 * k:3 * k], o[3 * k:]
            x[r, g, 15, a] = T0 - 1; x[r, g, 0, a] = 255; x[r, g, 1, a] = 0
            x[r, g, 15, b] = 0; x[r, g, 0, b] = rng.integers(0, 255, k); x[r, g, 1, b] = rng.integers(1, 256, k)
            x[r, g, 15, c] = rng.integers(0, T0, k); x[r, g, 15, e] = -1
            for q in (a[:k // 2], b, c): nb[r, g][:, q] = q
            sl[r, g] = a[rng.integers(0, k, (N - 1, G))]
            n = rng.choice(np.array([0, 1, CAP - 1, CAP, CAP + 1]), N - 1)
            if r == 0: n[0] = (CAP, CAP + 1, CAP - 1, 0, 1, CAP + 9, CAP, CAP + 1)[g]
            else: n[rng.integers(0, N - 1)] = CAP + 9
            to = np.concatenate([S + j * G + rng.integers(0, G, int(n[j])) for j in range(N - 1)])
            go = rng.permutation(b)[:len(to)]; nb[r, g][rng.integers(0, 16, len(to)), go] = to
            wl[r, g, 0] = rng.permutation(np.concatenate([go, rng.permutation(c)[:WN - len(to)]]))
    brim(rng, x, nb, w, wl, sl, 6)
    return pack(x, nb, pl, w, wl, sl)
def setup_inputs_ties(rng):
    x, nb, pl, w, wl, sl = parts(rng); n = (N, 8, 1, S); row = np.arange(15)[:, None]
    p = 100 + (row == rng.integers(0, 22, n)).astype(np.int64) - (row == rng.integers(0, 22, n)) + (rng.random(n) < 0.1)
    x = np.concatenate([p, rng.choice(np.array([-1, -1, -1, 0, 1, 2, T0 - 2, T0 - 1]), n)], axis=2); x[:, :, 15, ::S - 1] = 0
    wl[:, :, :, 0] = 0; wl[:, :, :, 1] = S - 1; nb[:, 1::2, 8:] = nb[:, 1::2, :8]
    return pack(x, nb, pl, w, wl, sl)
def setup_inputs_crowd(rng):
    x, nb, pl, w, wl, sl = parts(rng)
    x[:, :4, :15] = np.take_along_axis(x[:, :4, :15], rng.integers(0, 8, (N, 4, 1, S)), 3)
    nb = np.where(rng.random((N, 8, 1, S)) < 0.6, np.arange(S), nb)
    w[:, 5] = 0; x[:, 5, 15][:, 97 * np.arange(RO)] = -1
    ts, zs = np.nonzero((((np.arange(Q) ** 2 >> 5) + 97 * np.arange(RO)[:, None]) & (Q - 1)) == S)
    t = int(ts[0]); z = int(zs[rng.integers(0, int(np.sum(ts == t)))])
    w[:, 7] = 0; w[:, 7, 0] = z >> 4; w[:, 7, 1] = 1
    for r in range(N):
        for g in (0, 2, 4, 6):
            few = np.concatenate([np.array([0, S - 1]), rng.integers(0, S, 10)])
            x[r, g, 15, few] = T0 - 1; nb[r, g][:, few] = few; wl[r, g] = few[rng.integers(0, 12, (RO, WN))]
        half = 1 + rng.permutation(S - 1)[:S // 2]; few = half[:8]
        x[r, 7, 0, half] = 16; x[r, 7, 1, half] = z & 15; x[r, 7, 15, 0] = -1
        x[r, 7, 15, few] = T0 - 1; nb[r, 7][:, few] = few; wl[r, 7, t, :8] = few
    return pack(x, nb, pl, w, wl, sl)
def setup_inputs_bare(rng):
    x, nb, pl, w, wl, sl = parts(rng); q = rng.permutation(N); g = rng.permutation(8)
    x[:, g[0], 15] = -1; v = x[:, g[1], 15]; x[:, g[1], 15] = np.where(v < 0, rng.integers(0, T0, v.shape), v)
    nb[:, g[3]] = rng.choice(np.array([0, S - 1, S, W - 1]), (N, 16, S)); sl[:, g[2]] = rng.choice(np.array([0, S - 1, S // 2, 3]), (N, N - 1, G))
    nb[q[0]] = rng.integers(S, W, (8, 16, S)); nb[q[1]] = rng.integers(0, S, (8, 16, S))
    return pack(x, nb, pl, w, wl, sl)
def setup_inputs_spread(rng):
    x, nb, pl, w, wl, sl = parts(rng)
    p = np.minimum((np.exp2(8 * rng.random((N, 8, 1, S))) * rng.random((N, 8, 15, S))).astype(np.int64), 255)
    st = np.minimum(np.exp2(7.6 * rng.random((N, 8, 1, S))).astype(np.int64) - 1, T0 - 1)
    st = np.where(rng.random((N, 8, 1, S)) < rng.choice(np.array([0.1, 0.4, 0.8]), (N, 8, 1, 1)), -1, st)
    w = np.minimum(np.exp2(8 * rng.random((N, 8, 16, 1))).astype(np.int64), 255)
    pl = np.minimum((np.exp2(8 * rng.random((N, 8, 1, M))) * rng.random((N, 8, 16, M))).astype(np.int64), 255)
    nb = np.where(rng.random((N, 8, 1, S)) < 0.5, rng.integers(0, W, nb.shape), nb)
    return pack(np.concatenate([p, st], axis=2), nb, pl, w, rng.integers(0, S, wl.shape), sl)
def check_inputs(d):
    bad = []
    v = np.asarray(d["x0"]).astype(np.float32).reshape(N, 8, 16, S)
    for k, a, lo, hi in (("paths of x0", v[:, :, :15], 0, 255), ("stamps of x0", v[:, :, 15], -1, T0 - 1), ("pull", np.asarray(d["pull"]).astype(np.float32), 0, 255), ("wt", d["wt"], 0, 255),
                         ("nb", d["nb"], 0, W - 1), ("wants", d["wants"], 0, S - 1), ("snd", d["snd"], 0, S - 1)):
        if not np.all((a >= lo) & (a <= hi) & (a == np.floor(a))): bad.append("range of " + k)
    return bad
def reference(x0, nb, pull, wt, wants, snd):
    x = x0.astype(np.float32).astype(np.int64).reshape(N, 8, 16, S); nbr = nb.astype(np.int64).reshape(N, 8, 16, S)
    pl = pull.astype(np.float32).astype(np.int64).reshape(N, 8, 16, M); w = wt.astype(np.int64).reshape(N, 8, 1, 16)[..., :15]
    wl = np.stack([gentries(a) for a in wants]).astype(np.int64).reshape(N, 8, RO, WN); sl = np.stack([gentries(a) for a in snd]).astype(np.int64).reshape(N, 8, N - 1, G)
    gi = np.arange(8)[:, None]; g3 = gi[:, :, None]; lane = np.arange(L)
    req = np.full((N, 8, N - 1, CAP), -1, np.int64)
    for t in range(RO):
        new = x.copy(); ask = np.full((N, 8, N - 1, CAP), -1, np.int64)
        for r in range(N):
            f = np.concatenate([x[r]] + [np.take_along_axis(x[(r - e) % N], sl[(r - e) % N, :, e - 1][:, None, :], 2) for e in range(1, N)], axis=2)
            s = np.concatenate([req[r].reshape(8, -1), wl[r, :, t]], axis=1)
            climb = s >= 0; s = np.maximum(s, 0); climb = climb & (f[gi, 15, s] >= 0); done = np.zeros((8, L), bool)
            for h in range(H):
                c = nbr[r][g3, np.arange(16), np.minimum(s, S - 1)[:, :, None]]
                a = f[g3, :, c]; b = f[gi, :, s][:, :, None, :]
                cov = (a[..., 15] > b[..., 15]) & np.any(a[..., :15] > b[..., :15], axis=3) & np.any(a[..., :15] < b[..., :15], axis=3)
                may = climb & (s < S); cov = cov & may[:, :, None]
                best = np.argmax(np.where(cov, a[..., 15], -1), axis=2)
                hit = np.any(cov, axis=2); done = done | (may & ~hit); climb = climb & hit
                s = np.where(hit, np.take_along_axis(c, best[:, :, None], 2)[:, :, 0], s)
            for e in range(1, N):
                q = (r - e) % N; k = s - S - (e - 1) * G; on = ((k >= 0) & (k < G)).astype(np.int64)
                before = np.add.accumulate(on, axis=1) - on; gs, ls = np.nonzero((on == 1) & (before < CAP))
                ask[q, gs, e - 1, before[gs, ls]] = sl[q, gs, e - 1, k[gs, ls]]
            v = f[gi, :, s]
            z = np.sum(v[:, :, :15] * w[r], axis=2) & (Q - 1); d = ((z * z >> 5) + 97 * t) & (Q - 1); d = np.where(d >= S, d - S, d)
            ok = done & (f[gi, 15, d] < 0); gs, ls = np.nonzero(ok)
            first = np.full((8, S), L, np.int64); np.minimum.at(first, (gs, d[gs, ls]), ls)
            gs, ls = np.nonzero(ok & (first[gi, d] == lane)); dd = d[gs, ls]
            new[r][gs, :15, dd] = (v[gs, ls, :15] + pl[r][gs, :15, dd & (M - 1)]) >> 1
            new[r][gs, 15, dd] = T0 + t; new[r][gs, 15, s[gs, ls]] = -1
        x = new; req = ask
    return {"y": x.reshape(N, 128, S).astype(np.float32).astype(BF)}

@@ -1,0 +1,633 @@
+from concourse.mybir import AluOpType, ActivationFunctionType
+
+S, GH, CAP, RO = 1792, 384, 32, 4
+NULL, WX, TRASH = 2944, 2960, 3072
+VL = 64
+V16 = 16 * VL
+OP = AluOpType
+AF = ActivationFunctionType
+SIZES = {
+    "bfloat16": "XT 3584,EIN 2960,PUL 512,ZSA 2048,ZSB 2048,MSK 1024,SBA 1024,SBB 1024,DA 2048,DB 2048,NA 2048,NB 2048,EXP 1024,"
+                "ONE 1024,EQ 4096,PRB 1024,IDB 128,IDN 128,EMP 128,EMN 128,GM 128,GM2 128,RD 16,RN 16,RS 384,WZ 16,DQ 256,SZA 128,"
+                "SZB 128,STA 128,STB 128,XD 256,VAL 512,STL 24,RW 192,LB 16,IND 256,CNT 256,QC 256,GS 4608,LG 4608,RG 1536,YO 1792,"
+                "REB 128",
+    "float32": "NBF 2960,IOT 2960,GST 2960,REQ 2320,PRF 1024,IDF 128,WM 192,COL 64,GG 64,TMF 256,TM2 512,TRS 32,BSA 128,"
+               "BSB 128,TAA 128,TAB 128,MA 256,MB 256,RA 128,RB 128,KSA 64,KSB 64,DL 32,KD 128,SD 32,INV 16,TV 256,TV2 256,THE 32,"
+               "KL 128,LW 64,QX 512,GV 256,RX 192,REP 128,KQA 64,KQB 64",
+    "int32": "NBI 1792,WTI 8,WAN 40,SND 72,SNL 72,CI 32,OL 32,KIA 16,KIB 16,ZI 128,POI 32,RSN 24",
+    "uint16": "SNU 72,SLU 72,DG 8,OFX 16,ONA 128,ONB 128,DOF 16,POF 16,DBC 256,OFS 32,RQF 16,RQO 32,RIN 32,RRQ 32",
+}
+SCRATCH = {}
+for _d, _l in SIZES.items():
+    for _x in _l.split(","):
+        SCRATCH[_x.split()[0]] = ("sbuf", [128, int(_x.split()[1])], _d)
+BANKS = ("PA", "PB", "PC0", "PC1", "PTA", "PTB", "PM", "PM2")
+for _x in BANKS:
+    SCRATCH[_x] = ("psum", [128, 512], "float32")
+SEMAPHORES = (["sV", "sS", "sP", "sG", "ls", "rs"] + ["ld%d" % i for i in range(8)] + ["st%d" % i for i in range(4)]
+              + ["ga%d_%d" % (e, t) for e in (1, 2, 3) for t in range(4)] + ["rq%d_%d" % (e, t) for e in (1, 2, 3) for t in (1, 2, 3)]
+              + ["sn%d" % e for e in (1, 2, 3)] + ["rg%d" % t for t in range(4)] + ["rr%d" % t for t in (1, 2, 3)])
+
+
+def routes(T, topo):
+    n = len(T.cores)
+    rel = {}
+    for r in range(n):
+        c = T.cores[r]
+        near = True
+        for e in range(1, n):
+            d = (r + e) % n
+            if topo.may_write(c, T.cores[d]):
+                rel[(r, d)] = None
+                continue
+            cand = [k for k in topo.cores_of(c) if k != c and topo.may_write(k, T.cores[d]) and topo.may_write(c, k)]
+            pick = [k for k in cand if (topo.die(k) == topo.die(c)) == near] or cand
+            rel[(r, d)] = pick[0]
+            near = False
+    return rel
+
+
+def count(m):
+    return bin(m).count("1")
+
+
+def relay_program(g, core, T, topo, r, d):
+    n = len(T.cores)
+    src, dst = T.cores[r], T.cores[d]
+    e, eq = (d - r) % n, (r - d) % n
+    k_in, m = count(topo.mask(src, core)), topo.mask(core, dst)
+    rid, pid = topo.addr(dst, core)
+
+    def on(sem, out, in_, rsem):
+        g.wait_ge(T.sem[sem], k_in)
+        g.remote_dma(out, in_, T.sem[rsem], T.sem["ls"], pid, rid, m)
+    for t in range(RO):
+        on("rg%d" % t, T["LG"][:, t * 1152 + (e - 1) * GH:t * 1152 + e * GH], T["RG"][:, t * GH:(t + 1) * GH], "ga%d_%d" % (e, t))
+        if t == 0:
+            on("rs", T["SNL"][:, (e - 1) * 24:e * 24], T["RSN"][:, 0:24], "sn%d" % e)
+        else:
+            on("rr%d" % t, T["RIN"][:, t * 8 + 2 * (eq - 1):t * 8 + 2 * eq], T["RRQ"][:, t * 8:t * 8 + 2], "rq%d_%d" % (eq, t))
+    g.wait_ge(T.sem["ls"], 2 * RO * count(m))
+
+
+def rank_program(g, core, T, topo):
+    rel = routes(T, topo)
+    rank = T.rank_of(core)
+    if rank is None:
+        for (r, d), k in rel.items():
+            if k == core:
+                relay_program(g, core, T, topo, r, d)
+        return
+    n = len(T.cores)
+    queue = {"V": g.vector, "S": g.scalar, "P": g.tensor, "G": g, "Y": g.sync}
+    clock = {k: {} for k in queue}
+    total = {}
+    acc = {}
+    tape = [None]
+
+    def need(q, ev, ck):
+        s, v = ev
+        if clock[q].get(s, 0) < v:
+            queue[q].wait_ge(T.sem[s], v)
+            clock[q][s] = v
+        for a, b in ck.items():
+            if clock[q].get(a, 0) < b:
+                clock[q][a] = b
+
+    def span(s):
+        return (s[0], 0, 512) if s[0] in BANKS else (s[0], s[1], s[2])
+
+    def before(q, reads, writes):
+        todo = []
+        for w, lst in ((False, reads), (True, writes)):
+            for s in lst:
+                b, lo, hi = span(s)
+                for a in acc.get(b, []):
+                    if a[0] < hi and lo < a[1]:
+                        if not w and not a[2] and not (b in BANKS and a[3] != q):
+                            continue
+                        if a[3] == q and (w or b in BANKS and q == "P"):
+                            continue
+                        todo.append((a[4], a[5]))
+        todo.sort(key=lambda x: -x[0][1])
+        for ev, ck in todo:
+            if clock[q].get(ev[0], 0) < ev[1]:
+                need(q, ev, ck)
+
+    def after(q, ev, reads, writes, by):
+        ck = dict(clock[by])
+        for w, lst in ((False, reads), (True, writes)):
+            for s in lst:
+                b, lo, hi = span(s)
+                old = acc.setdefault(b, [])
+                if w and len(s) < 4:
+                    old[:] = [a for a in old if not (lo <= a[0] and a[1] <= hi)]
+                elif not w:
+                    old[:] = [a for a in old if a[2] or a[3] != q or not (lo <= a[0] and a[1] <= hi)]
+                old.append([lo, hi, w, q, ev, ck])
+
+    def do(q, fn, reads, writes):
+        if tape[0] is not None:
+            tape[0].append((q, fn, reads, writes))
+            return
+        before(q, reads, writes)
+        s = "s" + q
+        total[s] = total.get(s, 0) + 1
+        fn(queue[q]).then_inc(T.sem[s], 1)
+        after(q, (s, total[s]), reads, writes, q)
+
+    def rec(f, *args):
+        tape[0] = []
+        f(*args)
+        out, tape[0] = tape[0], None
+        return out
+
+    def weave(a, b, pat):
+        lists = {"a": a[:], "b": b[:]}
+        for c in pat + "a" * len(a) + "b" * len(b):
+            lst = lists[c]
+            seen = False
+            while lst and not (seen and lst[0][0] == "V"):
+                seen = seen or lst[0][0] == "V"
+                x = lst.pop(0)
+                if x[0] == "send":
+                    send(*x[1])
+                else:
+                    do(*x)
+
+    def dma(q, sem, out, in_, reads, writes):
+        before(q, reads, writes)
+        total[sem] = total.get(sem, 0) + 16
+        queue[q].dma_start(out, in_).then_inc(T.sem[sem], 16)
+        after(sem, (sem, total[sem]), reads, writes, q)
+
+    def lands(s, sem, k):
+        total[sem] = total.get(sem, 0) + k
+        acc.setdefault(s[0], []).append([s[1], s[2], True, "remote", (sem, total[sem]), {}])
+
+    def ap(s):
+        if s[0] == "I":
+            return ap(s[1]).indirect(ap(s[2]))
+        if len(s) == 5:
+            return T[s[0]][0:s[4], s[1]:s[2]]
+        return T[s[0]][:, s[1]:s[2]] if len(s) == 3 else T[s[0]][:, s[1]:s[2]:s[3]]
+
+    def rd(*ss):
+        out = []
+        for s in ss:
+            if isinstance(s, tuple):
+                out += [s[1], s[2]] if s[0] == "I" else [s]
+        return out
+
+    def wr(s):
+        return [s[1]] if s[0] == "I" else [s]
+
+    def val(s):
+        return ap(s) if isinstance(s, tuple) else s
+
+    def tt(out, a, b, op):
+        do("V", lambda v: v.tensor_tensor(ap(out), ap(a), ap(b), op), rd(a, b), wr(out))
+
+    def ts(out, a, s1, op0, s2=None, op1=None):
+        if op1 is None:
+            do("V", lambda v: v.tensor_scalar(ap(out), ap(a), val(s1), None, op0), rd(a, s1), wr(out))
+        else:
+            do("V", lambda v: v.tensor_scalar(ap(out), ap(a), val(s1), val(s2), op0, op1), rd(a, s1, s2), wr(out))
+
+    def cp(out, a):
+        do("V", lambda v: v.tensor_copy(ap(out), ap(a)), rd(a) + (rd(out)[1:] if out[0] == "I" else []), wr(out))
+
+    def scan(out, d0, d1, op0, op1):
+        do("V", lambda v: v.tensor_tensor_scan(ap(out), ap(d0), ap(d1), 0.0, op0, op1), rd(d0, d1), wr(out))
+
+    def fill(out, c):
+        do("V", lambda v: v.memset(ap(out), c), [], wr(out))
+
+    def act(out, a, func=AF.Copy, **kw):
+        do("S", lambda s: s.activation(ap(out), ap(a), func, **{k: val(x) for k, x in kw.items()}), rd(a, *kw.values()), wr(out))
+
+    def mm(out, l, r, start, stop):
+        do("P", lambda p: p.matmul(ap(out), ap(l), ap(r), start, stop), rd(l, r), wr(out))
+
+    def iota(out, pat, base=0, cm=0):
+        kw = {} if SCRATCH[out[0]][2] == "int32" else {"allow_small_or_imprecise_dtypes": True}
+        do("G", lambda q: q.iota(ap(out), pat, base, cm, **kw), [], wr(out))
+
+    def pick(out, a, pat, base):
+        do("G", lambda q: q.affine_select(ap(out), ap(a), pat, OP.is_equal, 0.0, base, 1), rd(a), wr(out))
+
+    def send(in_, d, kind, e, t):
+        if tape[0] is not None:
+            tape[0].append(("send", (in_, d, kind, e, t)))
+            return
+        k = rel[(rank, d)]
+        before("G", [in_], [])
+        if k is None:
+            out, sem = {"g": (("LG", t * 1152 + (e - 1) * GH), "ga%d_%d" % (e, t)), "s": (("SNL", (e - 1) * 24), "sn%d" % e),
+                        "q": (("RIN", t * 8 + 2 * (e - 1)), "rq%d_%d" % (e, t))}[kind]
+        else:
+            out, sem = {"g": (("RG", t * GH), "rg%d" % t), "s": (("RSN", 0), "rs"), "q": (("RRQ", t * 8), "rr%d" % t)}[kind]
+        to = T.cores[d] if k is None else k
+        rid, pid = topo.addr(to, core)
+        m = topo.mask(core, to)
+        g.remote_dma(T[out[0]][:, out[1]:out[1] + in_[2] - in_[1]], ap(in_), T.sem[sem], T.sem["ls"], pid, rid, m)
+        total["ls"] = total.get("ls", 0) + count(m)
+
+    def due(d):
+        k = rel[(d, rank)]
+        return count(topo.mask(T.cores[d] if k is None else k, core))
+
+    def col(i):
+        return ("COL", i, i + 1)
+
+    def ci(i):
+        return ("CI", i, i + 1)
+
+    QF, GF, N15, I15, SC, B1, HLF, THR, QP, TMPC, KB = [col(i) for i in range(11)]
+    NVB = [col(12 + i) for i in range(4)]
+    WIN, OWN, NBW = ("XT", 0, WX), ("XT", 0, S), ("NBF", 0, WX)
+    GM, GG = ("GM", 0, 128), ("GG", 0, 8)
+
+    dma("Y", "ld0", T["XT"][:, 0:S], T.x0[:, :], [], [OWN])
+    dma("S", "ld1", T["SND"][:, :], T.snd[:, :], [], [("SND", 0, 72)])
+    dma("Y", "ld2", T["NBI"][:, :], T.nb[:, :], [], [("NBI", 0, S)])
+    dma("S", "ld3", T["WAN"][:, :], T.wants[:, :], [], [("WAN", 0, 40)])
+    dma("S", "ld4", T["WTI"][:, 0:1], T.wt[:, :], [], [("WTI", 0, 1)])
+    dma("S", "ld5", T["PUL"][:, :], T.pull[:, :], [], [("PUL", 0, 512)])
+
+    iota(ci(0), [[1, 1]], 0, 1)
+    iota(("TMF", 0, 128), [[1, 8], [0, 16]])
+    iota(("TM2", 0, 128), [[0, 8], [1, 16]])
+    iota(GG, [[1, 8]])
+    iota(("QX", 0, 256), [[1, 16], [0, 16]])
+    iota(("MSK", 0, 1024), [[0, 64], [1, 16]])
+    fill(("ONE", 0, 1024), 1.0)
+    pick(("IDB", 0, 128), ("ONE", 0, 128), [[-1, 128]], 0)
+    fill(("XT", NULL, WX), 0.0)
+    ts(ci(1), ci(0), 15, OP.bitwise_and)
+    ts(ci(2), ci(0), 4, OP.logical_shift_right)
+    cp(QF, ci(1))
+    cp(GF, ci(2))
+    ts(N15, QF, 15.0, OP.is_lt)
+    ts(I15, QF, 15.0, OP.is_equal)
+    ts(TMPC, I15, -256.0, OP.mult)
+    ts(GM, ("TMF", 0, 128), GF, OP.is_equal)
+    ts(("TM2", 0, 128), ("TM2", 0, 128), 15.0, OP.is_lt)
+    tt(("TM2", 0, 128), ("TM2", 0, 128), GM, OP.mult)
+    ts(("EMP", 0, 128), ("TM2", 0, 128), TMPC, OP.mult)
+    ts(("EMN", 0, 128), ("EMP", 0, 128), -1.0, OP.mult)
+    cp(("SNU", 0, 72), ("SND", 0, 72))
+    for x in "AB":
+        for k in (0, 1024):
+            act(("ZS" + x, k, k + 1024), ("ONE", 0, 1024), AF.Identity, scale=0.0)
+        act(("SZ" + x, 0, 128), ("ONE", 0, 128), AF.Identity, scale=0.0)
+    fill(("OL", 0, 32), 0)
+    ts(GG, GG, GF, OP.is_equal)
+    ts(("RD", 0, 8), GG, N15, OP.mult, 16777216.0, OP.mult)
+    ts(("RD", 8, 16), GG, I15, OP.mult, 69632.0, OP.mult)
+    cp(("RN", 0, 8), ("RD", 0, 8))
+    cp(("RN", 8, 16), ("RD", 0, 8))
+    ts(col(16), N15, -16777216.0, OP.mult)
+    ts(col(17), I15, -69632.0, OP.mult)
+    ts(col(18), GF, 8.0, OP.add)
+    ts(("TM2", 0, 256), ("QX", 0, 256), GF, OP.is_equal, col(16), OP.mult)
+    ts(("TM2", 256, 512), ("QX", 0, 256), col(18), OP.is_equal, col(17), OP.mult)
+    fill(("RS", 0, 128), 0.0)
+    tt(("RS", 128, 384), ("TM2", 0, 256), ("TM2", 256, 512), OP.add)
+    cp(("IDF", 0, 128), ("IDB", 0, 128))
+    ts(("IDN", 0, 128), ("IDB", 0, 128), -1.0, OP.mult)
+    ts(ci(3), ci(1), 7, OP.bitwise_and)
+    ts(ci(4), ci(1), 3, OP.logical_shift_right)
+    ts(col(19), ci(3), 8.0, OP.mult)
+    ts(col(20), ci(4), 8.0, OP.mult)
+    tt(col(21), col(19), GF, OP.add)
+    tt(col(22), col(21), col(19), OP.add)
+    tt(col(23), col(22), col(20), OP.add)
+    cp(("DG", 0, 1), col(21))
+    cp(("DG", 2, 3), col(23))
+    cp(("DG", 3, 4), col(23))
+    ban = ["PC0", "PC1", "PTA", "PTB"]
+    part = [(448 * k, 448 * (k + 1)) for k in range(4)]
+    for k, (a, b) in enumerate(part):
+        ts(("YO", a, b), ("XT", a, b), 0.0, OP.is_lt)
+        mm((ban[k], 0, 448), ("EMP", 0, 128), ("YO", a, b), True, True)
+    for k, (a, b) in enumerate(part):
+        tt(("XT", a, b), ("XT", a, b), (ban[k], 0, 448), OP.add)
+
+    def ghosts(t):
+        at = t * 1152
+        act(("GS", at, at + 384), ("I", OWN, ("SNU", 0, 24)))
+        cp(("GS", at + 768, at + 1152), ("I", OWN, ("SNU", 48, 72)))
+        send(("GS", at, at + 384), (rank + 1) % n, "g", 1, t)
+        send(("GS", at + 768, at + 1152), (rank + 3) % n, "g", 3, t)
+        act(("GS", at + 384, at + 576), ("I", OWN, ("SNU", 24, 36)))
+        cp(("GS", at + 576, at + 768), ("I", OWN, ("SNU", 36, 48)))
+        send(("GS", at + 384, at + 768), (rank + 2) % n, "g", 2, t)
+        for e in (1, 2, 3):
+            lands(("LG", at + (e - 1) * GH, at + e * GH), "ga%d_%d" % (e, t), due((rank - e) % n))
+
+    ghosts(0)
+    for e in (1, 3, 2):
+        send(("SND", (e - 1) * 24, e * 24), (rank + e) % n, "s", e, 0)
+        lands(("SNL", (e - 1) * 24, e * 24), "sn%d" % e, due((rank - e) % n))
+
+    iota(("IOT", 0, WX), [[1, WX]])
+    pick(("EXP", 0, 2048 - V16), ("ONE", 0, 2048 - V16), [[-1, 128 - VL], [0, 16]], -VL)
+    pick(("REB", 0, 128), ("ONE", 0, 128), [[0, 8], [-1, 16]], 0)
+    pick(("PRB", 0, 1024), ("ONE", 0, 1024), [[-16, 8], [0, 8], [-1, 16]], 0)
+    iota(("TMF", 0, 256), [[0, 16], [1, 16]])
+    iota(("TRS", 0, 32), [[16, 32]], TRASH)
+    for b, lo, hi in (("GST", 0, S), ("GST", NULL, WX), ("EQ", 0, 4096)):
+        iota((b, lo, hi), [[0, hi - lo]])
+    ts(KB, QF, 1.0, OP.add, -4096.0, OP.mult)
+    ts(("MSK", 0, 1024), ("MSK", 0, 1024), 0.5, OP.is_gt)
+    cp(("NBF", 0, S), ("NBI", 0, S))
+    act(("NBF", S, WX), ("IOT", S, WX))
+    act(("REP", 0, 128), ("REB", 0, 128))
+    ts(("WZ", 8, 16), GG, I15, OP.mult)
+    cp(SC, N15)
+    ts(B1, N15, -255.0, OP.mult, -1.0, OP.add)
+    ts(HLF, N15, 0.5, OP.mult)
+    ts(col(24), N15, -8388608.0, OP.mult)
+    for t in range(RO):
+        ts(NVB[t], I15, float(192 + t), OP.mult, col(24), OP.add)
+    fill(QP, 32768.0)
+    for k in range(4):
+        ts(ci(8), ci(1), k, OP.logical_shift_right, 1, OP.bitwise_and)
+        ts(col(25), ci(8), 2.0 ** -(2 ** k) - 1.0, OP.mult, 1.0, OP.add)
+        tt(QP, QP, col(25), OP.mult)
+    for c in range(8):
+        w = 2.0 ** (17 * (7 - c) - 44)
+        ts(("WM", c * 24, c * 24 + 8), GG, QP, OP.mult, w, OP.mult)
+        ts(("WM", c * 24 + 8, c * 24 + 16), GG, QP, OP.mult, w, OP.mult)
+        ts(("WM", c * 24 + 16, c * 24 + 24), GG, 2.0 ** 92, OP.mult)
+        fill(("GG", 16 + c, 17 + c), 2.0 * w)
+    tt(("GG", 32, 40), GG, ("GG", 16, 24), OP.mult)
+    tt(("GG", 32, 36), ("GG", 32, 36), ("GG", 36, 40), OP.add)
+    tt(("GG", 32, 34), ("GG", 32, 34), ("GG", 34, 36), OP.add)
+    tt(col(26), ("GG", 32, 33), ("GG", 33, 34), OP.add)
+    tt(THR, col(26), QP, OP.mult)
+    ts(col(27), QF, 1.0, OP.add, 512.0, OP.mult)
+    ts(("GM2", 0, 128), GM, col(27), OP.mult)
+    act(("PRF", 0, 1024), ("PRB", 0, 1024))
+
+    def later_consts():
+        ts(("DQ", 0, 256), ("TMF", 0, 256), QF, OP.is_equal)
+        ts(("TRS", 0, 32), ("TRS", 0, 32), QF, OP.add)
+        cp(TMPC, ("WTI", 0, 1))
+        ts(("WZ", 0, 8), GG, TMPC, OP.mult, N15, OP.mult)
+        for e, lo, hi in ((1, S, S + GH), (2, S + GH, S + 2 * GH), (3, S + 2 * GH, NULL), (4, 0, S), (4, NULL, WX)):
+            if lo != NULL:
+                ts(col(27 + e), QF, float(e - 1), OP.is_equal)
+            act(("EIN", lo, hi), ("IOT", lo, hi), AF.Identity, scale=0.0, bias=col(27 + e))
+        for e in (2, 1, 3):
+            lo = S + (e - 1) * GH
+            cp(("SLU", (e - 1) * 24, e * 24), ("SNL", (e - 1) * 24, e * 24))
+            act(("GST", lo, lo + GH), ("I", ("IOT", 0, S), ("SLU", (e - 1) * 24, e * 24)))
+
+    O8 = {"A": 0, "B": 8}
+
+    def OFX(x, a, b):
+        return ("OFX", O8[x] + a, O8[x] + b)
+
+    def OLD(x, a, b):
+        return ("OL", 2 * O8[x] + a, 2 * O8[x] + b)
+
+    def start_a(t):
+        cp(OLD("A", 6, 8), ("WAN", t * 10, t * 10 + 2))
+        if t == 0:
+            fill(OLD("A", 0, 6), NULL)
+        else:
+            cp(OLD("A", 0, 6), ("RIN", t * 8, t * 8 + 6))
+        cp(OFX("A", 0, 8), OLD("A", 0, 8))
+
+    def own_v(x, win):
+        cp(("ON" + x, 0, 128), ("I", NBW, OFX(x, 0, 8)))
+        cp(("ZS" + x, 0, V16, 16), ("I", win, OFX(x, 0, VL // 16)))
+
+    def own_s(x, win):
+        act(("SZ" + x, VL, 128), ("I", win, OFX(x, VL // 16, 8)))
+        mm(("PT" + x, 128, 256), ("SZ" + x, 0, 128), ("IDN", 0, 128), True, True)
+        act(("BS" + x, 0, 128), ("I", NBW, OFX(x, 0, 8)), AF.Identity, bias=KB)
+        mm(("P" + x, 0, 384), ("SZ" + x, 0, 128), ("RS", 0, 384), True, False)
+        mm(("P" + x, 256, 384), ("BS" + x, 0, 128), ("IDF", 0, 128), False, False)
+
+    def prep_b(t):
+        cp(OLD("B", 0, 8), ("WAN", t * 10 + 2, t * 10 + 10))
+        cp(OFX("B", 0, 8), OLD("B", 0, 8))
+        own_s("B", OWN)
+        own_v("B", OWN)
+
+    def ghosts_in(t):
+        for e in (2, 1, 3):
+            lo = (e - 1) * GH
+            act(("XT", S + lo, S + lo + GH), ("LG", t * 1152 + lo, t * 1152 + lo + GH))
+
+    def own_t(x):
+        act(("ST" + x, 0, 128), ("PT" + x, 128, 256))
+
+    def gather_s(x, k):
+        a = V16 + 512 * k
+        act(("D" + x, a, a + 512), ("I", WIN, ("ON" + x, a // 16, a // 16 + 32)))
+
+    def diff(x, k):
+        a, pc = V16 + 512 * k, ("PC%d" % k, 0, 512)
+        mm(pc, ("IDB", 0, 128), ("D" + x, a, a + 512), True, False)
+        mm(pc, ("ST" + x, 0, 128), ("EXP", 512 * k, 512 * k + 512), False, True)
+
+    def relu(x, k):
+        a = V16 + 512 * k
+        act(("N" + x, a, a + 512), ("PC%d" % k, 0, 512), AF.Relu, scale=-1.0)
+
+    def big_v(x):
+        scan(("SB" + x, 0, V16), ("MSK", 0, V16), ("ZS" + x, 0, V16), OP.mult, OP.add)
+        for k in range(4):
+            a, b = V16 // 4 * k, V16 // 4 * (k + 1)
+            tt(("D" + x, a, b), ("I", WIN, ("ON" + x, a // 16, b // 16)), ("SB" + x, a, b), OP.subtract)
+        for k in range(4):
+            a, b = V16 // 4 * k, V16 // 4 * (k + 1)
+            ts(("N" + x, a, b), ("D" + x, a, b), -1.0, OP.mult, 0.0, OP.max)
+
+    def sums(ps, buf, rhs, lo, stop):
+        for i in range(16):
+            mm((ps, lo + i, lo + 256, 16), (buf, i, 2048, 16), (rhs, 0, 16), False, stop and i == 15)
+
+    def best_s(x):
+        act(("TA" + x, 0, 128), ("P" + x, 0, 128))
+
+    def best(x):
+        ps, m = "P" + x, "M" + x
+        tt((m, 0, 128), ("TA" + x, 0, 128), (ps, 128, 256), OP.min)
+        tt((m, 128, 256), (m, 0, 128), (ps, 256, 384), OP.min)
+        scan(("R" + x, 0, 128), ("MSK", 0, 128), (m, 128, 256), OP.mult, OP.max)
+
+    def turn(ps, w, mat, rhs):
+        for c in range(8):
+            mm((ps, c * w, c * w + w), (mat, c * 128, c * 128 + 128), rhs, True, True)
+
+    def perm(x):
+        for c in range(8):
+            mm(("PT" + x, 64 + c * 8, 72 + c * 8, 1, 16), ("IDF", c * 16, c * 16 + 16), ("R" + x, 15, 128, 16), True, True)
+
+    def step(x):
+        cp(("KQ" + x, 0, 64, 1, 16), ("PT" + x, 64, 128, 1, 16))
+        mm(("PT" + x, 0, 64), ("REP", 0, 128, 1, 16), ("KQ" + x, 0, 64, 1, 16), True, True)
+        cp(("KS" + x, 0, 64), ("PT" + x, 0, 64))
+        tt(("KI" + x, 0, 16), ("I", ("KS" + x, 0, 64), ("DG", 0, 1)), OLD(x, 0, 16), OP.max)
+        ts(OLD(x, 0, 16), ("KI" + x, 0, 16), 4095, OP.bitwise_and)
+        cp(OFX(x, 0, 8), OLD(x, 0, 8))
+
+    def places_p():
+        for b, x in enumerate("AB"):
+            for k in (0, 8):
+                o = ("PM", 2 * k + 8 * b, 2 * k + 8 * b + 8)
+                mm(o, ("ZS" + x, 0, 2048, 16), ("WZ", k, k + 8), True, False)
+                mm(o, ("SZ" + x, 0, 128), ("WZ", k, k + 8), False, True)
+
+    def places(t):
+        z = [("ZI", 16 * i, 16 * i + 16) for i in range(8)]
+        ts(("DL", 16, 32), ("PM", 16, 32), 0.0, OP.is_lt, float(NULL), OP.mult)
+        cp(z[0], ("PM", 0, 16))
+        ts(z[1], z[0], 2047, OP.bitwise_and)
+        tt(z[2], z[1], z[1], OP.mult)
+        ts(z[3], z[2], float(97 * t * 32), OP.add)
+        ts(z[4], z[3], 5, OP.logical_shift_right, 2047, OP.bitwise_and)
+        ts(z[5], z[4], float(S), OP.is_ge, -float(S), OP.mult)
+        tt(z[6], z[4], z[5], OP.add)
+        tt(("DL", 0, 16), z[6], ("DL", 16, 32), OP.max)
+        turn("PM2", 16, "PRF", ("DL", 0, 16))
+        for k, x in ((0, "A"), (8, "B")):
+            ts(("INV", k, k + 8), OLD(x, 0, 8), float(S), OP.is_ge, float(NULL), OP.mult)
+            cp(("SD", 16 + k, 24 + k), OLD(x, 0, 8))
+
+    def places2():
+        cp(("KD", 0, 128), ("PM2", 0, 128))
+        tt(("SD", 0, 16), ("I", ("KD", 0, 128), ("DG", 2, 3)), ("INV", 0, 16), OP.max)
+        cp(("DOF", 0, 16), ("SD", 0, 16))
+        cp(("DBC", 0, 256), ("I", ("IOT", 0, WX), ("DOF", 0, 16)))
+
+    def places3():
+        cp(("POI", 0, 16), ("SD", 0, 16))
+        for c in range(16):
+            ts(("EQ", c * 272, c * 256 + 256), ("DBC", 16 * c, 256), ("SD", c, c + 1), OP.is_equal)
+            if c == 5:
+                ts(("POI", 16, 32), ("POI", 0, 16), 511, OP.bitwise_and)
+            if c == 10:
+                cp(("POF", 0, 16), ("POI", 16, 32))
+
+    def places4():
+        for o, x in ((0, "A"), (128, "B")):
+            p, q = o // 16, (o + VL) // 16
+            tt(("TV", o, o + VL), ("I", ("PUL", 0, 512), ("POF", p, q)), ("ZS" + x, 0, V16, 16), OP.add)
+            tt(("TV", o + VL, o + 128), ("I", ("PUL", 0, 512), ("POF", q, p + 8)), ("SZ" + x, VL, 128), OP.add)
+
+    def places_s():
+        act(("XD", 0, 256), ("I", WIN, ("DOF", 0, 16)))
+        for b in (0, 1):
+            mm(("PM", 32 + 8 * b, 40 + 8 * b), ("XD", 128 * b, 128 * b + 128), ("WZ", 8, 16), True, True)
+        for o, x in ((256, "A"), (384, "B")):
+            act(("VAL", o, o + VL), ("ZS" + x, 0, V16, 16), AF.Identity, scale=SC, bias=B1)
+            act(("VAL", o + VL, o + 128), ("SZ" + x, VL, 128), AF.Identity, scale=SC, bias=B1)
+
+    def moves(t):
+        for k, x in ((0, "A"), (8, "B"), (16, "A")):
+            ts(("STL", k, k + 8), ("R" + x, 15, 128, 16), 0.0, OP.is_equal)
+        turn("PM2", 24, "PRB", ("STL", 0, 24))
+        places4()
+        ts(("THE", 0, 16), ("PM", 32, 48), 0.0, OP.is_lt, THR, OP.mult)
+        tt(("THE", 16, 32), ("THE", 0, 16), ("STL", 0, 16), OP.mult)
+        tt(("RW", 0, 192), ("PM2", 0, 192), ("WM", 0, 192), OP.mult)
+        for c in range(8):
+            mm(("PM", 0, 8), ("EQ", c * 256, c * 256 + 128), ("RW", c * 24, c * 24 + 8), c == 0, c == 7)
+        for c in range(16):
+            o = (c % 8) * 24 + (8 if c >= 8 else 16)
+            mm(("PM", 8, 16), ("EQ", c * 256 + 128, c * 256 + 256), ("RW", o, o + 8), c == 0, c == 15)
+        ts(("TV2", 0, 256), ("TV", 0, 256), -0.5, OP.add, 16777216.0, OP.add)
+        act(("VAL", 0, 256), ("TV2", 0, 256), AF.Identity, scale=HLF, bias=NVB[t])
+        tt(("LB", 0, 16), ("PM", 0, 16), ("THE", 16, 32), OP.is_ge)
+        turn("PM2", 16, "PRB", ("LB", 0, 16))
+        cp(("KL", 0, 128), ("PM2", 0, 128))
+        tt(("LW", 0, 32), ("I", ("KL", 0, 128), ("DG", 2, 4)), ("TRS", 0, 32), OP.mult)
+        tt(("LW", 32, 64), ("LW", 0, 32), ("SD", 0, 32), OP.max)
+        cp(("OFS", 0, 32), ("LW", 32, 64))
+        cp(("I", ("XT", 0, 3584), ("OFS", 0, 32)), ("VAL", 0, 512))
+
+    def requests(t):
+        act(("GV", 0, 256), ("I", ("GST", 0, WX), ("OFX", 0, 16)))
+        for e in (1, 2, 3):
+            act(("REQ", 512 * e + 1, 512 * e + 33), ("IOT", 0, CAP), AF.Identity, scale=0.0, bias=float(NULL))
+        cp(("IND", 0, 256), ("I", ("EIN", 0, WX), ("OFX", 0, 16)))
+        scan(("CNT", 0, 256), ("ONE", 0, 256), ("IND", 0, 256), OP.mult, OP.add)
+        tt(("QC", 0, 256), ("IND", 0, 256), ("CNT", 0, 256), OP.mult)
+        mm(("PC0", 0, 256), ("GM2", 0, 128), ("IND", 0, 256), True, False)
+        mm(("PC0", 0, 256), GM, ("QC", 0, 256), False, True)
+        tt(("QX", 0, 256), ("PC0", 0, 256), ("DQ", 0, 256), OP.mult)
+        scan(("QX", 256, 512), ("MSK", 0, 256), ("QX", 0, 256), OP.mult, OP.add)
+        cp(("RQF", 0, 16), ("QX", 271, 512, 16))
+        cp(("I", ("REQ", 0, 2320), ("RQF", 0, 16)), ("GV", 0, 256))
+        for e in (1, 2, 3):
+            tt(("RX", 32 * e - 32, 32 * e), ("REQ", 512 * e + 1, 512 * e + 33), ("DQ", 0, CAP), OP.mult)
+        scan(("RX", 96, 192), ("MSK", 0, 96), ("RX", 0, 96), OP.mult, OP.add)
+        o = (t + 1) * 8
+        cp(("RQO", o, o + 6), ("RX", 111, 192, 16))
+        for e in (1, 3, 2):
+            send(("RQO", o + 2 * (e - 1), o + 2 * e), (rank - e) % n, "q", e, t + 1)
+            lands(("RIN", o + 2 * (e - 1), o + 2 * e), "rq%d_%d" % (e, t + 1), due((rank + e) % n))
+
+    order = [("B", 0), ("A", 0), ("B", 1), ("A", 1), ("B", 2), ("A", 2)]
+    prep_b(0)
+    for t in range(RO):
+        ghosts_in(t)
+        for i, (x, h) in enumerate(order):
+            y = "B" if x == "A" else "A"
+            big = rec(big_v, x)
+            if i == 5:
+                places_p()
+            gather_s(x, 0)
+            own_t(x)
+            diff(x, 0)
+            if i == 5:
+                gather_s(x, 1)
+                diff(x, 1)
+                weave(big, rec(places, t), "ab" * 9)
+            else:
+                weave(big[:3], rec(best, y) if i else [], "ababab")
+                if i:
+                    perm(y)
+                gather_s(x, 1)
+                diff(x, 1)
+                weave(big[3:], rec(step, y) if i else rec(start_a, t), "abaabababab" if i else "aaaaaa")
+            relu(x, 0)
+            relu(x, 1)
+            sums("P" + x, "D" + x, "RD", 128, False)
+            sums("P" + x, "N" + x, "RN", 0, True)
+            if i < 5:
+                own_s(y, WIN)
+                best_s(x)
+                own_v(y, WIN)
+            if t == 0 and i == 3:
+                later_consts()
+        weave(rec(best, "B"), rec(places2), "abab")
+        best_s("A")
+        places_s()
+        weave(rec(best, "A"), rec(places3), "bbbbbbabbbabbbabbbba")
+        moves(t)
+        if t + 1 < RO:
+            ghosts(t + 1)
+            perm("B")
+            perm("A")
+            weave(rec(step, "B"), rec(step, "A"), "ab" * 5)
+            weave(rec(requests, t), rec(prep_b, t + 1), "aabababaabaaaaaa")
+
+    for k, (a, b) in enumerate(part):
+        ts(("DB", a, b), ("XT", a, b), 0.0, OP.is_lt)
+        mm((ban[k], 0, 448), ("IDB", 0, 128), ("XT", a, b), True, False)
+        mm((ban[k], 0, 448), ("EMN", 0, 128), ("DB", a, b), False, True)
+        if k % 2:
+            cp(("YO", a, b), (ban[k], 0, 448))
+        else:
+            act(("YO", a, b), (ban[k], 0, 448))
+        dma("Y", "st%d" % k, T.y[:, a:b], T["YO"][:, a:b], [("YO", a, b)], [])
+    for s in sorted(total):
+        if clock["G"].get(s, 0) < total[s]:
+            g.wait_ge(T.sem[s], total[s])

@@ -1,27 +1,35 @@
-from concourse.mybir import AluOpType, ActivationFunctionType
+from concourse.mybir import AluOpType, ActivationFunctionType, AxisListType
 
 S, GH, CAP, RO = 1792, 384, 32, 4
-NULL, WX, TRASH = 2944, 2960, 3072
-VL = 64
-V16 = 16 * VL
+NULL, WX, TRASH = 2944, 2960, 2960
+MID = 1472.0
+RATIO, TOP = 1.75, 2.0 ** 98
+MAGIC = 1.5 * 2.0 ** 24
+BLOCKS = [{"A": (0, 3), "B": (3, 4), "C": (7, 3)}] + [{"A": (0, 6), "B": (6, 5), "C": (11, 5)}] * 3
+ORDER = ["ABC", "BAC", "BAC", "BAC"]
+FUSED = {48: 16, 64: 16, 80: 16, 96: 32}
+CUT = {48: 32, 64: 32, 80: 64, 96: 64}
+PIECE = (16, 16, 16)
+ONV, NOUT = 1, 2
+CYC, PCYC, DONE, WAKE, LOAD, NEAR, FAR, SMALL = 0.00083, 0.00042, 0.1, 0.1, 1.9, 4.0, 6.5, 1.0
 OP = AluOpType
 AF = ActivationFunctionType
 SIZES = {
-    "bfloat16": "XT 3584,EIN 2960,PUL 512,ZSA 2048,ZSB 2048,MSK 1024,SBA 1024,SBB 1024,DA 2048,DB 2048,NA 2048,NB 2048,EXP 1024,"
-                "ONE 1024,EQ 4096,PRB 1024,IDB 128,IDN 128,EMP 128,EMN 128,GM 128,GM2 128,RD 16,RN 16,RS 384,WZ 16,DQ 256,SZA 128,"
-                "SZB 128,STA 128,STB 128,XD 256,VAL 512,STL 24,RW 192,LB 16,IND 256,CNT 256,QC 256,GS 4608,LG 4608,RG 1536,YO 1792,"
-                "REB 128",
-    "float32": "NBF 2960,IOT 2960,GST 2960,REQ 2320,PRF 1024,IDF 128,WM 192,COL 64,GG 64,TMF 256,TM2 512,TRS 32,BSA 128,"
-               "BSB 128,TAA 128,TAB 128,MA 256,MB 256,RA 128,RB 128,KSA 64,KSB 64,DL 32,KD 128,SD 32,INV 16,TV 256,TV2 256,THE 32,"
-               "KL 128,LW 64,QX 512,GV 256,RX 192,REP 128,KQA 64,KQB 64",
-    "int32": "NBI 1792,WTI 8,WAN 40,SND 72,SNL 72,CI 32,OL 32,KIA 16,KIB 16,ZI 128,POI 32,RSN 24",
-    "uint16": "SNU 72,SLU 72,DG 8,OFX 16,ONA 128,ONB 128,DOF 16,POF 16,DBC 256,OFS 32,RQF 16,RQO 32,RIN 32,RRQ 32",
+    "bfloat16": "XR 1792,XT 3584,YO 3584,EIN 2960,PUL 512,MSK 512,RAW 3072,EXP 1536,ONE 768,EQ 4096,PRB 768,IDB 128,IDK 128,GM 128,"
+                "GM2 128,GGK 128,WZ 16,ZER 96,DQ 256,XD 256,VAL 512,STL 24,RW 128,LB 24,IND 256,CNT 256,QC 256,GS 4608,LG 4608,"
+                "RG 1536",
+    "float16": "ZSA 1536,ZSB 1536,ZSC 1536,DA 1536,DB 1536,DC 1536,SB 512,BSA 96,BSB 96,BSC 96,STA 128,STB 128,STC 128,EA 96,EB 96,"
+               "EC 96,RD 16,RS 256,RE 256,WY 16,PRW 2304,DL 24,DBC 256",
+    "float32": "NBF 2960,IOT 2960,REQ 2320,PUF 1024,REP 128,COL 64,GG 16,TMF 128,NN 128,WC 32,M 128,RA 136,RB 136,RC 136,"
+               "KQ 48,DN 24,KD 128,SD 64,INV 32,TV 256,TV2 256,THE 48,KL 128,LW 64,QX 512,GV 256,RX 192,RQO 32,RIN 32,RRQ 32",
+    "int32": "NBI 1792,WTI 8,WAN 40,WK 320,SND 72,SNL 72,CI 16,OL 128,KI 48,WI 128,FI 128,ZI 168,POI 64,RSN 24",
+    "uint16": "SNU 72,SLU 72,DG 16,RL 4,XL 4,OFA 16,OFB 16,OFC 16,OFX 16,ONA 96,ONB 96,ONC 96,DOF 32,POF 32,OFS 64,RQF 16",
 }
 SCRATCH = {}
 for _d, _l in SIZES.items():
     for _x in _l.split(","):
         SCRATCH[_x.split()[0]] = ("sbuf", [128, int(_x.split()[1])], _d)
-BANKS = ("PA", "PB", "PC0", "PC1", "PTA", "PTB", "PM", "PM2")
+BANKS = ("PA", "PB", "PC", "X0", "X1", "PT", "PM", "PM2")
 for _x in BANKS:
     SCRATCH[_x] = ("psum", [128, 512], "float32")
 SEMAPHORES = (["sV", "sS", "sP", "sG", "ls", "rs"] + ["ld%d" % i for i in range(8)] + ["st%d" % i for i in range(4)]
@@ -61,13 +69,68 @@ def relay_program(g, core, T, topo, r, d):
     def on(sem, out, in_, rsem):
         g.wait_ge(T.sem[sem], k_in)
         g.remote_dma(out, in_, T.sem[rsem], T.sem["ls"], pid, rid, m)
+    on("rs", T["SNL"][:, (e - 1) * 24:e * 24], T["RSN"][:, 0:24], "sn%d" % e)
     for t in range(RO):
         on("rg%d" % t, T["LG"][:, t * 1152 + (e - 1) * GH:t * 1152 + e * GH], T["RG"][:, t * GH:(t + 1) * GH], "ga%d_%d" % (e, t))
-        if t == 0:
-            on("rs", T["SNL"][:, (e - 1) * 24:e * 24], T["RSN"][:, 0:24], "sn%d" % e)
-        else:
+        if t:
             on("rr%d" % t, T["RIN"][:, t * 8 + 2 * (eq - 1):t * 8 + 2 * eq], T["RRQ"][:, t * 8:t * 8 + 2], "rq%d_%d" % (eq, t))
     g.wait_ge(T.sem["ls"], 2 * RO * count(m))
+
+
+def span(s):
+    return (s[0], 0, 512) if s[0] in BANKS else (s[0], s[1], s[2])
+
+
+def meets(acc, q, reads, writes, adds):
+    out = []
+    for w, lst in ((False, reads), (True, writes)):
+        for s in lst:
+            b, lo, hi = span(s)
+            for a in acc.get(b, []):
+                if a[0] < hi and lo < a[1] and (w or a[2] or b in BANKS and a[3] != q):
+                    out.append((a, not (a[3] == q == "P" and (adds or a[-1][2] <= s[1] or s[2] <= a[-1][1]))))
+    return out
+
+
+def note(acc, q, reads, writes, *more):
+    for w, lst in ((False, reads), (True, writes)):
+        for s in lst:
+            b, lo, hi = span(s)
+            old = acc.setdefault(b, [])
+            if w:
+                old[:] = [a for a in old if not (lo <= a[0] and a[1] <= hi and len(s) < 4)]
+            old.append([lo, hi, w, q] + list(more) + [s])
+
+
+def issue_order(calls):
+    acc, left, post = {}, [], [{} for c in calls]
+    for i, c in enumerate(calls):
+        p = {j: calls[j][0] != c[0] for j in c[5]}
+        for a, done in meets(acc, c[0], c[3], c[4], c[6] == "add"):
+            p[a[4]] = p.get(a[4], False) or done
+        for j, done in p.items():
+            post[j][i] = calls[j][2] + DONE if done else 0.0
+        left.append(len(p))
+        note(acc, c[0], c[3], c[4], i)
+    way = [0.0] * len(calls)
+    for i in reversed(range(len(calls))):
+        way[i] = calls[i][1] + max([way[k] + w + (WAKE if w else 0.0) for k, w in post[i].items()] + [calls[i][2]])
+    ready, free, pool, order = [0.0] * len(calls), {}, {}, []
+    for i, c in enumerate(calls):
+        if not left[i]:
+            pool.setdefault(c[0], []).append(i)
+    for k in calls:
+        at, q = min((max(free.get(q, 0.0), min(ready[i] for i in lst)), q) for q, lst in pool.items() if lst)
+        i = max((i for i in pool[q] if ready[i] <= at), key=lambda i: (way[i], -i))
+        pool[q].remove(i)
+        order.append(i)
+        free[q] = (at if ready[i] <= free.get(q, 0.0) else at + WAKE) + calls[i][1]
+        for j, w in post[i].items():
+            ready[j] = max(ready[j], free[q] + w)
+            left[j] -= 1
+            if not left[j]:
+                pool.setdefault(calls[j][0], []).append(j)
+    return order
 
 
 def rank_program(g, core, T, topo):
@@ -80,97 +143,22 @@ def rank_program(g, core, T, topo):
         return
     n = len(T.cores)
     queue = {"V": g.vector, "S": g.scalar, "P": g.tensor, "G": g, "Y": g.sync}
-    clock = {k: {} for k in queue}
-    total = {}
-    acc = {}
-    tape = [None]
+    calls = []
 
-    def need(q, ev, ck):
-        s, v = ev
-        if clock[q].get(s, 0) < v:
-            queue[q].wait_ge(T.sem[s], v)
-            clock[q][s] = v
-        for a, b in ck.items():
-            if clock[q].get(a, 0) < b:
-                clock[q][a] = b
+    def last_of(kind, q):
+        return [i for i, c in enumerate(calls) if c[6] == kind and c[0] == q][-1:]
 
-    def span(s):
-        return (s[0], 0, 512) if s[0] in BANKS else (s[0], s[1], s[2])
+    def do(q, cost, fn, reads, writes):
+        calls.append([q, cost, 0.0, reads, writes, [], "do", fn])
 
-    def before(q, reads, writes):
-        todo = []
-        for w, lst in ((False, reads), (True, writes)):
-            for s in lst:
-                b, lo, hi = span(s)
-                for a in acc.get(b, []):
-                    if a[0] < hi and lo < a[1]:
-                        if not w and not a[2] and not (b in BANKS and a[3] != q):
-                            continue
-                        if a[3] == q and (w or b in BANKS and q == "P"):
-                            continue
-                        todo.append((a[4], a[5]))
-        todo.sort(key=lambda x: -x[0][1])
-        for ev, ck in todo:
-            if clock[q].get(ev[0], 0) < ev[1]:
-                need(q, ev, ck)
-
-    def after(q, ev, reads, writes, by):
-        ck = dict(clock[by])
-        for w, lst in ((False, reads), (True, writes)):
-            for s in lst:
-                b, lo, hi = span(s)
-                old = acc.setdefault(b, [])
-                if w and len(s) < 4:
-                    old[:] = [a for a in old if not (lo <= a[0] and a[1] <= hi)]
-                elif not w:
-                    old[:] = [a for a in old if a[2] or a[3] != q or not (lo <= a[0] and a[1] <= hi)]
-                old.append([lo, hi, w, q, ev, ck])
-
-    def do(q, fn, reads, writes):
-        if tape[0] is not None:
-            tape[0].append((q, fn, reads, writes))
-            return
-        before(q, reads, writes)
-        s = "s" + q
-        total[s] = total.get(s, 0) + 1
-        fn(queue[q]).then_inc(T.sem[s], 1)
-        after(q, (s, total[s]), reads, writes, q)
-
-    def rec(f, *args):
-        tape[0] = []
-        f(*args)
-        out, tape[0] = tape[0], None
-        return out
-
-    def weave(a, b, pat):
-        lists = {"a": a[:], "b": b[:]}
-        for c in pat + "a" * len(a) + "b" * len(b):
-            lst = lists[c]
-            seen = False
-            while lst and not (seen and lst[0][0] == "V"):
-                seen = seen or lst[0][0] == "V"
-                x = lst.pop(0)
-                if x[0] == "send":
-                    send(*x[1])
-                else:
-                    do(*x)
-
-    def dma(q, sem, out, in_, reads, writes):
-        before(q, reads, writes)
-        total[sem] = total.get(sem, 0) + 16
-        queue[q].dma_start(out, in_).then_inc(T.sem[sem], 16)
-        after(sem, (sem, total[sem]), reads, writes, q)
-
-    def lands(s, sem, k):
-        total[sem] = total.get(sem, 0) + k
-        acc.setdefault(s[0], []).append([s[1], s[2], True, "remote", (sem, total[sem]), {}])
+    def dma(q, sem, out, in_, reads, writes, after):
+        calls.append([q, 0.05, after, reads, writes, last_of("dma", q), "dma", (sem, out, in_)])
 
     def ap(s):
         if s[0] == "I":
             return ap(s[1]).indirect(ap(s[2]))
-        if len(s) == 5:
-            return T[s[0]][0:s[4], s[1]:s[2]]
-        return T[s[0]][:, s[1]:s[2]] if len(s) == 3 else T[s[0]][:, s[1]:s[2]:s[3]]
+        rows = slice(s[5] if len(s) > 5 else 0, s[4]) if len(s) > 4 else slice(None)
+        return T[s[0]][rows, s[1]:s[2]:s[3]] if len(s) > 3 and s[3] > 1 else T[s[0]][rows, s[1]:s[2]]
 
     def rd(*ss):
         out = []
@@ -185,449 +173,445 @@ def rank_program(g, core, T, topo):
     def val(s):
         return ap(s) if isinstance(s, tuple) else s
 
+    def size(s):
+        return -(-(s[2] - s[1]) // (s[3] if len(s) > 3 else 1))
+
+    def cost(rate, out, *ins):
+        if out[0] == "I":
+            return 0.05 + 3.8 * CYC * size(ins[0])
+        if ins and ins[0][0] == "I":
+            return 0.06 + 1.56 * CYC * size(out)
+        if rate == 0:
+            rate = 0.5 if all(SCRATCH[s[0]][2].endswith("16") for s in (out,) + ins) else 1
+        return max(64, rate * size(out)) * CYC
+
     def tt(out, a, b, op):
-        do("V", lambda v: v.tensor_tensor(ap(out), ap(a), ap(b), op), rd(a, b), wr(out))
+        do("V", cost(1 if a[0] in BANKS or b[0] in BANKS else 2, out, a), lambda v: v.tensor_tensor(ap(out), ap(a), ap(b), op), rd(a, b), wr(out))
 
     def ts(out, a, s1, op0, s2=None, op1=None):
         if op1 is None:
-            do("V", lambda v: v.tensor_scalar(ap(out), ap(a), val(s1), None, op0), rd(a, s1), wr(out))
+            do("V", cost(0, out, a), lambda v: v.tensor_scalar(ap(out), ap(a), val(s1), None, op0), rd(a, s1), wr(out))
         else:
-            do("V", lambda v: v.tensor_scalar(ap(out), ap(a), val(s1), val(s2), op0, op1), rd(a, s1, s2), wr(out))
+            do("V", cost(0, out, a), lambda v: v.tensor_scalar(ap(out), ap(a), val(s1), val(s2), op0, op1), rd(a, s1, s2), wr(out))
 
     def cp(out, a):
-        do("V", lambda v: v.tensor_copy(ap(out), ap(a)), rd(a) + (rd(out)[1:] if out[0] == "I" else []), wr(out))
+        do("V", cost(0, out, a), lambda v: v.tensor_copy(ap(out), ap(a)), rd(a) + (rd(out)[1:] if out[0] == "I" else []), wr(out))
 
-    def scan(out, d0, d1, op0, op1):
-        do("V", lambda v: v.tensor_tensor_scan(ap(out), ap(d0), ap(d1), 0.0, op0, op1), rd(d0, d1), wr(out))
+    def scan(out, d0, d1, op0, op1, first=0.0):
+        do("V", cost(0, out, d0, d1), lambda v: v.tensor_tensor_scan(ap(out), ap(d0), ap(d1), val(first), op0, op1), rd(d0, d1, first), wr(out))
 
     def fill(out, c):
-        do("V", lambda v: v.memset(ap(out), c), [], wr(out))
+        do("V", cost(0, out), lambda v: v.memset(ap(out), c), [], wr(out))
 
     def act(out, a, func=AF.Copy, **kw):
-        do("S", lambda s: s.activation(ap(out), ap(a), func, **{k: val(x) for k, x in kw.items()}), rd(a, *kw.values()), wr(out))
+        do("S", cost(1, out, a), lambda s: s.activation(ap(out), ap(a), func, **{k: val(x) for k, x in kw.items()}), rd(a, *kw.values()), wr(out))
 
     def mm(out, l, r, start, stop):
-        do("P", lambda p: p.matmul(ap(out), ap(l), ap(r), start, stop), rd(l, r), wr(out))
+        c = max(min(64, size(l)), size(r)) * PCYC * (4 if SCRATCH[l[0]][2] == "float32" else 1)
+        calls.append(["P", c, 0.0, rd(l, r), wr(out), [], "do" if start else "add", lambda p: p.matmul(ap(out), ap(l), ap(r), start, stop)])
 
     def iota(out, pat, base=0, cm=0):
         kw = {} if SCRATCH[out[0]][2] == "int32" else {"allow_small_or_imprecise_dtypes": True}
-        do("G", lambda q: q.iota(ap(out), pat, base, cm, **kw), [], wr(out))
+        do("G", 0.13 + 2 * CYC * size(out), lambda q: q.iota(ap(out), pat, base, cm, **kw), [], wr(out))
 
     def pick(out, a, pat, base):
-        do("G", lambda q: q.affine_select(ap(out), ap(a), pat, OP.is_equal, 0.0, base, 1), rd(a), wr(out))
+        do("G", 0.17 + 2 * CYC * size(out), lambda q: q.affine_select(ap(out), ap(a), pat, OP.is_equal, 0.0, base, 1), rd(a), wr(out))
 
-    def send(in_, d, kind, e, t):
-        if tape[0] is not None:
-            tape[0].append(("send", (in_, d, kind, e, t)))
-            return
+    def send(in_, kind, e, t):
+        at, sem, at2, sem2 = {"g": (("LG", t * 1152 + (e - 1) * GH, GH), "ga%d_%d" % (e, t), ("RG", t * GH), "rg%d" % t),
+                              "s": (("SNL", (e - 1) * 24, 24), "sn%d" % e, ("RSN", 0), "rs"),
+                              "q": (("RIN", t * 8 + 2 * (e - 1), 2), "rq%d_%d" % (e, t), ("RRQ", t * 8), "rr%d" % t)}[kind]
+        sign = -1 if kind == "q" else 1
+        d, src = (rank + sign * e) % n, (rank - sign * e) % n
         k = rel[(rank, d)]
-        before("G", [in_], [])
-        if k is None:
-            out, sem = {"g": (("LG", t * 1152 + (e - 1) * GH), "ga%d_%d" % (e, t)), "s": (("SNL", (e - 1) * 24), "sn%d" % e),
-                        "q": (("RIN", t * 8 + 2 * (e - 1)), "rq%d_%d" % (e, t))}[kind]
-        else:
-            out, sem = {"g": (("RG", t * GH), "rg%d" % t), "s": (("RSN", 0), "rs"), "q": (("RRQ", t * 8), "rr%d" % t)}[kind]
-        to = T.cores[d] if k is None else k
-        rid, pid = topo.addr(to, core)
-        m = topo.mask(core, to)
-        g.remote_dma(T[out[0]][:, out[1]:out[1] + in_[2] - in_[1]], ap(in_), T.sem[sem], T.sem["ls"], pid, rid, m)
-        total["ls"] = total.get("ls", 0) + count(m)
+        to, out, rsem = (T.cores[d], at, sem) if k is None else (k, at2, sem2)
+        calls.append(["G", 0.3, 0.0, [in_], [], last_of("send", "G"), "send", (T[out[0]][:, out[1]:out[1] + at[2]], ap(in_), rsem, to)])
+        k = rel[(src, rank)]
+        due = count(topo.mask(T.cores[src] if k is None else k, core))
+        way = (NEAR if k is None else FAR) - (0.0 if kind == "g" else SMALL if k is None else 2 * SMALL)
+        calls.append(["in" + sem, 0.0, way, [], [(at[0], at[1], at[1] + at[2])], [len(calls) - 1], "lands", (sem, due)])
 
-    def due(d):
-        k = rel[(d, rank)]
-        return count(topo.mask(T.cores[d] if k is None else k, core))
-
-    def col(i):
-        return ("COL", i, i + 1)
+    def col(i, rows=128):
+        return ("COL", i, i + 1, 1, rows) if rows < 128 else ("COL", i, i + 1)
 
     def ci(i):
         return ("CI", i, i + 1)
 
-    QF, GF, N15, I15, SC, B1, HLF, THR, QP, TMPC, KB = [col(i) for i in range(11)]
-    NVB = [col(12 + i) for i in range(4)]
+    (QF, GF, N15, I15, I0, CEN, UNC, EPS, THE0, HLF, QR, TH, SB0, SB3, WTF, PF, Q8, QW, EMP) = [col(i) for i in range(19)]
+    NVB = [col(20 + t) for t in range(RO)]
+    THR = {c0: 24 + k for k, c0 in enumerate((0, 3, 7, 6, 11))}
+    DGA = {nc: 2 * k for k, nc in enumerate((3, 4, 5, 6, 7, 10, 11, 16))}
     WIN, OWN, NBW = ("XT", 0, WX), ("XT", 0, S), ("NBF", 0, WX)
     GM, GG = ("GM", 0, 128), ("GG", 0, 8)
+    far = [e for e in (1, 2, 3) if rel[(rank, (rank + e) % n)] is not None]
+    far_first = far + [e for e in (1, 2, 3) if e not in far]
 
-    dma("Y", "ld0", T["XT"][:, 0:S], T.x0[:, :], [], [OWN])
-    dma("S", "ld1", T["SND"][:, :], T.snd[:, :], [], [("SND", 0, 72)])
-    dma("Y", "ld2", T["NBI"][:, :], T.nb[:, :], [], [("NBI", 0, S)])
-    dma("S", "ld3", T["WAN"][:, :], T.wants[:, :], [], [("WAN", 0, 40)])
-    dma("S", "ld4", T["WTI"][:, 0:1], T.wt[:, :], [], [("WTI", 0, 1)])
-    dma("S", "ld5", T["PUL"][:, :], T.pull[:, :], [], [("PUL", 0, 512)])
+    dma("Y", "ld0", T["XR"][:, :], T.x0[:, :], [], [("XR", 0, S)], LOAD + 1.5)
+    dma("S", "ld1", T["SND"][:, :], T.snd[:, :], [], [("SND", 0, 72)], LOAD)
+    dma("Y", "ld3", T["WAN"][:, :], T.wants[:, :], [], [("WAN", 0, 40)], LOAD + 1.7)
+    dma("Y", "ld2", T["NBI"][:, :], T.nb[:, :], [], [("NBI", 0, S)], LOAD + 4.4)
+    dma("Y", "ld4", T["WTI"][:, 0:1], T.wt[:, :], [], [("WTI", 0, 1)], LOAD + 4.6)
+    dma("Y", "ld5", T["PUL"][:, :], T.pull[:, :], [], [("PUL", 0, 512)], LOAD + 5.0)
 
     iota(ci(0), [[1, 1]], 0, 1)
     iota(("TMF", 0, 128), [[1, 8], [0, 16]])
-    iota(("TM2", 0, 128), [[0, 8], [1, 16]])
-    iota(GG, [[1, 8]])
-    iota(("QX", 0, 256), [[1, 16], [0, 16]])
-    iota(("MSK", 0, 1024), [[0, 64], [1, 16]])
-    fill(("ONE", 0, 1024), 1.0)
+    iota(("NN", 0, 128), [[0, 8], [1, 16]])
+    iota(("GGK", 0, 128), [[0, 16], [1, 8]])
+    fill(("ONE", 0, 768), 1.0)
     pick(("IDB", 0, 128), ("ONE", 0, 128), [[-1, 128]], 0)
-    fill(("XT", NULL, WX), 0.0)
     ts(ci(1), ci(0), 15, OP.bitwise_and)
     ts(ci(2), ci(0), 4, OP.logical_shift_right)
+    fill(("XT", NULL, WX), 0.0)
     cp(QF, ci(1))
     cp(GF, ci(2))
+    cp(PF, ci(0))
+    fill(("ZER", 0, 96), 0.0)
     ts(N15, QF, 15.0, OP.is_lt)
     ts(I15, QF, 15.0, OP.is_equal)
-    ts(TMPC, I15, -256.0, OP.mult)
+    ts(I0, QF, 0.0, OP.is_equal)
+    ts(CEN, N15, -127.5, OP.mult)
+    ts(UNC, N15, 127.5, OP.mult)
+    ts(EPS, N15, -0.0625, OP.mult)
+    ts(THE0, N15, 1000.5, OP.mult, -0.5, OP.add)
+    ts(HLF, N15, 0.5, OP.mult)
+    ts(SB0, N15, 1.0625, OP.mult, -1.0, OP.add)
+    ts(SB3, N15, 128.5625, OP.mult, -1.0, OP.add)
+    for t in range(RO):
+        ts(NVB[t], I15, 192.0 + t, OP.mult, CEN if t + 1 < RO else 0.0, OP.add)
     ts(GM, ("TMF", 0, 128), GF, OP.is_equal)
-    ts(("TM2", 0, 128), ("TM2", 0, 128), 15.0, OP.is_lt)
-    tt(("TM2", 0, 128), ("TM2", 0, 128), GM, OP.mult)
-    ts(("EMP", 0, 128), ("TM2", 0, 128), TMPC, OP.mult)
-    ts(("EMN", 0, 128), ("EMP", 0, 128), -1.0, OP.mult)
+    ts(("GGK", 0, 128), ("GGK", 0, 128), GF, OP.is_equal)
+    cp(GG, ("GGK", 0, 8))
+    for x in "ABC":
+        act(("ZS" + x, 0, 512), ("ONE", 0, 512), AF.Identity, scale=0.0)
+        act(("R" + x, 0, 136), ("ONE", 0, 136), AF.Identity, scale=0.0)
+    fill(("STL", 0, 24), 0.0)
+    fill(("YO", S, NULL), 0.0)
+    for e in far_first:
+        send(("SND", (e - 1) * 24, e * 24), "s", e, 0)
     cp(("SNU", 0, 72), ("SND", 0, 72))
-    for x in "AB":
-        for k in (0, 1024):
-            act(("ZS" + x, k, k + 1024), ("ONE", 0, 1024), AF.Identity, scale=0.0)
-        act(("SZ" + x, 0, 128), ("ONE", 0, 128), AF.Identity, scale=0.0)
-    fill(("OL", 0, 32), 0)
-    ts(GG, GG, GF, OP.is_equal)
-    ts(("RD", 0, 8), GG, N15, OP.mult, 16777216.0, OP.mult)
-    ts(("RD", 8, 16), GG, I15, OP.mult, 69632.0, OP.mult)
-    cp(("RN", 0, 8), ("RD", 0, 8))
-    cp(("RN", 8, 16), ("RD", 0, 8))
-    ts(col(16), N15, -16777216.0, OP.mult)
-    ts(col(17), I15, -69632.0, OP.mult)
-    ts(col(18), GF, 8.0, OP.add)
-    ts(("TM2", 0, 256), ("QX", 0, 256), GF, OP.is_equal, col(16), OP.mult)
-    ts(("TM2", 256, 512), ("QX", 0, 256), col(18), OP.is_equal, col(17), OP.mult)
-    fill(("RS", 0, 128), 0.0)
-    tt(("RS", 128, 384), ("TM2", 0, 256), ("TM2", 256, 512), OP.add)
-    cp(("IDF", 0, 128), ("IDB", 0, 128))
-    ts(("IDN", 0, 128), ("IDB", 0, 128), -1.0, OP.mult)
-    ts(ci(3), ci(1), 7, OP.bitwise_and)
-    ts(ci(4), ci(1), 3, OP.logical_shift_right)
-    ts(col(19), ci(3), 8.0, OP.mult)
-    ts(col(20), ci(4), 8.0, OP.mult)
-    tt(col(21), col(19), GF, OP.add)
-    tt(col(22), col(21), col(19), OP.add)
-    tt(col(23), col(22), col(20), OP.add)
-    cp(("DG", 0, 1), col(21))
-    cp(("DG", 2, 3), col(23))
-    cp(("DG", 3, 4), col(23))
-    ban = ["PC0", "PC1", "PTA", "PTB"]
-    part = [(448 * k, 448 * (k + 1)) for k in range(4)]
-    for k, (a, b) in enumerate(part):
-        ts(("YO", a, b), ("XT", a, b), 0.0, OP.is_lt)
-        mm((ban[k], 0, 448), ("EMP", 0, 128), ("YO", a, b), True, True)
-    for k, (a, b) in enumerate(part):
-        tt(("XT", a, b), ("XT", a, b), (ban[k], 0, 448), OP.add)
+    ts(("RD", 0, 8), GG, N15, OP.mult, 16384.0, OP.mult)
+    ts(("RD", 8, 16), GG, I15, OP.mult, 4.25, OP.mult)
+    ts(("RS", 0, 128), GM, N15, OP.mult, -16384.0, OP.mult)
+    ts(("RS", 128, 256), GM, I15, OP.mult, -4.25, OP.mult)
+    ts(("RE", 0, 128), GM, I0, OP.mult, -15360.0, OP.mult)
+    ts(("M", 0, 128), ("NN", 0, 128), -0.25, OP.mult, MID / 16384.0 - 0.25, OP.add)
+    ts(EMP, I15, -1024.0, OP.mult)
+    ts(("TV", 0, 128), ("M", 0, 128), I0, OP.mult, EMP, OP.add)
+    tt(("RE", 128, 256), ("TV", 0, 128), GM, OP.mult)
+    ts(("IDK", 0, 128), ("IDB", 0, 128), 1.0 / 16384.0, OP.mult)
+    ts(("REP", 0, 128), ("NN", 0, 128), QF, OP.is_equal, 16384.0, OP.mult)
+    mm(("PM", 0, 96, 1, 96), ("IDB", 0, 96), ("ZER", 0, 96), True, True)
+    ts(("MSK", 0, 128), ("NN", 0, 128), 0.5, OP.is_gt)
+    cp(("MSK", 128, 256), ("MSK", 0, 128))
+    cp(("MSK", 256, 512), ("MSK", 0, 256))
+    ts(("DQ", 0, 128), ("NN", 0, 128), QF, OP.is_equal)
+    cp(("DQ", 128, 256), ("DQ", 0, 128))
 
     def ghosts(t):
         at = t * 1152
-        act(("GS", at, at + 384), ("I", OWN, ("SNU", 0, 24)))
-        cp(("GS", at + 768, at + 1152), ("I", OWN, ("SNU", 48, 72)))
-        send(("GS", at, at + 384), (rank + 1) % n, "g", 1, t)
-        send(("GS", at + 768, at + 1152), (rank + 3) % n, "g", 3, t)
-        act(("GS", at + 384, at + 576), ("I", OWN, ("SNU", 24, 36)))
-        cp(("GS", at + 576, at + 768), ("I", OWN, ("SNU", 36, 48)))
-        send(("GS", at + 384, at + 768), (rank + 2) % n, "g", 2, t)
-        for e in (1, 2, 3):
-            lands(("LG", at + (e - 1) * GH, at + e * GH), "ga%d_%d" % (e, t), due((rank - e) % n))
+        for e in far_first:
+            a, b, c = (e - 1) * GH, (e - 1) * GH + GH // 2, e * GH
+            if t:
+                act(("GS", at + a, at + b), ("I", OWN, ("SNU", a // 16, b // 16)))
+                cp(("GS", at + b, at + c), ("I", OWN, ("SNU", b // 16, c // 16)))
+            else:
+                act(("GS", a, b), ("I", ("XR", 0, S), ("SNU", a // 16, b // 16)), AF.Identity, bias=CEN)
+                ts(("GS", b, c), ("I", ("XR", 0, S), ("SNU", b // 16, c // 16)), CEN, OP.add)
+            send(("GS", at + a, at + c), "g", e, t)
 
     ghosts(0)
-    for e in (1, 3, 2):
-        send(("SND", (e - 1) * 24, e * 24), (rank + e) % n, "s", e, 0)
-        lands(("SNL", (e - 1) * 24, e * 24), "sn%d" % e, due((rank - e) % n))
-
-    iota(("IOT", 0, WX), [[1, WX]])
-    pick(("EXP", 0, 2048 - V16), ("ONE", 0, 2048 - V16), [[-1, 128 - VL], [0, 16]], -VL)
-    pick(("REB", 0, 128), ("ONE", 0, 128), [[0, 8], [-1, 16]], 0)
-    pick(("PRB", 0, 1024), ("ONE", 0, 1024), [[-16, 8], [0, 8], [-1, 16]], 0)
-    iota(("TMF", 0, 256), [[0, 16], [1, 16]])
-    iota(("TRS", 0, 32), [[16, 32]], TRASH)
-    for b, lo, hi in (("GST", 0, S), ("GST", NULL, WX), ("EQ", 0, 4096)):
-        iota((b, lo, hi), [[0, hi - lo]])
-    ts(KB, QF, 1.0, OP.add, -4096.0, OP.mult)
-    ts(("MSK", 0, 1024), ("MSK", 0, 1024), 0.5, OP.is_gt)
-    cp(("NBF", 0, S), ("NBI", 0, S))
-    act(("NBF", S, WX), ("IOT", S, WX))
-    act(("REP", 0, 128), ("REB", 0, 128))
-    ts(("WZ", 8, 16), GG, I15, OP.mult)
-    cp(SC, N15)
-    ts(B1, N15, -255.0, OP.mult, -1.0, OP.add)
-    ts(HLF, N15, 0.5, OP.mult)
-    ts(col(24), N15, -8388608.0, OP.mult)
-    for t in range(RO):
-        ts(NVB[t], I15, float(192 + t), OP.mult, col(24), OP.add)
-    fill(QP, 32768.0)
+    for k in (0, 1):
+        iota(("NBF", S + 584 * k, S + 584 * k + 584), [[1, 584]], S + 584 * k)
+    for k in range(3):
+        pick(("EXP", 512 * k, 512 * k + 512), ("ONE", 0, 512), [[-1, 32], [0, 16]], -32 * k)
+    for k in (0, 1):
+        pick(("PRB", 384 * k, 384 * k + 384), ("ONE", 0, 384), [[-16, 3], [0, 8], [-1, 16]], -48 * k)
     for k in range(4):
-        ts(ci(8), ci(1), k, OP.logical_shift_right, 1, OP.bitwise_and)
-        ts(col(25), ci(8), 2.0 ** -(2 ** k) - 1.0, OP.mult, 1.0, OP.add)
-        tt(QP, QP, col(25), OP.mult)
-    for c in range(8):
-        w = 2.0 ** (17 * (7 - c) - 44)
-        ts(("WM", c * 24, c * 24 + 8), GG, QP, OP.mult, w, OP.mult)
-        ts(("WM", c * 24 + 8, c * 24 + 16), GG, QP, OP.mult, w, OP.mult)
-        ts(("WM", c * 24 + 16, c * 24 + 24), GG, 2.0 ** 92, OP.mult)
-        fill(("GG", 16 + c, 17 + c), 2.0 * w)
-    tt(("GG", 32, 40), GG, ("GG", 16, 24), OP.mult)
-    tt(("GG", 32, 36), ("GG", 32, 36), ("GG", 36, 40), OP.add)
-    tt(("GG", 32, 34), ("GG", 32, 34), ("GG", 34, 36), OP.add)
-    tt(col(26), ("GG", 32, 33), ("GG", 33, 34), OP.add)
-    tt(THR, col(26), QP, OP.mult)
-    ts(col(27), QF, 1.0, OP.add, 512.0, OP.mult)
-    ts(("GM2", 0, 128), GM, col(27), OP.mult)
-    act(("PRF", 0, 1024), ("PRB", 0, 1024))
+        iota(("IOT", 448 * k, 448 * k + 448), [[1, 448]], 448 * k)
+    iota(("IOT", NULL, WX), [[1, WX - NULL]], NULL)
+    for k in range(8):
+        iota(("EQ", 512 * k, 512 * k + 512), [[0, 512]])
+    for k in range(4):
+        ts(("XT", 448 * k, 448 * k + 448), ("XR", 448 * k, 448 * k + 448), CEN, OP.add)
+    for k in range(8):
+        cp(("NBF", 224 * k, 224 * k + 224), ("NBI", 224 * k, 224 * k + 224))
+        cp(("WK", k, 320, 8), ("WAN", 0, 40))
+    for k, (nc, at) in enumerate(DGA.items()):
+        ts(col(44 + k), QF, float(nc - 1), OP.min, 8.0, OP.mult)
+        for j in (0, 1):
+            ts(("DG", at + j, at + j + 1), col(44 + k), GF, OP.add)
+    ts(Q8, QF, 8.0, OP.is_ge)
+    ts(col(56), Q8, -8.0, OP.mult, QF, OP.add)
+    ts(col(57), col(56), 16.0, OP.mult, 15.0 - 128.0, OP.add)
+    tt(col(58), GF, Q8, OP.subtract)
+    for k in range(3):
+        ts(("RL", k, k + 1), Q8, 2.0 * k, OP.add)
+        ts(col(59 + k), col(58), 2.0 * k, OP.is_equal, col(57), OP.mult)
+        ts(("XL", k, k + 1), col(59 + k), 128.0, OP.add)
+    cp(WTF, ("WTI", 0, 1))
+    ts(("WZ", 0, 8), GG, WTF, OP.mult, N15, OP.mult)
+    ts(("WZ", 8, 16), GG, I15, OP.mult)
+    ts(("WY", 0, 8), ("WZ", 0, 8), 128.0, OP.mult)
+    ts(("WY", 8, 16), ("WZ", 0, 8), -0.4375, OP.mult)
+    fill(QR, TOP)
+    fill(("WC", 16, 32), RATIO ** -16)
+    for k in range(4):
+        ts(ci(8 + k), ci(1), k, OP.logical_shift_right, 1, OP.bitwise_and)
+        ts(col(52 + k), ci(8 + k), RATIO ** -(2 ** k) - 1.0, OP.mult, 1.0, OP.add)
+    for k in (0, 2):
+        ts(QR, QR, col(52 + k), OP.mult, col(53 + k), OP.mult)
+    ts(QR, QR, RATIO ** 16, OP.mult)
+    scan(("WC", 0, 16), ("WC", 16, 32), ("ZER", 0, 16), OP.mult, OP.add, QR)
+    ts(("THE", 0, 16), ("NN", 0, 16), GF, OP.is_equal)
+    tt(("THE", 16, 32), ("THE", 0, 16), ("WC", 0, 16), OP.mult)
+    do("V", 64 * CYC, lambda v: v.tensor_reduce(ap(TH), ap(("THE", 16, 32)), AxisListType.X, OP.add), [("THE", 16, 32)], [TH])
+    for c0, k in THR.items():
+        ts(col(k), TH, RATIO ** (-8 * c0), OP.mult, 2.54 * RATIO ** (-8 * c0), OP.mult)
+    for b in range(3):
+        ts(col(32 + b), PF, 2.0, OP.mult, TRASH + 192.0 * b, OP.add)
+        for k in (0, 1):
+            act(("PRW", 768 * b + 384 * k, 768 * b + 384 * k + 384), ("PRB", 384 * k, 384 * k + 384), AF.Identity, scale=col(32 + b))
+    ts(QW, QF, 1.0, OP.add, 512.0, OP.mult)
+    ts(("GM2", 0, 128), GM, QW, OP.mult)
+    for k in (0, 256):
+        act(("PUF", k, k + 256), ("PUL", k, k + 256), AF.Identity, bias=127.0)
+        act(("PUF", 512 + k, 768 + k), ("PUL", k, k + 256), AF.Identity, bias=-0.5)
+    for e in (1, 2, 3, 4):
+        ts(col(35 + e), QF, float(e - 1), OP.is_equal)
+        for lo, hi in [(S + (e - 1) * GH, S + e * GH)] if e < 4 else [(448 * k, 448 * k + 448) for k in range(4)] + [(NULL, WX)]:
+            act(("EIN", lo, hi), ("XR", 0, hi - lo), AF.Identity, scale=0.0, bias=col(35 + e))
+    for e in (1, 2, 3):
+        cp(("SLU", (e - 1) * 24, e * 24), ("SNL", (e - 1) * 24, e * 24))
+        for k in (0, 1):
+            lo = (e - 1) * GH + 192 * k
+            act(("IOT", S + lo, S + lo + 192), ("I", ("IOT", 0, S), ("SLU", lo // 16, lo // 16 + 12)))
 
-    def later_consts():
-        ts(("DQ", 0, 256), ("TMF", 0, 256), QF, OP.is_equal)
-        ts(("TRS", 0, 32), ("TRS", 0, 32), QF, OP.add)
-        cp(TMPC, ("WTI", 0, 1))
-        ts(("WZ", 0, 8), GG, TMPC, OP.mult, N15, OP.mult)
-        for e, lo, hi in ((1, S, S + GH), (2, S + GH, S + 2 * GH), (3, S + 2 * GH, NULL), (4, 0, S), (4, NULL, WX)):
-            if lo != NULL:
-                ts(col(27 + e), QF, float(e - 1), OP.is_equal)
-            act(("EIN", lo, hi), ("IOT", lo, hi), AF.Identity, scale=0.0, bias=col(27 + e))
-        for e in (2, 1, 3):
-            lo = S + (e - 1) * GH
-            cp(("SLU", (e - 1) * 24, e * 24), ("SNL", (e - 1) * 24, e * 24))
-            act(("GST", lo, lo + GH), ("I", ("IOT", 0, S), ("SLU", (e - 1) * 24, e * 24)))
+    def geo(t, x):
+        c0, nc = BLOCKS[t][x]
+        return c0, nc, 16 * nc, FUSED[16 * nc]
 
-    O8 = {"A": 0, "B": 8}
-
-    def OFX(x, a, b):
-        return ("OFX", O8[x] + a, O8[x] + b)
-
-    def OLD(x, a, b):
-        return ("OL", 2 * O8[x] + a, 2 * O8[x] + b)
-
-    def start_a(t):
-        cp(OLD("A", 6, 8), ("WAN", t * 10, t * 10 + 2))
-        if t == 0:
-            fill(OLD("A", 0, 6), NULL)
+    def own(t, x, h, win):
+        c0, nc, L, a = geo(t, x)
+        ps, of, zs = "P" + x, ("OF" + x, 0, nc), ("ZS" + x, 0, 16 * L, 16)
+        act(("BS" + x, 0, L), ("I", NBW, of), AF.Identity, bias=-MID)
+        act(zs, ("I", win, of), AF.Identity, bias=EPS)
+        if ONV:
+            cp(("ON" + x, 0, L), ("I", NBW, of))
         else:
-            cp(OLD("A", 0, 6), ("RIN", t * 8, t * 8 + 6))
-        cp(OFX("A", 0, 8), OLD("A", 0, 8))
+            ts(("ON" + x, 0, L), ("BS" + x, 0, L), MID, OP.add)
+        mm((ps, 256, 384, 1, L), zs, ("IDB", 0, 128), True, True)
+        act(("ST" + x, 0, 128, 1, L), (ps, 256, 384, 1, L))
+        if h == 0:
+            ts(("E" + x, 0, L), zs, THE0, OP.is_lt)
+        mm((ps, 0, 256, 1, L), zs, ("RS", 0, 256), True, False)
+        mm((ps, 0, 256, 1, L), ("E" + x, 0, L), ("RE", 0, 256), False, False)
+        mm((ps, 128, 256, 1, L), ("BS" + x, 0, L), ("IDK", 0, 128), False, False)
 
-    def own_v(x, win):
-        cp(("ON" + x, 0, 128), ("I", NBW, OFX(x, 0, 8)))
-        cp(("ZS" + x, 0, V16, 16), ("I", win, OFX(x, 0, VL // 16)))
+    def start(t, x):
+        c0, nc, L, a = geo(t, x)
+        if t and x == "A":
+            cp(("OFA", 0, 6), ("RIN", 8 * t, 8 * t + 6))
+            cp(("OL", 0, 48), ("I", ("RIN", 8 * t, 8 * t + 6), ("RL", 0, 3)))
+        else:
+            w = 10 * t + c0 - (6 if t else 0)
+            cp(("OF" + x, 0, nc), ("WAN", w, w + nc))
+        own(t, x, 0, OWN if not (t and x == "A") else WIN)
 
-    def own_s(x, win):
-        act(("SZ" + x, VL, 128), ("I", win, OFX(x, VL // 16, 8)))
-        mm(("PT" + x, 128, 256), ("SZ" + x, 0, 128), ("IDN", 0, 128), True, True)
-        act(("BS" + x, 0, 128), ("I", NBW, OFX(x, 0, 8)), AF.Identity, bias=KB)
-        mm(("P" + x, 0, 384), ("SZ" + x, 0, 128), ("RS", 0, 384), True, False)
-        mm(("P" + x, 256, 384), ("BS" + x, 0, 128), ("IDF", 0, 128), False, False)
+    def look(t, x, par):
+        c0, nc, L, a = geo(t, x)
+        ps = "P" + x
+        scan(("SB", 0, 16 * a), ("MSK", 0, 16 * a), ("ZS" + x, 0, 16 * a), OP.mult, OP.add)
+        for l in range(0, a, PIECE[0]):
+            m = min(l + PIECE[0], a)
+            tt(("D" + x, 16 * l, 16 * m), ("I", WIN, ("ON" + x, l, m)), ("SB", 16 * l, 16 * m), OP.max)
+        for k, l0 in enumerate(range(a, L, 32)):
+            l1, at, bank = min(l0 + 32, L), 1536 * par + 512 * k, "X%d" % (k % 2)
+            for l in range(0, l1 - l0, PIECE[2]):
+                m = min(l + PIECE[2], l1 - l0)
+                act(("RAW", at + 16 * l, at + 16 * m), ("I", WIN, ("ON" + x, l0 + l, l0 + m)))
+            mm((bank, 0, 16 * (l1 - l0)), ("ST" + x, 0, 128, 1, L), ("EXP", 16 * l0, 16 * l1, 1, L), True, True)
+            for l in range(0, l1 - l0, PIECE[1]):
+                m = min(l + PIECE[1], l1 - l0)
+                tt(("D" + x, 16 * (l0 + l), 16 * (l0 + m)), ("RAW", at + 16 * l, at + 16 * m), (bank, 16 * l, 16 * m), OP.max)
+        for l0, l1 in ((0, CUT[L]), (CUT[L], L)):
+            for i in range(16):
+                mm((ps, i, 256, 16, l1, l0), ("D" + x, 16 * l0 + i, 16 * l1, 16), ("RD", 0, 16), False, i == 15)
+        ts(("WI", 0, 128, 1, L), (ps, 0, 128, 1, L), 0.0, OP.max)
+        ts(("FI", 0, 128, 1, L), ("WI", 0, 128, 1, L), 15 * 1024, OP.bitwise_and)
+        tt(("M", 0, 128, 1, L), ("FI", 0, 128, 1, L), (ps, 128, 256, 1, L), OP.min)
+        scan(("R" + x, 0, 128, 1, L), ("MSK", 0, 128, 1, L), ("M", 0, 128, 1, L), OP.mult, OP.max)
 
-    def prep_b(t):
-        cp(OLD("B", 0, 8), ("WAN", t * 10 + 2, t * 10 + 10))
-        cp(OFX("B", 0, 8), OLD("B", 0, 8))
-        own_s("B", OWN)
-        own_v("B", OWN)
+    def step(t, x, h):
+        c0, nc, L, a = geo(t, x)
+        k = (nc + 1) // 2
+        act(("KQ", 0, 16 * k), ("I", ("R" + x, 0, 136), ("XL", 0, k)))
+        mm(("PT", 0, 8 * nc), ("REP", 0, 128), ("KQ", 0, 8 * nc), True, True)
+        ol = ("OL", 8 * c0, 8 * (c0 + nc))
+        w = 8 * (10 * t + c0 - (6 if t else 0))
+        tt(("KI", 0, 8 * nc), ("PT", 0, 8 * nc), ol if h or (t and x == "A") else ("WK", w, w + 8 * nc), OP.max)
+        ts(ol, ("KI", 0, 8 * nc), 4095, OP.bitwise_and)
+        if h < 2:
+            cp(("OF" + x, 0, 16), ("I", ol, ("DG", DGA[nc], DGA[nc] + 1)))
+            own(t, x, h + 1, WIN)
 
-    def ghosts_in(t):
-        for e in (2, 1, 3):
-            lo = (e - 1) * GH
-            act(("XT", S + lo, S + lo + GH), ("LG", t * 1152 + lo, t * 1152 + lo + GH))
+    def cols(t):
+        return sum(nc for c0, nc in BLOCKS[t].values())
 
-    def own_t(x):
-        act(("ST" + x, 0, 128), ("PT" + x, 128, 256))
+    def part(t, only):
+        mine = [(b, x) + geo(t, x) for b, x in enumerate("ABC") if x in only]
+        lo, hi = mine[0][2], mine[-1][2] + mine[-1][3]
+        return mine, 8 * mine[0][0], 8 * mine[-1][0] + 8, lo, hi, ("DG", DGA[hi - lo], DGA[hi - lo] + 1), 0 if lo == 0 else 32
 
-    def gather_s(x, k):
-        a = V16 + 512 * k
-        act(("D" + x, a, a + 512), ("I", WIN, ("ON" + x, a // 16, a // 16 + 32)))
+    def turn(mine, mat, stride, src):
+        for b, x, c0, nc, L, a in mine:
+            for c in range(nc):
+                at = stride * b + 128 * c
+                mm(("PM2", 8 * (c0 + c), 8 * (c0 + c) + 8), (mat, at, at + 128, 1, 96), (src, 8 * b, 8 * b + 8, 1, 96), True, True)
 
-    def diff(x, k):
-        a, pc = V16 + 512 * k, ("PC%d" % k, 0, 512)
-        mm(pc, ("IDB", 0, 128), ("D" + x, a, a + 512), True, False)
-        mm(pc, ("ST" + x, 0, 128), ("EXP", 512 * k, 512 * k + 512), False, True)
-
-    def relu(x, k):
-        a = V16 + 512 * k
-        act(("N" + x, a, a + 512), ("PC%d" % k, 0, 512), AF.Relu, scale=-1.0)
-
-    def big_v(x):
-        scan(("SB" + x, 0, V16), ("MSK", 0, V16), ("ZS" + x, 0, V16), OP.mult, OP.add)
-        for k in range(4):
-            a, b = V16 // 4 * k, V16 // 4 * (k + 1)
-            tt(("D" + x, a, b), ("I", WIN, ("ON" + x, a // 16, b // 16)), ("SB" + x, a, b), OP.subtract)
-        for k in range(4):
-            a, b = V16 // 4 * k, V16 // 4 * (k + 1)
-            ts(("N" + x, a, b), ("D" + x, a, b), -1.0, OP.mult, 0.0, OP.max)
-
-    def sums(ps, buf, rhs, lo, stop):
-        for i in range(16):
-            mm((ps, lo + i, lo + 256, 16), (buf, i, 2048, 16), (rhs, 0, 16), False, stop and i == 15)
-
-    def best_s(x):
-        act(("TA" + x, 0, 128), ("P" + x, 0, 128))
-
-    def best(x):
-        ps, m = "P" + x, "M" + x
-        tt((m, 0, 128), ("TA" + x, 0, 128), (ps, 128, 256), OP.min)
-        tt((m, 128, 256), (m, 0, 128), (ps, 256, 384), OP.min)
-        scan(("R" + x, 0, 128), ("MSK", 0, 128), (m, 128, 256), OP.mult, OP.max)
-
-    def turn(ps, w, mat, rhs):
-        for c in range(8):
-            mm((ps, c * w, c * w + w), (mat, c * 128, c * 128 + 128), rhs, True, True)
-
-    def perm(x):
-        for c in range(8):
-            mm(("PT" + x, 64 + c * 8, 72 + c * 8, 1, 16), ("IDF", c * 16, c * 16 + 16), ("R" + x, 15, 128, 16), True, True)
-
-    def step(x):
-        cp(("KQ" + x, 0, 64, 1, 16), ("PT" + x, 64, 128, 1, 16))
-        mm(("PT" + x, 0, 64), ("REP", 0, 128, 1, 16), ("KQ" + x, 0, 64, 1, 16), True, True)
-        cp(("KS" + x, 0, 64), ("PT" + x, 0, 64))
-        tt(("KI" + x, 0, 16), ("I", ("KS" + x, 0, 64), ("DG", 0, 1)), OLD(x, 0, 16), OP.max)
-        ts(OLD(x, 0, 16), ("KI" + x, 0, 16), 4095, OP.bitwise_and)
-        cp(OFX(x, 0, 8), OLD(x, 0, 8))
-
-    def places_p():
-        for b, x in enumerate("AB"):
-            for k in (0, 8):
-                o = ("PM", 2 * k + 8 * b, 2 * k + 8 * b + 8)
-                mm(o, ("ZS" + x, 0, 2048, 16), ("WZ", k, k + 8), True, False)
-                mm(o, ("SZ" + x, 0, 128), ("WZ", k, k + 8), False, True)
-
-    def places(t):
-        z = [("ZI", 16 * i, 16 * i + 16) for i in range(8)]
-        ts(("DL", 16, 32), ("PM", 16, 32), 0.0, OP.is_lt, float(NULL), OP.mult)
-        cp(z[0], ("PM", 0, 16))
+    def places(t, only):
+        mine, b0, b1, lo, hi, dg, o = part(t, only)
+        last, j0, j1 = int(t + 1 == RO), 16 * lo, 16 * hi
+        for b, x, c0, nc, L, a in mine:
+            zs = ("ZS" + x, 0, 16 * L, 16)
+            mm(("PM", 8 * b, 8 * b + 8, 1, L), zs, ("WZ", 0, 8), True, False)
+            mm(("PM", 8 * b, 8 * b + 8, 1, L), ("E" + x, 0, L), ("WY", 0, 8), False, False)
+            mm(("PM", 8 * b, 8 * b + 8, 1, L), ("E" + x, 0, L), ("WY", 8, 16), False, True)
+            mm(("PM", 24 + 8 * b, 32 + 8 * b, 1, L), zs, ("WZ", 8, 16), True, True)
+            act(("VAL", 256 + 16 * c0, 256 + 16 * c0 + L), zs, AF.Identity, scale=N15, bias=SB3 if last else SB0)
+        z = [("ZI", 24 * i + b0, 24 * i + b1, 1, 96) for i in range(7)]
+        sd, ss, inv, dof = ("SD", o, o + 16), ("SD", o + 16, o + 32), ("INV", o // 2, o // 2 + 16), ("DOF", o // 2, o // 2 + hi - lo)
+        cp(ss, ("I", ("OL", 8 * lo, 8 * hi), dg))
+        cp(z[0], ("PM", b0, b1, 1, 96))
         ts(z[1], z[0], 2047, OP.bitwise_and)
+        ts(("DN", b0, b1, 1, 96), ("PM", 24 + b0, 24 + b1, 1, 96), 0.0, OP.is_lt, float(NULL), OP.mult)
         tt(z[2], z[1], z[1], OP.mult)
-        ts(z[3], z[2], float(97 * t * 32), OP.add)
-        ts(z[4], z[3], 5, OP.logical_shift_right, 2047, OP.bitwise_and)
+        if t:
+            ts(z[3], z[2], float(97 * t * 32), OP.add)
+        ts(z[4], z[3 if t else 2], 5, OP.logical_shift_right, 2047, OP.bitwise_and)
         ts(z[5], z[4], float(S), OP.is_ge, -float(S), OP.mult)
         tt(z[6], z[4], z[5], OP.add)
-        tt(("DL", 0, 16), z[6], ("DL", 16, 32), OP.max)
-        turn("PM2", 16, "PRF", ("DL", 0, 16))
-        for k, x in ((0, "A"), (8, "B")):
-            ts(("INV", k, k + 8), OLD(x, 0, 8), float(S), OP.is_ge, float(NULL), OP.mult)
-            cp(("SD", 16 + k, 24 + k), OLD(x, 0, 8))
+        tt(("DL", b0, b1, 1, 96), z[6], ("DN", b0, b1, 1, 96), OP.max)
+        turn(mine, "PRB", 0, "DL")
+        act(("KD", 8 * lo, 8 * hi), ("PM2", 8 * lo, 8 * hi))
+        ts(inv, ss, float(S), OP.is_ge, float(NULL), OP.mult)
+        tt(sd, ("I", ("KD", 8 * lo, 8 * hi), dg), inv, OP.max)
+        cp(("DOF", o // 2, o // 2 + 16), sd)
+        act(("DBC", j0, j1), ("I", ("IOT", 0, WX), dof))
+        for c in range(lo, hi):
+            ts(("EQ", c * 272, c * 256 + j1), ("DBC", 16 * c, j1), ("SD", o + c - lo, o + c - lo + 1), OP.is_equal, ("WC", c, c + 1), OP.mult)
+        cp(("POI", o, o + 16), sd)
+        ts(("POI", o + 16, o + 32), ("POI", o, o + 16), 511, OP.bitwise_and)
+        cp(("POF", o // 2, o // 2 + 16), ("POI", o + 16, o + 32))
+        tt(("TV", j0, j1), ("I", ("PUF", 512 * last, 512 * last + 512), ("POF", o // 2, o // 2 + hi - lo)), ("VAL", 256 + j0, 256 + j1), OP.add)
+        ts(("TV2", j0, j1), ("TV", j0, j1), MAGIC, OP.add, -MAGIC, OP.add)
+        act(("VAL", j0, j1), ("TV2", j0, j1), AF.Identity, scale=HLF, bias=NVB[t])
 
-    def places2():
-        cp(("KD", 0, 128), ("PM2", 0, 128))
-        tt(("SD", 0, 16), ("I", ("KD", 0, 128), ("DG", 2, 3)), ("INV", 0, 16), OP.max)
-        cp(("DOF", 0, 16), ("SD", 0, 16))
-        cp(("DBC", 0, 256), ("I", ("IOT", 0, WX), ("DOF", 0, 16)))
+    def moves(t, only):
+        mine, b0, b1, lo, hi, dg, o = part(t, only)
+        to = "XT" if t + 1 < RO else "YO"
+        act(("XD", 16 * lo, 16 * hi), ("I", (to, 0, WX), ("DOF", o // 2, o // 2 + hi - lo)))
+        if lo:
+            leave(t, "AB")
+        for b, x, c0, nc, L, a in mine:
+            mm(("PM", 48 + 8 * b, 56 + 8 * b, 1, L), ("XD", 16 * c0, 16 * c0 + L), ("WZ", 8, 16), True, True)
+        for b, x, c0, nc, L, a in mine:
+            ts(("THE", 8 * b, 8 * b + 8, 1, 96), ("PM", 48 + 8 * b, 56 + 8 * b, 1, 96), 0.0, OP.is_lt, col(THR[c0], 96), OP.mult)
+            ts(("STL", 8 * b, 8 * b + 8, 1, L), ("R" + x, 15, 128, 16, L), 0.0, OP.is_equal)
+        turn(mine, "PRB", 0, "STL")
+        tt(("RW", 8 * lo, 8 * hi), ("PM2", 8 * lo, 8 * hi), ("GGK", 8 * lo, 8 * hi), OP.mult)
+        tt(("THE", 24 + b0, 24 + b1, 1, 96), ("THE", b0, b1, 1, 96), ("STL", b0, b1, 1, 96), OP.mult)
+        for b, x, c0, nc, L, a in mine:
+            for c in range(lo, c0 + nc):
+                at = c * 256 + 16 * c0
+                mm(("PM", 72 + 8 * b, 80 + 8 * b, 1, L), ("EQ", at, at + L), ("RW", 8 * c, 8 * c + 8), c == lo, c == c0 + nc - 1)
+        tt(("LB", b0, b1, 1, 96), ("PM", 72 + b0, 72 + b1, 1, 96), ("THE", 24 + b0, 24 + b1, 1, 96), OP.is_ge)
+        turn(mine, "PRW", 768, "LB")
+        act(("KL", 8 * lo, 8 * hi), ("PM2", 8 * lo, 8 * hi))
+        tt(("LW", o, o + 32), ("I", ("KL", 8 * lo, 8 * hi), (dg[0], dg[1], dg[1] + 2)), ("SD", o, o + 32), OP.max)
+        cp(("OFS", o, o + 32), ("LW", o, o + 32))
+        cp(("I", (to, 0, 3584), ("OFS", o, o + hi - lo)), ("VAL", 16 * lo, 16 * hi))
 
-    def places3():
-        cp(("POI", 0, 16), ("SD", 0, 16))
-        for c in range(16):
-            ts(("EQ", c * 272, c * 256 + 256), ("DBC", 16 * c, 256), ("SD", c, c + 1), OP.is_equal)
-            if c == 5:
-                ts(("POI", 16, 32), ("POI", 0, 16), 511, OP.bitwise_and)
-            if c == 10:
-                cp(("POF", 0, 16), ("POI", 16, 32))
-
-    def places4():
-        for o, x in ((0, "A"), (128, "B")):
-            p, q = o // 16, (o + VL) // 16
-            tt(("TV", o, o + VL), ("I", ("PUL", 0, 512), ("POF", p, q)), ("ZS" + x, 0, V16, 16), OP.add)
-            tt(("TV", o + VL, o + 128), ("I", ("PUL", 0, 512), ("POF", q, p + 8)), ("SZ" + x, VL, 128), OP.add)
-
-    def places_s():
-        act(("XD", 0, 256), ("I", WIN, ("DOF", 0, 16)))
-        for b in (0, 1):
-            mm(("PM", 32 + 8 * b, 40 + 8 * b), ("XD", 128 * b, 128 * b + 128), ("WZ", 8, 16), True, True)
-        for o, x in ((256, "A"), (384, "B")):
-            act(("VAL", o, o + VL), ("ZS" + x, 0, V16, 16), AF.Identity, scale=SC, bias=B1)
-            act(("VAL", o + VL, o + 128), ("SZ" + x, VL, 128), AF.Identity, scale=SC, bias=B1)
-
-    def moves(t):
-        for k, x in ((0, "A"), (8, "B"), (16, "A")):
-            ts(("STL", k, k + 8), ("R" + x, 15, 128, 16), 0.0, OP.is_equal)
-        turn("PM2", 24, "PRB", ("STL", 0, 24))
-        places4()
-        ts(("THE", 0, 16), ("PM", 32, 48), 0.0, OP.is_lt, THR, OP.mult)
-        tt(("THE", 16, 32), ("THE", 0, 16), ("STL", 0, 16), OP.mult)
-        tt(("RW", 0, 192), ("PM2", 0, 192), ("WM", 0, 192), OP.mult)
-        for c in range(8):
-            mm(("PM", 0, 8), ("EQ", c * 256, c * 256 + 128), ("RW", c * 24, c * 24 + 8), c == 0, c == 7)
-        for c in range(16):
-            o = (c % 8) * 24 + (8 if c >= 8 else 16)
-            mm(("PM", 8, 16), ("EQ", c * 256 + 128, c * 256 + 256), ("RW", o, o + 8), c == 0, c == 15)
-        ts(("TV2", 0, 256), ("TV", 0, 256), -0.5, OP.add, 16777216.0, OP.add)
-        act(("VAL", 0, 256), ("TV2", 0, 256), AF.Identity, scale=HLF, bias=NVB[t])
-        tt(("LB", 0, 16), ("PM", 0, 16), ("THE", 16, 32), OP.is_ge)
-        turn("PM2", 16, "PRB", ("LB", 0, 16))
-        cp(("KL", 0, 128), ("PM2", 0, 128))
-        tt(("LW", 0, 32), ("I", ("KL", 0, 128), ("DG", 2, 4)), ("TRS", 0, 32), OP.mult)
-        tt(("LW", 32, 64), ("LW", 0, 32), ("SD", 0, 32), OP.max)
-        cp(("OFS", 0, 32), ("LW", 32, 64))
-        cp(("I", ("XT", 0, 3584), ("OFS", 0, 32)), ("VAL", 0, 512))
+    def leave(t, only):
+        mine, b0, b1, lo, hi, dg, o = part(t, only)
+        cp(("I", ("XT" if t + 1 < RO else "YO", 0, 3584), ("OFS", o + 16, o + 16 + hi - lo)), ("VAL", 256 + 16 * lo, 256 + 16 * hi))
 
     def requests(t):
-        act(("GV", 0, 256), ("I", ("GST", 0, WX), ("OFX", 0, 16)))
+        nt = cols(t)
+        NL, of = 16 * nt, ("OFX", 0, nt)
+        cp(("OFX", 0, 16), ("I", ("OL", 0, 8 * nt), ("DG", DGA[nt], DGA[nt] + 1)))
+        act(("GV", 0, NL), ("I", ("IOT", 0, WX), of))
         for e in (1, 2, 3):
-            act(("REQ", 512 * e + 1, 512 * e + 33), ("IOT", 0, CAP), AF.Identity, scale=0.0, bias=float(NULL))
-        cp(("IND", 0, 256), ("I", ("EIN", 0, WX), ("OFX", 0, 16)))
-        scan(("CNT", 0, 256), ("ONE", 0, 256), ("IND", 0, 256), OP.mult, OP.add)
-        tt(("QC", 0, 256), ("IND", 0, 256), ("CNT", 0, 256), OP.mult)
-        mm(("PC0", 0, 256), ("GM2", 0, 128), ("IND", 0, 256), True, False)
-        mm(("PC0", 0, 256), GM, ("QC", 0, 256), False, True)
-        tt(("QX", 0, 256), ("PC0", 0, 256), ("DQ", 0, 256), OP.mult)
-        scan(("QX", 256, 512), ("MSK", 0, 256), ("QX", 0, 256), OP.mult, OP.add)
-        cp(("RQF", 0, 16), ("QX", 271, 512, 16))
-        cp(("I", ("REQ", 0, 2320), ("RQF", 0, 16)), ("GV", 0, 256))
+            act(("REQ", 512 * e + 1, 512 * e + 33), ("NN", 0, CAP), AF.Identity, scale=0.0, bias=float(NULL))
+        act(("IND", 0, NL), ("I", ("EIN", 0, WX), of))
+        scan(("CNT", 0, NL), ("ONE", 0, NL), ("IND", 0, NL), OP.mult, OP.add)
+        tt(("QC", 0, NL), ("IND", 0, NL), ("CNT", 0, NL), OP.mult)
+        mm(("PT", 128, 128 + NL), ("GM2", 0, 128), ("IND", 0, NL), True, False)
+        mm(("PT", 128, 128 + NL), GM, ("QC", 0, NL), False, True)
+        tt(("QX", 0, NL), ("PT", 128, 128 + NL), ("DQ", 0, NL), OP.mult)
+        scan(("QX", 256, 256 + NL), ("MSK", 0, NL), ("QX", 0, NL), OP.mult, OP.add)
+        cp(("RQF", 0, nt), ("QX", 271, 256 + NL, 16))
+        cp(("I", ("REQ", 0, 2320), ("RQF", 0, nt)), ("GV", 0, NL))
         for e in (1, 2, 3):
             tt(("RX", 32 * e - 32, 32 * e), ("REQ", 512 * e + 1, 512 * e + 33), ("DQ", 0, CAP), OP.mult)
         scan(("RX", 96, 192), ("MSK", 0, 96), ("RX", 0, 96), OP.mult, OP.add)
         o = (t + 1) * 8
         cp(("RQO", o, o + 6), ("RX", 111, 192, 16))
-        for e in (1, 3, 2):
-            send(("RQO", o + 2 * (e - 1), o + 2 * e), (rank - e) % n, "q", e, t + 1)
-            lands(("RIN", o + 2 * (e - 1), o + 2 * e), "rq%d_%d" % (e, t + 1), due((rank + e) % n))
+        for e in far_first:
+            send(("RQO", o + 2 * (e - 1), o + 2 * e), "q", e, t + 1)
 
-    order = [("B", 0), ("A", 0), ("B", 1), ("A", 1), ("B", 2), ("A", 2)]
-    prep_b(0)
+    par = 0
     for t in range(RO):
-        ghosts_in(t)
-        for i, (x, h) in enumerate(order):
-            y = "B" if x == "A" else "A"
-            big = rec(big_v, x)
-            if i == 5:
-                places_p()
-            gather_s(x, 0)
-            own_t(x)
-            diff(x, 0)
-            if i == 5:
-                gather_s(x, 1)
-                diff(x, 1)
-                weave(big, rec(places, t), "ab" * 9)
-            else:
-                weave(big[:3], rec(best, y) if i else [], "ababab")
-                if i:
-                    perm(y)
-                gather_s(x, 1)
-                diff(x, 1)
-                weave(big[3:], rec(step, y) if i else rec(start_a, t), "abaabababab" if i else "aaaaaa")
-            relu(x, 0)
-            relu(x, 1)
-            sums("P" + x, "D" + x, "RD", 128, False)
-            sums("P" + x, "N" + x, "RN", 0, True)
-            if i < 5:
-                own_s(y, WIN)
-                best_s(x)
-                own_v(y, WIN)
-            if t == 0 and i == 3:
-                later_consts()
-        weave(rec(best, "B"), rec(places2), "abab")
-        best_s("A")
-        places_s()
-        weave(rec(best, "A"), rec(places3), "bbbbbbabbbabbbabbbba")
-        moves(t)
-        if t + 1 < RO:
+        last = t + 1 == RO
+        for e in (1, 2, 3):
+            lo = (e - 1) * GH
+            cp(("XT", S + lo, S + lo + GH), ("LG", t * 1152 + lo, t * 1152 + lo + GH))
+        for x in ORDER[t]:
+            start(t, x)
+        for h in range(3):
+            for x in ORDER[t]:
+                if h == 2 and x in (ORDER[t][0], "C"):
+                    places(t, "C" if x == "C" else "AB")
+                look(t, x, par)
+                par = 1 - par
+                if h < 2 or not last:
+                    step(t, x, h)
+        if last:
+            for lo, hi in [(448 * k, 448 * k + 448) for k in range(4)] + [(NULL, WX)]:
+                act(("YO", lo, hi), ("XT", lo, hi), AF.Identity, bias=UNC)
+        moves(t, "AB")
+        moves(t, "C")
+        leave(t, "C")
+        if not last:
             ghosts(t + 1)
-            perm("B")
-            perm("A")
-            weave(rec(step, "B"), rec(step, "A"), "ab" * 5)
-            weave(rec(requests, t), rec(prep_b, t + 1), "aabababaabaaaaaa")
+            requests(t)
+    for k in range(NOUT):
+        w = S // NOUT
+        dma("YS"[k % 2], "st%d" % k, T.y[:, w * k:w * k + w], T["YO"][:, w * k:w * k + w], [("YO", w * k, w * k + w)], [], LOAD)
 
-    for k, (a, b) in enumerate(part):
-        ts(("DB", a, b), ("XT", a, b), 0.0, OP.is_lt)
-        mm((ban[k], 0, 448), ("IDB", 0, 128), ("XT", a, b), True, False)
-        mm((ban[k], 0, 448), ("EMN", 0, 128), ("DB", a, b), False, True)
-        if k % 2:
-            cp(("YO", a, b), (ban[k], 0, 448))
-        else:
-            act(("YO", a, b), (ban[k], 0, 448))
-        dma("Y", "st%d" % k, T.y[:, a:b], T["YO"][:, a:b], [("YO", a, b)], [])
+    clock = {k: {} for k in queue}
+    total, acc = {}, {}
+    for i in issue_order(calls):
+        q, c1, c2, reads, writes, follows, kind, what = calls[i]
+        if kind == "lands":
+            total[what[0]] = what[1]
+            note(acc, q, [], writes, what, {})
+            continue
+        for (s, v), ck in sorted(((a[4], a[5]) for a, done in meets(acc, q, reads, writes, kind == "add") if done), key=lambda x: -x[0][1]):
+            if clock[q].get(s, 0) < v:
+                queue[q].wait_ge(T.sem[s], v)
+                clock[q][s] = v
+                for a, b in ck.items():
+                    clock[q][a] = max(clock[q].get(a, 0), b)
+        if kind == "send":
+            out, in_, rsem, to = what
+            rid, pid = topo.addr(to, core)
+            g.remote_dma(out, in_, T.sem[rsem], T.sem["ls"], pid, rid, topo.mask(core, to))
+            total["ls"] = total.get("ls", 0) + count(topo.mask(core, to))
+            continue
+        s, k = (what[0], 16) if kind == "dma" else ("s" + q, 1)
+        total[s] = total.get(s, 0) + k
+        (queue[q].dma_start(what[1], what[2]) if kind == "dma" else what(queue[q])).then_inc(T.sem[s], k)
+        note(acc, s if kind == "dma" else q, reads, writes, (s, total[s]), dict(clock[q]))
     for s in sorted(total):
         if clock["G"].get(s, 0) < total[s]:
             g.wait_ge(T.sem[s], total[s])

@@ -5,34 +5,34 @@ NULL, WX, TRASH = 2944, 2960, 2960
 MID = 1472.0
 RATIO, TOP = 1.75, 2.0 ** 98
 MAGIC = 1.5 * 2.0 ** 24
-BLOCKS = [{"A": (0, 3), "B": (3, 4), "C": (7, 3)}] + [{"A": (0, 6), "B": (6, 5), "C": (11, 5)}] * 3
-ORDER = ["ABC", "BAC", "BAC", "BAC"]
-FUSED = {48: 16, 64: 16, 80: 16, 96: 32}
-CUT = {48: 32, 64: 32, 80: 64, 96: 64}
-PIECE = (16, 16, 16)
-ONV, NOUT = 1, 2
-CYC, PCYC, DONE, WAKE, LOAD, NEAR, FAR, SMALL = 0.00083, 0.00042, 0.1, 0.1, 1.9, 4.0, 6.5, 1.0
+ROOM = 288
+BLOCKS = [{"A": (0, 5), "B": (5, 5)}] + [{"A": (0, 8), "B": (8, 8)}] * 3
+FUSED = {80: 32, 128: 40}
+CUT = {80: 64, 128: 96}
+PIECE = (16, 8, 16)
+NB1, NOUT = 896, 2
+LINE = ("RAW", "DA", "DB")
+CYC, PCYC, DONE, WAKE, LOAD, NEAR, FAR, SMALL, LISTS = 0.00083, 0.00042, 0.1, 0.1, 1.9, 4.0, 6.5, 1.0, 10.0
 OP = AluOpType
 AF = ActivationFunctionType
 SIZES = {
-    "bfloat16": "XR 1792,XT 3584,YO 3584,EIN 2960,PUL 512,MSK 512,RAW 3072,EXP 1536,ONE 768,EQ 4096,PRB 768,IDB 128,IDK 128,GM 128,"
-                "GM2 128,GGK 128,WZ 16,ZER 96,DQ 256,XD 256,VAL 512,STL 24,RW 128,LB 24,IND 256,CNT 256,QC 256,GS 4608,LG 4608,"
-                "RG 1536",
-    "float16": "ZSA 1536,ZSB 1536,ZSC 1536,DA 1536,DB 1536,DC 1536,SB 512,BSA 96,BSB 96,BSC 96,STA 128,STB 128,STC 128,EA 96,EB 96,"
-               "EC 96,RD 16,RS 256,RE 256,WY 16,PRW 2304,DL 24,DBC 256",
-    "float32": "NBF 2960,IOT 2960,REQ 2320,PUF 1024,REP 128,COL 64,GG 16,TMF 128,NN 128,WC 32,M 128,RA 136,RB 136,RC 136,"
-               "KQ 48,DN 24,KD 128,SD 64,INV 32,TV 256,TV2 256,THE 48,KL 128,LW 64,QX 512,GV 256,RX 192,RQO 32,RIN 32,RRQ 32",
-    "int32": "NBI 1792,WTI 8,WAN 40,WK 320,SND 72,SNL 72,CI 16,OL 128,KI 48,WI 128,FI 128,ZI 168,POI 64,RSN 24",
-    "uint16": "SNU 72,SLU 72,DG 16,RL 4,XL 4,OFA 16,OFB 16,OFC 16,OFX 16,ONA 96,ONB 96,ONC 96,DOF 32,POF 32,OFS 64,RQF 16",
+    "bfloat16": "XR 1792,XT 3584,YO 3584,EIN 2960,PUL 512,PUT 2960,VC 256,MSK 640,RAW 3072,EXP 2048,ONE 768,EQ 4096,PRB 1024,IDB 128,"
+                "IDK 128,GM 128,GQ 2048,GGK 128,WZ 16,ZER 64,DQ 32,XD 256,VAL 512,STL 16,RW 128,LB 16,IND 256,GS 4608,LG 4608,RG 1536",
+    "float16": "ZSA 2048,ZSB 2048,DA 2048,DB 2048,SB 1280,BSA 128,BSB 128,STA 128,STB 128,EA 128,EB 128,RD 16,RS 256,RE 128,WY 16,"
+               "PRW 2048,DL 16,QC 256,DBC 256",
+    "float32": "IOT 2960,REQ 1424,REP 128,COL 80,GG 16,TMF 128,NN 128,WC 32,M 256,RA 136,RB 136,KQ 128,DN 16,KD 128,SD 32,INV 16,"
+               "TV 256,TV2 256,THE 32,KL 128,LW 32,GV 256,RX 192,RQO 32,RIN 32,RRQ 32",
+    "int32": "NBI 2960,WTI 8,WAN 40,WK 320,SND 72,SNL 72,CI 16,OL 128,KI 128,WI 256,FI 256,ZI 112,RSN 24",
+    "uint16": "SNU 72,SLU 72,DG 8,RL 4,XL 4,OFA 16,OFB 16,OFX 16,ONA 128,ONB 128,DOF 16,OFS 32,RQF 16",
 }
 SCRATCH = {}
 for _d, _l in SIZES.items():
     for _x in _l.split(","):
         SCRATCH[_x.split()[0]] = ("sbuf", [128, int(_x.split()[1])], _d)
-BANKS = ("PA", "PB", "PC", "X0", "X1", "PT", "PM", "PM2")
+BANKS = ("PA", "PB", "X0", "X1", "X2", "PT", "PM", "PM2")
 for _x in BANKS:
     SCRATCH[_x] = ("psum", [128, 512], "float32")
-SEMAPHORES = (["sV", "sS", "sP", "sG", "ls", "rs"] + ["ld%d" % i for i in range(8)] + ["st%d" % i for i in range(4)]
+SEMAPHORES = (["sV", "sS", "sP", "sG", "ls", "rs", "go"] + ["ld%d" % i for i in range(8)] + ["st%d" % i for i in range(4)]
               + ["ga%d_%d" % (e, t) for e in (1, 2, 3) for t in range(4)] + ["rq%d_%d" % (e, t) for e in (1, 2, 3) for t in (1, 2, 3)]
               + ["sn%d" % e for e in (1, 2, 3)] + ["rg%d" % t for t in range(4)] + ["rr%d" % t for t in (1, 2, 3)])
 
@@ -112,9 +112,11 @@ def issue_order(calls):
             post[j][i] = calls[j][2] + DONE if done else 0.0
         left.append(len(p))
         note(acc, c[0], c[3], c[4], i)
-    way = [0.0] * len(calls)
+    way, line = [0.0] * len(calls), {}
     for i in reversed(range(len(calls))):
         way[i] = calls[i][1] + max([way[k] + w + (WAKE if w else 0.0) for k, w in post[i].items()] + [calls[i][2]])
+        if calls[i][4] and calls[i][4][0][0] in LINE:
+            way[i] = line[calls[i][0]] = max(way[i], calls[i][1] + line.get(calls[i][0], 0.0))
     ready, free, pool, order = [0.0] * len(calls), {}, {}, []
     for i, c in enumerate(calls):
         if not left[i]:
@@ -145,8 +147,8 @@ def rank_program(g, core, T, topo):
     queue = {"V": g.vector, "S": g.scalar, "P": g.tensor, "G": g, "Y": g.sync}
     calls = []
 
-    def last_of(kind, q):
-        return [i for i, c in enumerate(calls) if c[6] == kind and c[0] == q][-1:]
+    def last_of(kind, q, k=1):
+        return [i for i, c in enumerate(calls) if c[6] == kind and c[0] == q][-k:]
 
     def do(q, cost, fn, reads, writes):
         calls.append([q, cost, 0.0, reads, writes, [], "do", fn])
@@ -206,6 +208,9 @@ def rank_program(g, core, T, topo):
     def act(out, a, func=AF.Copy, **kw):
         do("S", cost(1, out, a), lambda s: s.activation(ap(out), ap(a), func, **{k: val(x) for k, x in kw.items()}), rd(a, *kw.values()), wr(out))
 
+    def zero(out):
+        act(out, ("ONE", 0, size(out)), AF.Identity, scale=0.0)
+
     def mm(out, l, r, start, stop):
         c = max(min(64, size(l)), size(r)) * PCYC * (4 if SCRATCH[l[0]][2] == "float32" else 1)
         calls.append(["P", c, 0.0, rd(l, r), wr(out), [], "do" if start else "add", lambda p: p.matmul(ap(out), ap(l), ap(r), start, stop)])
@@ -225,33 +230,34 @@ def rank_program(g, core, T, topo):
         d, src = (rank + sign * e) % n, (rank - sign * e) % n
         k = rel[(rank, d)]
         to, out, rsem = (T.cores[d], at, sem) if k is None else (k, at2, sem2)
-        calls.append(["G", 0.3, 0.0, [in_], [], last_of("send", "G"), "send", (T[out[0]][:, out[1]:out[1] + at[2]], ap(in_), rsem, to)])
+        calls.append(["G", 0.3, 0.0, [in_], [], last_of("send", "G") or last_of("do", "G", 9), "send",
+                      (T[out[0]][:, out[1]:out[1] + at[2]], ap(in_), rsem, to)])
         k = rel[(src, rank)]
         due = count(topo.mask(T.cores[src] if k is None else k, core))
-        way = (NEAR if k is None else FAR) - (0.0 if kind == "g" else SMALL if k is None else 2 * SMALL)
+        way = {"g": NEAR if k is None else FAR, "q": NEAR - SMALL if k is None else FAR - 2 * SMALL, "s": LISTS}[kind]
         calls.append(["in" + sem, 0.0, way, [], [(at[0], at[1], at[1] + at[2])], [len(calls) - 1], "lands", (sem, due)])
 
-    def col(i, rows=128):
-        return ("COL", i, i + 1, 1, rows) if rows < 128 else ("COL", i, i + 1)
+    def col(i):
+        return ("COL", i, i + 1)
 
     def ci(i):
         return ("CI", i, i + 1)
 
-    (QF, GF, N15, I15, I0, CEN, UNC, EPS, THE0, HLF, QR, TH, SB0, SB3, WTF, PF, Q8, QW, EMP) = [col(i) for i in range(19)]
+    (QF, GF, N15, I15, I0, CEN, UNC, EPS, M15, HLF, QR, TH, SB0, SB3, WTF, PF, Q8, QW, EMP) = [col(i) for i in range(19)]
     NVB = [col(20 + t) for t in range(RO)]
-    THR = {c0: 24 + k for k, c0 in enumerate((0, 3, 7, 6, 11))}
-    DGA = {nc: 2 * k for k, nc in enumerate((3, 4, 5, 6, 7, 10, 11, 16))}
-    WIN, OWN, NBW = ("XT", 0, WX), ("XT", 0, S), ("NBF", 0, WX)
+    THR = {c0: col(24 + k) for k, c0 in enumerate(sorted({c0 for b in BLOCKS for c0, nc in b.values()}))}
+    widths = {w for b in BLOCKS for w in (b["A"][1], b["B"][1], sum(b["B"]))}
+    DGA = {nc: 2 * k for k, nc in enumerate(sorted(widths))}
+    WIN, OWN, NBW = ("XT", 0, WX), ("XT", 0, S), ("NBI", 0, WX)
     GM, GG = ("GM", 0, 128), ("GG", 0, 8)
     far = [e for e in (1, 2, 3) if rel[(rank, (rank + e) % n)] is not None]
     far_first = far + [e for e in (1, 2, 3) if e not in far]
+    mark = []
 
     dma("Y", "ld0", T["XR"][:, :], T.x0[:, :], [], [("XR", 0, S)], LOAD + 1.5)
     dma("S", "ld1", T["SND"][:, :], T.snd[:, :], [], [("SND", 0, 72)], LOAD)
     dma("Y", "ld3", T["WAN"][:, :], T.wants[:, :], [], [("WAN", 0, 40)], LOAD + 1.7)
-    dma("Y", "ld2", T["NBI"][:, :], T.nb[:, :], [], [("NBI", 0, S)], LOAD + 4.4)
-    dma("Y", "ld4", T["WTI"][:, 0:1], T.wt[:, :], [], [("WTI", 0, 1)], LOAD + 4.6)
-    dma("Y", "ld5", T["PUL"][:, :], T.pull[:, :], [], [("PUL", 0, 512)], LOAD + 5.0)
+    dma("Y", "ld2", T["NBI"][:, 0:NB1], T.nb[:, 0:NB1], [], [("NBI", 0, NB1)], LOAD + 1.7 + 2.7 * NB1 / S)
 
     iota(ci(0), [[1, 1]], 0, 1)
     iota(("TMF", 0, 128), [[1, 8], [0, 16]])
@@ -265,14 +271,14 @@ def rank_program(g, core, T, topo):
     cp(QF, ci(1))
     cp(GF, ci(2))
     cp(PF, ci(0))
-    fill(("ZER", 0, 96), 0.0)
+    fill(("ZER", 0, 64), 0.0)
     ts(N15, QF, 15.0, OP.is_lt)
     ts(I15, QF, 15.0, OP.is_equal)
     ts(I0, QF, 0.0, OP.is_equal)
     ts(CEN, N15, -127.5, OP.mult)
     ts(UNC, N15, 127.5, OP.mult)
     ts(EPS, N15, -0.0625, OP.mult)
-    ts(THE0, N15, 1000.5, OP.mult, -0.5, OP.add)
+    ts(M15, I15, -1.0, OP.mult)
     ts(HLF, N15, 0.5, OP.mult)
     ts(SB0, N15, 1.0625, OP.mult, -1.0, OP.add)
     ts(SB3, N15, 128.5625, OP.mult, -1.0, OP.add)
@@ -281,31 +287,30 @@ def rank_program(g, core, T, topo):
     ts(GM, ("TMF", 0, 128), GF, OP.is_equal)
     ts(("GGK", 0, 128), ("GGK", 0, 128), GF, OP.is_equal)
     cp(GG, ("GGK", 0, 8))
-    for x in "ABC":
-        act(("ZS" + x, 0, 512), ("ONE", 0, 512), AF.Identity, scale=0.0)
-        act(("R" + x, 0, 136), ("ONE", 0, 136), AF.Identity, scale=0.0)
-    fill(("STL", 0, 24), 0.0)
-    fill(("YO", S, NULL), 0.0)
+    for x in "AB":
+        zero(("ZS" + x, 0, 640))
+        zero(("R" + x, 0, 136))
+    fill(("STL", 0, 16), 0.0)
     for e in far_first:
         send(("SND", (e - 1) * 24, e * 24), "s", e, 0)
+    iota(("NBI", S, S + 448), [[1, 448]], S)
+    calls[-1][5] = last_of("send", "G")
     cp(("SNU", 0, 72), ("SND", 0, 72))
     ts(("RD", 0, 8), GG, N15, OP.mult, 16384.0, OP.mult)
     ts(("RD", 8, 16), GG, I15, OP.mult, 4.25, OP.mult)
     ts(("RS", 0, 128), GM, N15, OP.mult, -16384.0, OP.mult)
     ts(("RS", 128, 256), GM, I15, OP.mult, -4.25, OP.mult)
-    ts(("RE", 0, 128), GM, I0, OP.mult, -15360.0, OP.mult)
     ts(("M", 0, 128), ("NN", 0, 128), -0.25, OP.mult, MID / 16384.0 - 0.25, OP.add)
     ts(EMP, I15, -1024.0, OP.mult)
     ts(("TV", 0, 128), ("M", 0, 128), I0, OP.mult, EMP, OP.add)
-    tt(("RE", 128, 256), ("TV", 0, 128), GM, OP.mult)
+    tt(("RE", 0, 128), ("TV", 0, 128), GM, OP.mult)
     ts(("IDK", 0, 128), ("IDB", 0, 128), 1.0 / 16384.0, OP.mult)
     ts(("REP", 0, 128), ("NN", 0, 128), QF, OP.is_equal, 16384.0, OP.mult)
-    mm(("PM", 0, 96, 1, 96), ("IDB", 0, 96), ("ZER", 0, 96), True, True)
+    mm(("PM", 0, 64), ("IDB", 0, 128), ("ZER", 0, 64), True, True)
     ts(("MSK", 0, 128), ("NN", 0, 128), 0.5, OP.is_gt)
-    cp(("MSK", 128, 256), ("MSK", 0, 128))
-    cp(("MSK", 256, 512), ("MSK", 0, 256))
-    ts(("DQ", 0, 128), ("NN", 0, 128), QF, OP.is_equal)
-    cp(("DQ", 128, 256), ("DQ", 0, 128))
+    for lo, hi in ((128, 256), (256, 512), (512, 640)):
+        cp(("MSK", lo, hi), ("MSK", 0, hi - lo))
+    ts(("DQ", 0, 32), ("NN", 0, 32), QF, OP.is_equal)
 
     def ghosts(t):
         at = t * 1152
@@ -317,34 +322,41 @@ def rank_program(g, core, T, topo):
             else:
                 act(("GS", a, b), ("I", ("XR", 0, S), ("SNU", a // 16, b // 16)), AF.Identity, bias=CEN)
                 ts(("GS", b, c), ("I", ("XR", 0, S), ("SNU", b // 16, c // 16)), CEN, OP.add)
+            if e in far:
+                mark[:] = last_of("do", "V")
             send(("GS", at + a, at + c), "g", e, t)
 
     ghosts(0)
-    for k in (0, 1):
-        iota(("NBF", S + 584 * k, S + 584 * k + 584), [[1, 584]], S + 584 * k)
-    for k in range(3):
+    calls.append(["G", 0.0, 0.0, [], [("go", 0, 1)], last_of("send", "G"), "inc", None])
+    dma("Y", "ld6", T["NBI"][:, NB1:S], T.nb[:, NB1:S], [("go", 0, 1)], [("NBI", NB1, S)], LOAD + 1.5 + 2.7 * (S - NB1) / S)
+    dma("Y", "ld4", T["WTI"][:, 0:1], T.wt[:, :], [], [("WTI", 0, 1)], LOAD + 3.0)
+    dma("Y", "ld5", T["PUL"][:, :], T.pull[:, :], [], [("PUL", 0, 512)], LOAD + 3.5)
+    late = len(calls)
+    iota(("NBI", S + 448, WX), [[1, WX - S - 448]], S + 448)
+    for k in range(4):
         pick(("EXP", 512 * k, 512 * k + 512), ("ONE", 0, 512), [[-1, 32], [0, 16]], -32 * k)
     for k in (0, 1):
-        pick(("PRB", 384 * k, 384 * k + 384), ("ONE", 0, 384), [[-16, 3], [0, 8], [-1, 16]], -48 * k)
+        pick(("PRB", 512 * k, 512 * k + 512), ("ONE", 0, 512), [[-16, 4], [0, 8], [-1, 16]], -64 * k)
     for k in range(4):
         iota(("IOT", 448 * k, 448 * k + 448), [[1, 448]], 448 * k)
     iota(("IOT", NULL, WX), [[1, WX - NULL]], NULL)
     for k in range(8):
         iota(("EQ", 512 * k, 512 * k + 512), [[0, 512]])
+    for c in calls[late:]:
+        c[5] = last_of("send", "G")
     for k in range(4):
         ts(("XT", 448 * k, 448 * k + 448), ("XR", 448 * k, 448 * k + 448), CEN, OP.add)
     for k in range(8):
-        cp(("NBF", 224 * k, 224 * k + 224), ("NBI", 224 * k, 224 * k + 224))
         cp(("WK", k, 320, 8), ("WAN", 0, 40))
     for k, (nc, at) in enumerate(DGA.items()):
-        ts(col(44 + k), QF, float(nc - 1), OP.min, 8.0, OP.mult)
+        ts(col(64 + k), QF, float(nc - 1), OP.min, 8.0, OP.mult)
         for j in (0, 1):
-            ts(("DG", at + j, at + j + 1), col(44 + k), GF, OP.add)
+            ts(("DG", at + j, at + j + 1), col(64 + k), GF, OP.add)
     ts(Q8, QF, 8.0, OP.is_ge)
     ts(col(56), Q8, -8.0, OP.mult, QF, OP.add)
     ts(col(57), col(56), 16.0, OP.mult, 15.0 - 128.0, OP.add)
     tt(col(58), GF, Q8, OP.subtract)
-    for k in range(3):
+    for k in range(4):
         ts(("RL", k, k + 1), Q8, 2.0 * k, OP.add)
         ts(col(59 + k), col(58), 2.0 * k, OP.is_equal, col(57), OP.mult)
         ts(("XL", k, k + 1), col(59 + k), 128.0, OP.add)
@@ -366,16 +378,19 @@ def rank_program(g, core, T, topo):
     tt(("THE", 16, 32), ("THE", 0, 16), ("WC", 0, 16), OP.mult)
     do("V", 64 * CYC, lambda v: v.tensor_reduce(ap(TH), ap(("THE", 16, 32)), AxisListType.X, OP.add), [("THE", 16, 32)], [TH])
     for c0, k in THR.items():
-        ts(col(k), TH, RATIO ** (-8 * c0), OP.mult, 2.54 * RATIO ** (-8 * c0), OP.mult)
-    for b in range(3):
-        ts(col(32 + b), PF, 2.0, OP.mult, TRASH + 192.0 * b, OP.add)
-        for k in (0, 1):
-            act(("PRW", 768 * b + 384 * k, 768 * b + 384 * k + 384), ("PRB", 384 * k, 384 * k + 384), AF.Identity, scale=col(32 + b))
-    ts(QW, QF, 1.0, OP.add, 512.0, OP.mult)
-    ts(("GM2", 0, 128), GM, QW, OP.mult)
-    for k in (0, 256):
-        act(("PUF", k, k + 256), ("PUL", k, k + 256), AF.Identity, bias=127.0)
-        act(("PUF", 512 + k, 768 + k), ("PUL", k, k + 256), AF.Identity, bias=-0.5)
+        ts(k, TH, RATIO ** (-8 * c0), OP.mult, -2.54 * RATIO ** (-8 * c0), OP.mult)
+    for b in range(2):
+        ts(col(32 + b), PF, 2.0, OP.mult, TRASH + 256.0 * b, OP.add)
+        for k in range(0, 1024, 256):
+            act(("PRW", 1024 * b + k, 1024 * b + k + 256), ("PRB", k, k + 256), AF.Identity, scale=col(32 + b))
+    ts(QW, QF, 1.0, OP.add, float(ROOM), OP.mult)
+    for k in range(4):
+        zero(("GQ", 512 * k, 512 * k + 512))
+    for q in range(16):
+        cp(("GQ", 129 * q, 128 * q + 128, 16), GG)
+    for k in range(0, WX, 512):
+        w = min(512, WX - k)
+        ts(("PUT", k, k + w), ("PUL", 0, w), -1.0, OP.add)
     for e in (1, 2, 3, 4):
         ts(col(35 + e), QF, float(e - 1), OP.is_equal)
         for lo, hi in [(S + (e - 1) * GH, S + e * GH)] if e < 4 else [(448 * k, 448 * k + 448) for k in range(4)] + [(NULL, WX)]:
@@ -388,44 +403,45 @@ def rank_program(g, core, T, topo):
 
     def geo(t, x):
         c0, nc = BLOCKS[t][x]
-        return c0, nc, 16 * nc, FUSED[16 * nc]
+        return "AB".index(x), c0, nc, 16 * nc
 
     def own(t, x, h, win):
-        c0, nc, L, a = geo(t, x)
+        b, c0, nc, L = geo(t, x)
         ps, of, zs = "P" + x, ("OF" + x, 0, nc), ("ZS" + x, 0, 16 * L, 16)
-        act(("BS" + x, 0, L), ("I", NBW, of), AF.Identity, bias=-MID)
         act(zs, ("I", win, of), AF.Identity, bias=EPS)
-        if ONV:
-            cp(("ON" + x, 0, L), ("I", NBW, of))
-        else:
-            ts(("ON" + x, 0, L), ("BS" + x, 0, L), MID, OP.add)
+        cp(("ON" + x, 0, L), ("I", NBW, of))
+        act(("BS" + x, 0, L), ("ON" + x, 0, L), AF.Identity, bias=-MID)
         mm((ps, 256, 384, 1, L), zs, ("IDB", 0, 128), True, True)
         act(("ST" + x, 0, 128, 1, L), (ps, 256, 384, 1, L))
         if h == 0:
-            ts(("E" + x, 0, L), zs, THE0, OP.is_lt)
+            act(("E" + x, 0, L), zs, AF.Relu, scale=M15, bias=N15)
         mm((ps, 0, 256, 1, L), zs, ("RS", 0, 256), True, False)
-        mm((ps, 0, 256, 1, L), ("E" + x, 0, L), ("RE", 0, 256), False, False)
+        mm((ps, 128, 256, 1, L), ("E" + x, 0, L), ("RE", 0, 128), False, False)
         mm((ps, 128, 256, 1, L), ("BS" + x, 0, L), ("IDK", 0, 128), False, False)
 
     def start(t, x):
-        c0, nc, L, a = geo(t, x)
-        if t and x == "A":
-            cp(("OFA", 0, 6), ("RIN", 8 * t, 8 * t + 6))
-            cp(("OL", 0, 48), ("I", ("RIN", 8 * t, 8 * t + 6), ("RL", 0, 3)))
-        else:
-            w = 10 * t + c0 - (6 if t else 0)
-            cp(("OF" + x, 0, nc), ("WAN", w, w + nc))
-        own(t, x, 0, OWN if not (t and x == "A") else WIN)
+        b, c0, nc, L = geo(t, x)
+        k = 6 if t and x == "A" else 0
+        w = 10 * t + c0 + k - (6 if t else 0)
+        if k:
+            cp(("OFA", 0, k), ("RIN", 8 * t, 8 * t + k))
+            calls[-1][5] = mark[:]
+            cp(("OL", 0, 8 * k), ("I", ("RIN", 8 * t, 8 * t + k), ("RL", 0, k // 2)))
+            calls[-1][5] = mark[:]
+            cp(("OL", 8 * k, 8 * nc), ("WK", 8 * w, 8 * (w + nc - k)))
+        cp(("OF" + x, k, nc), ("WAN", w, w + nc - k))
+        own(t, x, 0, WIN if k else OWN)
 
     def look(t, x, par):
-        c0, nc, L, a = geo(t, x)
-        ps = "P" + x
-        scan(("SB", 0, 16 * a), ("MSK", 0, 16 * a), ("ZS" + x, 0, 16 * a), OP.mult, OP.add)
+        b, c0, nc, L = geo(t, x)
+        ps, a, sb = "P" + x, FUSED[L], 640 * b
+        wi, fi, mi = [(k, 128 * b, 128 * b + 128, 1, L) for k in ("WI", "FI", "M")]
+        scan(("SB", sb, sb + 16 * a), ("MSK", 0, 16 * a), ("ZS" + x, 0, 16 * a), OP.mult, OP.add)
         for l in range(0, a, PIECE[0]):
             m = min(l + PIECE[0], a)
-            tt(("D" + x, 16 * l, 16 * m), ("I", WIN, ("ON" + x, l, m)), ("SB", 16 * l, 16 * m), OP.max)
+            tt(("D" + x, 16 * l, 16 * m), ("I", WIN, ("ON" + x, l, m)), ("SB", sb + 16 * l, sb + 16 * m), OP.max)
         for k, l0 in enumerate(range(a, L, 32)):
-            l1, at, bank = min(l0 + 32, L), 1536 * par + 512 * k, "X%d" % (k % 2)
+            l1, at, bank = min(l0 + 32, L), 1536 * par + 512 * k, "X%d" % k
             for l in range(0, l1 - l0, PIECE[2]):
                 m = min(l + PIECE[2], l1 - l0)
                 act(("RAW", at + 16 * l, at + 16 * m), ("I", WIN, ("ON" + x, l0 + l, l0 + m)))
@@ -436,123 +452,111 @@ def rank_program(g, core, T, topo):
         for l0, l1 in ((0, CUT[L]), (CUT[L], L)):
             for i in range(16):
                 mm((ps, i, 256, 16, l1, l0), ("D" + x, 16 * l0 + i, 16 * l1, 16), ("RD", 0, 16), False, i == 15)
-        ts(("WI", 0, 128, 1, L), (ps, 0, 128, 1, L), 0.0, OP.max)
-        ts(("FI", 0, 128, 1, L), ("WI", 0, 128, 1, L), 15 * 1024, OP.bitwise_and)
-        tt(("M", 0, 128, 1, L), ("FI", 0, 128, 1, L), (ps, 128, 256, 1, L), OP.min)
-        scan(("R" + x, 0, 128, 1, L), ("MSK", 0, 128, 1, L), ("M", 0, 128, 1, L), OP.mult, OP.max)
+        ts(wi, (ps, 0, 128, 1, L), -15360.0, OP.add, 0.0, OP.max)
+        ts(fi, wi, 15 * 1024, OP.bitwise_and)
+        tt(mi, fi, (ps, 128, 256, 1, L), OP.min)
+        scan(("R" + x, 0, 128, 1, L), ("MSK", 0, 128, 1, L), mi, OP.mult, OP.max)
 
     def step(t, x, h):
-        c0, nc, L, a = geo(t, x)
-        k = (nc + 1) // 2
-        act(("KQ", 0, 16 * k), ("I", ("R" + x, 0, 136), ("XL", 0, k)))
-        mm(("PT", 0, 8 * nc), ("REP", 0, 128), ("KQ", 0, 8 * nc), True, True)
+        b, c0, nc, L = geo(t, x)
+        k, o = (nc + 1) // 2, 64 * b
+        act(("KQ", o, o + 16 * k), ("I", ("R" + x, 0, 136), ("XL", 0, k)))
+        mm(("PT", 0, 8 * nc), ("REP", 0, 128), ("KQ", o, o + 8 * nc), True, True)
         ol = ("OL", 8 * c0, 8 * (c0 + nc))
         w = 8 * (10 * t + c0 - (6 if t else 0))
-        tt(("KI", 0, 8 * nc), ("PT", 0, 8 * nc), ol if h or (t and x == "A") else ("WK", w, w + 8 * nc), OP.max)
-        ts(ol, ("KI", 0, 8 * nc), 4095, OP.bitwise_and)
+        tt(("KI", o, o + 8 * nc), ("PT", 0, 8 * nc), ol if h or (t and x == "A") else ("WK", w, w + 8 * nc), OP.max)
+        ts(ol, ("KI", o, o + 8 * nc), 4095, OP.bitwise_and)
         if h < 2:
             cp(("OF" + x, 0, 16), ("I", ol, ("DG", DGA[nc], DGA[nc] + 1)))
             own(t, x, h + 1, WIN)
 
-    def cols(t):
-        return sum(nc for c0, nc in BLOCKS[t].values())
+    def each(t):
+        return [(x,) + geo(t, x) for x in "AB"]
 
-    def part(t, only):
-        mine = [(b, x) + geo(t, x) for b, x in enumerate("ABC") if x in only]
-        lo, hi = mine[0][2], mine[-1][2] + mine[-1][3]
-        return mine, 8 * mine[0][0], 8 * mine[-1][0] + 8, lo, hi, ("DG", DGA[hi - lo], DGA[hi - lo] + 1), 0 if lo == 0 else 32
-
-    def turn(mine, mat, stride, src):
-        for b, x, c0, nc, L, a in mine:
+    def turn(t, mat, stride, src):
+        for x, b, c0, nc, L in each(t):
             for c in range(nc):
                 at = stride * b + 128 * c
-                mm(("PM2", 8 * (c0 + c), 8 * (c0 + c) + 8), (mat, at, at + 128, 1, 96), (src, 8 * b, 8 * b + 8, 1, 96), True, True)
+                mm(("PM2", 8 * (c0 + c), 8 * (c0 + c) + 8), (mat, at, at + 128), (src, 8 * b, 8 * b + 8), True, True)
 
-    def places(t, only):
-        mine, b0, b1, lo, hi, dg, o = part(t, only)
-        last, j0, j1 = int(t + 1 == RO), 16 * lo, 16 * hi
-        for b, x, c0, nc, L, a in mine:
+    def places(t):
+        nt, last = sum(BLOCKS[t]["B"]), t + 1 == RO
+        NL, dg, dof = 16 * nt, ("DG", DGA[nt], DGA[nt] + 1), ("DOF", 0, nt)
+        for x, b, c0, nc, L in each(t):
             zs = ("ZS" + x, 0, 16 * L, 16)
             mm(("PM", 8 * b, 8 * b + 8, 1, L), zs, ("WZ", 0, 8), True, False)
             mm(("PM", 8 * b, 8 * b + 8, 1, L), ("E" + x, 0, L), ("WY", 0, 8), False, False)
             mm(("PM", 8 * b, 8 * b + 8, 1, L), ("E" + x, 0, L), ("WY", 8, 16), False, True)
-            mm(("PM", 24 + 8 * b, 32 + 8 * b, 1, L), zs, ("WZ", 8, 16), True, True)
+            mm(("PM", 16 + 8 * b, 24 + 8 * b, 1, L), zs, ("WZ", 8, 16), True, True)
             act(("VAL", 256 + 16 * c0, 256 + 16 * c0 + L), zs, AF.Identity, scale=N15, bias=SB3 if last else SB0)
-        z = [("ZI", 24 * i + b0, 24 * i + b1, 1, 96) for i in range(7)]
-        sd, ss, inv, dof = ("SD", o, o + 16), ("SD", o + 16, o + 32), ("INV", o // 2, o // 2 + 16), ("DOF", o // 2, o // 2 + hi - lo)
-        cp(ss, ("I", ("OL", 8 * lo, 8 * hi), dg))
-        cp(z[0], ("PM", b0, b1, 1, 96))
+            if last:
+                act(("VC", 16 * c0, 16 * c0 + L), zs, AF.Identity, scale=N15, bias=SB0)
+        z = [("ZI", 16 * i, 16 * i + 16) for i in range(7)]
+        cp(("SD", 16, 32), ("I", ("OL", 0, 8 * nt), dg))
+        cp(z[0], ("PM", 0, 16))
         ts(z[1], z[0], 2047, OP.bitwise_and)
-        ts(("DN", b0, b1, 1, 96), ("PM", 24 + b0, 24 + b1, 1, 96), 0.0, OP.is_lt, float(NULL), OP.mult)
+        act(("DN", 0, 16), ("PM", 16, 32), AF.Relu, scale=-float(NULL))
         tt(z[2], z[1], z[1], OP.mult)
         if t:
             ts(z[3], z[2], float(97 * t * 32), OP.add)
         ts(z[4], z[3 if t else 2], 5, OP.logical_shift_right, 2047, OP.bitwise_and)
         ts(z[5], z[4], float(S), OP.is_ge, -float(S), OP.mult)
         tt(z[6], z[4], z[5], OP.add)
-        tt(("DL", b0, b1, 1, 96), z[6], ("DN", b0, b1, 1, 96), OP.max)
-        turn(mine, "PRB", 0, "DL")
-        act(("KD", 8 * lo, 8 * hi), ("PM2", 8 * lo, 8 * hi))
-        ts(inv, ss, float(S), OP.is_ge, float(NULL), OP.mult)
-        tt(sd, ("I", ("KD", 8 * lo, 8 * hi), dg), inv, OP.max)
-        cp(("DOF", o // 2, o // 2 + 16), sd)
-        act(("DBC", j0, j1), ("I", ("IOT", 0, WX), dof))
-        for c in range(lo, hi):
-            ts(("EQ", c * 272, c * 256 + j1), ("DBC", 16 * c, j1), ("SD", o + c - lo, o + c - lo + 1), OP.is_equal, ("WC", c, c + 1), OP.mult)
-        cp(("POI", o, o + 16), sd)
-        ts(("POI", o + 16, o + 32), ("POI", o, o + 16), 511, OP.bitwise_and)
-        cp(("POF", o // 2, o // 2 + 16), ("POI", o + 16, o + 32))
-        tt(("TV", j0, j1), ("I", ("PUF", 512 * last, 512 * last + 512), ("POF", o // 2, o // 2 + hi - lo)), ("VAL", 256 + j0, 256 + j1), OP.add)
-        ts(("TV2", j0, j1), ("TV", j0, j1), MAGIC, OP.add, -MAGIC, OP.add)
-        act(("VAL", j0, j1), ("TV2", j0, j1), AF.Identity, scale=HLF, bias=NVB[t])
+        tt(("DL", 0, 16), z[6], ("DN", 0, 16), OP.max)
+        turn(t, "PRB", 0, "DL")
+        act(("KD", 0, 8 * nt), ("PM2", 0, 8 * nt))
+        ts(("INV", 0, 16), ("SD", 16, 32), float(S), OP.is_ge, float(NULL), OP.mult)
+        tt(("SD", 0, 16), ("I", ("KD", 0, 8 * nt), dg), ("INV", 0, 16), OP.max)
+        cp(("DOF", 0, 16), ("SD", 0, 16))
+        act(("DBC", 0, NL), ("I", ("IOT", 0, WX), dof))
+        for c in range(nt):
+            ts(("EQ", c * 272, c * 256 + NL), ("DBC", 16 * c, NL), ("SD", c, c + 1), OP.is_equal, ("WC", c, c + 1), OP.mult)
+        act(("XD", 0, NL), ("I", WIN, dof))
+        for x, b, c0, nc, L in each(t):
+            mm(("PM", 32 + 8 * b, 40 + 8 * b, 1, L), ("XD", 16 * c0, 16 * c0 + L), ("WZ", 8, 16), True, True)
+        for x, b, c0, nc, L in each(t):
+            act(("THE", 8 * b, 8 * b + 8), ("PM", 32 + 8 * b, 40 + 8 * b), AF.Relu, scale=THR[c0])
+        tt(("TV", 0, NL), ("I", ("PUT", 0, WX), dof), ("VC", 0, NL) if last else ("VAL", 256, 256 + NL), OP.add)
+        ts(("TV2", 0, NL), ("TV", 0, NL), MAGIC + 128.0, OP.add, -MAGIC, OP.add)
+        act(("VAL", 0, NL), ("TV2", 0, NL), AF.Identity, scale=HLF, bias=NVB[t])
 
-    def moves(t, only):
-        mine, b0, b1, lo, hi, dg, o = part(t, only)
-        to = "XT" if t + 1 < RO else "YO"
-        act(("XD", 16 * lo, 16 * hi), ("I", (to, 0, WX), ("DOF", o // 2, o // 2 + hi - lo)))
-        if lo:
-            leave(t, "AB")
-        for b, x, c0, nc, L, a in mine:
-            mm(("PM", 48 + 8 * b, 56 + 8 * b, 1, L), ("XD", 16 * c0, 16 * c0 + L), ("WZ", 8, 16), True, True)
-        for b, x, c0, nc, L, a in mine:
-            ts(("THE", 8 * b, 8 * b + 8, 1, 96), ("PM", 48 + 8 * b, 56 + 8 * b, 1, 96), 0.0, OP.is_lt, col(THR[c0], 96), OP.mult)
-            ts(("STL", 8 * b, 8 * b + 8, 1, L), ("R" + x, 15, 128, 16, L), 0.0, OP.is_equal)
-        turn(mine, "PRB", 0, "STL")
-        tt(("RW", 8 * lo, 8 * hi), ("PM2", 8 * lo, 8 * hi), ("GGK", 8 * lo, 8 * hi), OP.mult)
-        tt(("THE", 24 + b0, 24 + b1, 1, 96), ("THE", b0, b1, 1, 96), ("STL", b0, b1, 1, 96), OP.mult)
-        for b, x, c0, nc, L, a in mine:
-            for c in range(lo, c0 + nc):
+    def moves(t):
+        nt = sum(BLOCKS[t]["B"])
+        to = ("XT" if t + 1 < RO else "YO", 0, 3584)
+        act(("STL", 8, 16, 1, geo(t, "B")[3]), ("RB", 15, 128, 16, geo(t, "B")[3]), AF.Relu, scale=-8.0, bias=1.0)
+        ts(("STL", 0, 8, 1, geo(t, "A")[3]), ("RA", 15, 128, 16, geo(t, "A")[3]), 0.0, OP.is_equal)
+        turn(t, "PRB", 0, "STL")
+        tt(("RW", 0, 8 * nt), ("PM2", 0, 8 * nt), ("GGK", 0, 8 * nt), OP.mult)
+        tt(("THE", 16, 32), ("THE", 0, 16), ("STL", 0, 16), OP.mult)
+        for x, b, c0, nc, L in each(t):
+            for c in range(c0 + nc):
                 at = c * 256 + 16 * c0
-                mm(("PM", 72 + 8 * b, 80 + 8 * b, 1, L), ("EQ", at, at + L), ("RW", 8 * c, 8 * c + 8), c == lo, c == c0 + nc - 1)
-        tt(("LB", b0, b1, 1, 96), ("PM", 72 + b0, 72 + b1, 1, 96), ("THE", 24 + b0, 24 + b1, 1, 96), OP.is_ge)
-        turn(mine, "PRW", 768, "LB")
-        act(("KL", 8 * lo, 8 * hi), ("PM2", 8 * lo, 8 * hi))
-        tt(("LW", o, o + 32), ("I", ("KL", 8 * lo, 8 * hi), (dg[0], dg[1], dg[1] + 2)), ("SD", o, o + 32), OP.max)
-        cp(("OFS", o, o + 32), ("LW", o, o + 32))
-        cp(("I", (to, 0, 3584), ("OFS", o, o + hi - lo)), ("VAL", 16 * lo, 16 * hi))
-
-    def leave(t, only):
-        mine, b0, b1, lo, hi, dg, o = part(t, only)
-        cp(("I", ("XT" if t + 1 < RO else "YO", 0, 3584), ("OFS", o + 16, o + 16 + hi - lo)), ("VAL", 256 + 16 * lo, 256 + 16 * hi))
+                mm(("PM", 48 + 8 * b, 56 + 8 * b, 1, L), ("EQ", at, at + L), ("RW", 8 * c, 8 * c + 8), c == 0, c == c0 + nc - 1)
+        tt(("LB", 0, 16), ("PM", 48, 64), ("THE", 16, 32), OP.is_ge)
+        turn(t, "PRW", 1024, "LB")
+        act(("KL", 0, 8 * nt), ("PM2", 0, 8 * nt))
+        tt(("LW", 0, 32), ("I", ("KL", 0, 8 * nt), ("DG", DGA[nt], DGA[nt] + 2)), ("SD", 0, 32), OP.max)
+        cp(("OFS", 0, 32), ("LW", 0, 32))
+        for k in (0, 16):
+            cp(("I", to, ("OFS", k, k + nt)), ("VAL", 16 * k, 16 * (k + nt)))
 
     def requests(t):
-        nt = cols(t)
+        nt = sum(BLOCKS[t]["B"])
         NL, of = 16 * nt, ("OFX", 0, nt)
         cp(("OFX", 0, 16), ("I", ("OL", 0, 8 * nt), ("DG", DGA[nt], DGA[nt] + 1)))
         act(("GV", 0, NL), ("I", ("IOT", 0, WX), of))
         for e in (1, 2, 3):
-            act(("REQ", 512 * e + 1, 512 * e + 33), ("NN", 0, CAP), AF.Identity, scale=0.0, bias=float(NULL))
+            act(("REQ", ROOM * e + 1, ROOM * e + 33), ("NN", 0, CAP), AF.Identity, scale=0.0, bias=float(NULL))
         act(("IND", 0, NL), ("I", ("EIN", 0, WX), of))
-        scan(("CNT", 0, NL), ("ONE", 0, NL), ("IND", 0, NL), OP.mult, OP.add)
-        tt(("QC", 0, NL), ("IND", 0, NL), ("CNT", 0, NL), OP.mult)
-        mm(("PT", 128, 128 + NL), ("GM2", 0, 128), ("IND", 0, NL), True, False)
-        mm(("PT", 128, 128 + NL), GM, ("QC", 0, NL), False, True)
-        tt(("QX", 0, NL), ("PT", 128, 128 + NL), ("DQ", 0, NL), OP.mult)
-        scan(("QX", 256, 256 + NL), ("MSK", 0, NL), ("QX", 0, NL), OP.mult, OP.add)
-        cp(("RQF", 0, nt), ("QX", 271, 256 + NL, 16))
-        cp(("I", ("REQ", 0, 2320), ("RQF", 0, nt)), ("GV", 0, NL))
+        scan(("PT", 128, 128 + NL), ("ONE", 0, NL), ("IND", 0, NL), OP.mult, OP.add, QW)
+        tt(("QC", 0, NL), ("IND", 0, NL), ("PT", 128, 128 + NL), OP.mult)
+        for q in range(16):
+            mm(("PM2", 256, 256 + nt), ("GQ", 128 * q, 128 * q + 128), ("QC", q, NL, 16), q == 0, q == 15)
+        cp(("RQF", 0, nt), ("PM2", 256, 256 + nt))
+        cp(("I", ("REQ", 0, 1424), ("RQF", 0, nt)), ("GV", 0, NL))
+        calls[-1][5] = mark[:]
         for e in (1, 2, 3):
-            tt(("RX", 32 * e - 32, 32 * e), ("REQ", 512 * e + 1, 512 * e + 33), ("DQ", 0, CAP), OP.mult)
+            tt(("RX", 32 * e - 32, 32 * e), ("REQ", ROOM * e + 1, ROOM * e + 33), ("DQ", 0, CAP), OP.mult)
         scan(("RX", 96, 192), ("MSK", 0, 96), ("RX", 0, 96), OP.mult, OP.add)
         o = (t + 1) * 8
         cp(("RQO", o, o + 6), ("RX", 111, 192, 16))
@@ -565,22 +569,21 @@ def rank_program(g, core, T, topo):
         for e in (1, 2, 3):
             lo = (e - 1) * GH
             cp(("XT", S + lo, S + lo + GH), ("LG", t * 1152 + lo, t * 1152 + lo + GH))
-        for x in ORDER[t]:
+        mark[:] = last_of("do", "V", 3)
+        for x in "BA":
             start(t, x)
         for h in range(3):
-            for x in ORDER[t]:
-                if h == 2 and x in (ORDER[t][0], "C"):
-                    places(t, "C" if x == "C" else "AB")
+            if h == 2:
+                places(t)
+            for x in "BA":
                 look(t, x, par)
                 par = 1 - par
                 if h < 2 or not last:
                     step(t, x, h)
         if last:
-            for lo, hi in [(448 * k, 448 * k + 448) for k in range(4)] + [(NULL, WX)]:
-                act(("YO", lo, hi), ("XT", lo, hi), AF.Identity, bias=UNC)
-        moves(t, "AB")
-        moves(t, "C")
-        leave(t, "C")
+            for k in range(4):
+                act(("YO", 448 * k, 448 * k + 448), ("XT", 448 * k, 448 * k + 448), AF.Identity, bias=UNC)
+        moves(t)
         if not last:
             ghosts(t + 1)
             requests(t)
@@ -608,8 +611,12 @@ def rank_program(g, core, T, topo):
             g.remote_dma(out, in_, T.sem[rsem], T.sem["ls"], pid, rid, topo.mask(core, to))
             total["ls"] = total.get("ls", 0) + count(topo.mask(core, to))
             continue
-        s, k = (what[0], 16) if kind == "dma" else ("s" + q, 1)
+        s, k = (what[0], 16) if kind == "dma" else ("go", 1) if kind == "inc" else ("s" + q, 1)
         total[s] = total.get(s, 0) + k
+        if kind == "inc":
+            g.sem_inc(T.sem[s], 1)
+            note(acc, s, reads, writes, (s, total[s]), {})
+            continue
         (queue[q].dma_start(what[1], what[2]) if kind == "dma" else what(queue[q])).then_inc(T.sem[s], k)
         note(acc, s if kind == "dma" else q, reads, writes, (s, total[s]), dict(clock[q]))
     for s in sorted(total):

from concourse.mybir import AluOpType, ActivationFunctionType, AxisListType

S, GH, CAP, RO = 1792, 384, 32, 4
NULL, WX, TRASH = 2944, 2960, 2960
MID = 1472.0
RATIO, TOP = 1.75, 2.0 ** 98
MAGIC = 1.5 * 2.0 ** 24
ROOM = 288
BLOCKS = [{"A": (0, 5), "B": (5, 5)}] + [{"A": (0, 8), "B": (8, 8)}] * 3
FUSED = {80: 32, 128: 40}
CUT = {80: 64, 128: 96}
PIECE = (16, 8, 16)
NB1, NOUT = 896, 2
LINE = ("RAW", "DA", "DB")
CYC, PCYC, DONE, WAKE, LOAD, NEAR, FAR, SMALL, LISTS = 0.00083, 0.00042, 0.1, 0.1, 1.9, 4.0, 6.5, 1.0, 10.0
OP = AluOpType
AF = ActivationFunctionType
SIZES = {
    "bfloat16": "XR 1792,XT 3584,YO 3584,EIN 2960,PUL 512,PUT 2960,VC 256,MSK 640,RAW 3072,EXP 2048,ONE 768,EQ 4096,PRB 1024,IDB 128,"
                "IDK 128,GM 128,GQ 2048,GGK 128,WZ 16,ZER 64,DQ 32,XD 256,VAL 512,STL 16,RW 128,LB 16,IND 256,GS 4608,LG 4608,RG 1536",
    "float16": "ZSA 2048,ZSB 2048,DA 2048,DB 2048,SB 1280,BSA 128,BSB 128,STA 128,STB 128,EA 128,EB 128,RD 16,RS 256,RE 128,WY 16,"
               "PRW 2048,DL 16,QC 256,DBC 256",
    "float32": "IOT 2960,REQ 1424,REP 128,COL 80,GG 16,TMF 128,NN 128,WC 32,M 256,RA 136,RB 136,KQ 128,DN 16,KD 128,SD 32,INV 16,"
               "TV 256,TV2 256,THE 32,KL 128,LW 32,GV 256,RX 192,RQO 32,RIN 32,RRQ 32",
    "int32": "NBI 2960,WTI 8,WAN 40,WK 320,SND 72,SNL 72,CI 16,OL 128,KI 128,WI 256,FI 256,ZI 112,RSN 24",
    "uint16": "SNU 72,SLU 72,DG 8,RL 4,XL 4,OFA 16,OFB 16,OFX 16,ONA 128,ONB 128,DOF 16,OFS 32,RQF 16",
}
SCRATCH = {}
for _d, _l in SIZES.items():
    for _x in _l.split(","):
        SCRATCH[_x.split()[0]] = ("sbuf", [128, int(_x.split()[1])], _d)
BANKS = ("PA", "PB", "X0", "X1", "X2", "PT", "PM", "PM2")
for _x in BANKS:
    SCRATCH[_x] = ("psum", [128, 512], "float32")
SEMAPHORES = (["sV", "sS", "sP", "sG", "ls", "rs", "go"] + ["ld%d" % i for i in range(8)] + ["st%d" % i for i in range(4)]
              + ["ga%d_%d" % (e, t) for e in (1, 2, 3) for t in range(4)] + ["rq%d_%d" % (e, t) for e in (1, 2, 3) for t in (1, 2, 3)]
              + ["sn%d" % e for e in (1, 2, 3)] + ["rg%d" % t for t in range(4)] + ["rr%d" % t for t in (1, 2, 3)])


def routes(T, topo):
    n = len(T.cores)
    rel = {}
    for r in range(n):
        c = T.cores[r]
        near = True
        for e in range(1, n):
            d = (r + e) % n
            if topo.may_write(c, T.cores[d]):
                rel[(r, d)] = None
                continue
            cand = [k for k in topo.cores_of(c) if k != c and topo.may_write(k, T.cores[d]) and topo.may_write(c, k)]
            pick = [k for k in cand if (topo.die(k) == topo.die(c)) == near] or cand
            rel[(r, d)] = pick[0]
            near = False
    return rel


def count(m):
    return bin(m).count("1")


def relay_program(g, core, T, topo, r, d):
    n = len(T.cores)
    src, dst = T.cores[r], T.cores[d]
    e, eq = (d - r) % n, (r - d) % n
    k_in, m = count(topo.mask(src, core)), topo.mask(core, dst)
    rid, pid = topo.addr(dst, core)

    def on(sem, out, in_, rsem):
        g.wait_ge(T.sem[sem], k_in)
        g.remote_dma(out, in_, T.sem[rsem], T.sem["ls"], pid, rid, m)
    on("rs", T["SNL"][:, (e - 1) * 24:e * 24], T["RSN"][:, 0:24], "sn%d" % e)
    for t in range(RO):
        on("rg%d" % t, T["LG"][:, t * 1152 + (e - 1) * GH:t * 1152 + e * GH], T["RG"][:, t * GH:(t + 1) * GH], "ga%d_%d" % (e, t))
        if t:
            on("rr%d" % t, T["RIN"][:, t * 8 + 2 * (eq - 1):t * 8 + 2 * eq], T["RRQ"][:, t * 8:t * 8 + 2], "rq%d_%d" % (eq, t))
    g.wait_ge(T.sem["ls"], 2 * RO * count(m))


def span(s):
    return (s[0], 0, 512) if s[0] in BANKS else (s[0], s[1], s[2])


def meets(acc, q, reads, writes, adds):
    out = []
    for w, lst in ((False, reads), (True, writes)):
        for s in lst:
            b, lo, hi = span(s)
            for a in acc.get(b, []):
                if a[0] < hi and lo < a[1] and (w or a[2] or b in BANKS and a[3] != q):
                    out.append((a, not (a[3] == q == "P" and (adds or a[-1][2] <= s[1] or s[2] <= a[-1][1]))))
    return out


def note(acc, q, reads, writes, *more):
    for w, lst in ((False, reads), (True, writes)):
        for s in lst:
            b, lo, hi = span(s)
            old = acc.setdefault(b, [])
            if w:
                old[:] = [a for a in old if not (lo <= a[0] and a[1] <= hi and len(s) < 4)]
            old.append([lo, hi, w, q] + list(more) + [s])


def issue_order(calls):
    acc, left, post = {}, [], [{} for c in calls]
    for i, c in enumerate(calls):
        p = {j: calls[j][0] != c[0] for j in c[5]}
        for a, done in meets(acc, c[0], c[3], c[4], c[6] == "add"):
            p[a[4]] = p.get(a[4], False) or done
        for j, done in p.items():
            post[j][i] = calls[j][2] + DONE if done else 0.0
        left.append(len(p))
        note(acc, c[0], c[3], c[4], i)
    way, line = [0.0] * len(calls), {}
    for i in reversed(range(len(calls))):
        way[i] = calls[i][1] + max([way[k] + w + (WAKE if w else 0.0) for k, w in post[i].items()] + [calls[i][2]])
        if calls[i][4] and calls[i][4][0][0] in LINE:
            way[i] = line[calls[i][0]] = max(way[i], calls[i][1] + line.get(calls[i][0], 0.0))
    ready, free, pool, order = [0.0] * len(calls), {}, {}, []
    for i, c in enumerate(calls):
        if not left[i]:
            pool.setdefault(c[0], []).append(i)
    for k in calls:
        at, q = min((max(free.get(q, 0.0), min(ready[i] for i in lst)), q) for q, lst in pool.items() if lst)
        i = max((i for i in pool[q] if ready[i] <= at), key=lambda i: (way[i], -i))
        pool[q].remove(i)
        order.append(i)
        free[q] = (at if ready[i] <= free.get(q, 0.0) else at + WAKE) + calls[i][1]
        for j, w in post[i].items():
            ready[j] = max(ready[j], free[q] + w)
            left[j] -= 1
            if not left[j]:
                pool.setdefault(calls[j][0], []).append(j)
    return order


def rank_program(g, core, T, topo):
    rel = routes(T, topo)
    rank = T.rank_of(core)
    if rank is None:
        for (r, d), k in rel.items():
            if k == core:
                relay_program(g, core, T, topo, r, d)
        return
    n = len(T.cores)
    queue = {"V": g.vector, "S": g.scalar, "P": g.tensor, "G": g, "Y": g.sync}
    calls = []

    def last_of(kind, q, k=1):
        return [i for i, c in enumerate(calls) if c[6] == kind and c[0] == q][-k:]

    def do(q, cost, fn, reads, writes):
        calls.append([q, cost, 0.0, reads, writes, [], "do", fn])

    def dma(q, sem, out, in_, reads, writes, after):
        calls.append([q, 0.05, after, reads, writes, last_of("dma", q), "dma", (sem, out, in_)])

    def ap(s):
        if s[0] == "I":
            return ap(s[1]).indirect(ap(s[2]))
        rows = slice(s[5] if len(s) > 5 else 0, s[4]) if len(s) > 4 else slice(None)
        return T[s[0]][rows, s[1]:s[2]:s[3]] if len(s) > 3 and s[3] > 1 else T[s[0]][rows, s[1]:s[2]]

    def rd(*ss):
        out = []
        for s in ss:
            if isinstance(s, tuple):
                out += [s[1], s[2]] if s[0] == "I" else [s]
        return out

    def wr(s):
        return [s[1]] if s[0] == "I" else [s]

    def val(s):
        return ap(s) if isinstance(s, tuple) else s

    def size(s):
        return -(-(s[2] - s[1]) // (s[3] if len(s) > 3 else 1))

    def cost(rate, out, *ins):
        if out[0] == "I":
            return 0.05 + 3.8 * CYC * size(ins[0])
        if ins and ins[0][0] == "I":
            return 0.06 + 1.56 * CYC * size(out)
        if rate == 0:
            rate = 0.5 if all(SCRATCH[s[0]][2].endswith("16") for s in (out,) + ins) else 1
        return max(64, rate * size(out)) * CYC

    def tt(out, a, b, op):
        do("V", cost(1 if a[0] in BANKS or b[0] in BANKS else 2, out, a), lambda v: v.tensor_tensor(ap(out), ap(a), ap(b), op), rd(a, b), wr(out))

    def ts(out, a, s1, op0, s2=None, op1=None):
        if op1 is None:
            do("V", cost(0, out, a), lambda v: v.tensor_scalar(ap(out), ap(a), val(s1), None, op0), rd(a, s1), wr(out))
        else:
            do("V", cost(0, out, a), lambda v: v.tensor_scalar(ap(out), ap(a), val(s1), val(s2), op0, op1), rd(a, s1, s2), wr(out))

    def cp(out, a):
        do("V", cost(0, out, a), lambda v: v.tensor_copy(ap(out), ap(a)), rd(a) + (rd(out)[1:] if out[0] == "I" else []), wr(out))

    def scan(out, d0, d1, op0, op1, first=0.0):
        do("V", cost(0, out, d0, d1), lambda v: v.tensor_tensor_scan(ap(out), ap(d0), ap(d1), val(first), op0, op1), rd(d0, d1, first), wr(out))

    def fill(out, c):
        do("V", cost(0, out), lambda v: v.memset(ap(out), c), [], wr(out))

    def act(out, a, func=AF.Copy, **kw):
        do("S", cost(1, out, a), lambda s: s.activation(ap(out), ap(a), func, **{k: val(x) for k, x in kw.items()}), rd(a, *kw.values()), wr(out))

    def zero(out):
        act(out, ("ONE", 0, size(out)), AF.Identity, scale=0.0)

    def mm(out, l, r, start, stop):
        c = max(min(64, size(l)), size(r)) * PCYC * (4 if SCRATCH[l[0]][2] == "float32" else 1)
        calls.append(["P", c, 0.0, rd(l, r), wr(out), [], "do" if start else "add", lambda p: p.matmul(ap(out), ap(l), ap(r), start, stop)])

    def iota(out, pat, base=0, cm=0):
        kw = {} if SCRATCH[out[0]][2] == "int32" else {"allow_small_or_imprecise_dtypes": True}
        do("G", 0.13 + 2 * CYC * size(out), lambda q: q.iota(ap(out), pat, base, cm, **kw), [], wr(out))

    def pick(out, a, pat, base):
        do("G", 0.17 + 2 * CYC * size(out), lambda q: q.affine_select(ap(out), ap(a), pat, OP.is_equal, 0.0, base, 1), rd(a), wr(out))

    def send(in_, kind, e, t):
        at, sem, at2, sem2 = {"g": (("LG", t * 1152 + (e - 1) * GH, GH), "ga%d_%d" % (e, t), ("RG", t * GH), "rg%d" % t),
                              "s": (("SNL", (e - 1) * 24, 24), "sn%d" % e, ("RSN", 0), "rs"),
                              "q": (("RIN", t * 8 + 2 * (e - 1), 2), "rq%d_%d" % (e, t), ("RRQ", t * 8), "rr%d" % t)}[kind]
        sign = -1 if kind == "q" else 1
        d, src = (rank + sign * e) % n, (rank - sign * e) % n
        k = rel[(rank, d)]
        to, out, rsem = (T.cores[d], at, sem) if k is None else (k, at2, sem2)
        calls.append(["G", 0.3, 0.0, [in_], [], last_of("send", "G") or last_of("do", "G", 9), "send",
                      (T[out[0]][:, out[1]:out[1] + at[2]], ap(in_), rsem, to)])
        k = rel[(src, rank)]
        due = count(topo.mask(T.cores[src] if k is None else k, core))
        way = {"g": NEAR if k is None else FAR, "q": NEAR - SMALL if k is None else FAR - 2 * SMALL, "s": LISTS}[kind]
        calls.append(["in" + sem, 0.0, way, [], [(at[0], at[1], at[1] + at[2])], [len(calls) - 1], "lands", (sem, due)])

    def col(i):
        return ("COL", i, i + 1)

    def ci(i):
        return ("CI", i, i + 1)

    (QF, GF, N15, I15, I0, CEN, UNC, EPS, M15, HLF, QR, TH, SB0, SB3, WTF, PF, Q8, QW, EMP) = [col(i) for i in range(19)]
    NVB = [col(20 + t) for t in range(RO)]
    THR = {c0: col(24 + k) for k, c0 in enumerate(sorted({c0 for b in BLOCKS for c0, nc in b.values()}))}
    widths = {w for b in BLOCKS for w in (b["A"][1], b["B"][1], sum(b["B"]))}
    DGA = {nc: 2 * k for k, nc in enumerate(sorted(widths))}
    WIN, OWN, NBW = ("XT", 0, WX), ("XT", 0, S), ("NBI", 0, WX)
    GM, GG = ("GM", 0, 128), ("GG", 0, 8)
    far = [e for e in (1, 2, 3) if rel[(rank, (rank + e) % n)] is not None]
    far_first = far + [e for e in (1, 2, 3) if e not in far]
    mark = []

    dma("Y", "ld0", T["XR"][:, :], T.x0[:, :], [], [("XR", 0, S)], LOAD + 1.5)
    dma("S", "ld1", T["SND"][:, :], T.snd[:, :], [], [("SND", 0, 72)], LOAD)
    dma("Y", "ld3", T["WAN"][:, :], T.wants[:, :], [], [("WAN", 0, 40)], LOAD + 1.7)
    dma("Y", "ld2", T["NBI"][:, 0:NB1], T.nb[:, 0:NB1], [], [("NBI", 0, NB1)], LOAD + 1.7 + 2.7 * NB1 / S)

    iota(ci(0), [[1, 1]], 0, 1)
    iota(("TMF", 0, 128), [[1, 8], [0, 16]])
    iota(("NN", 0, 128), [[0, 8], [1, 16]])
    iota(("GGK", 0, 128), [[0, 16], [1, 8]])
    fill(("ONE", 0, 768), 1.0)
    pick(("IDB", 0, 128), ("ONE", 0, 128), [[-1, 128]], 0)
    ts(ci(1), ci(0), 15, OP.bitwise_and)
    ts(ci(2), ci(0), 4, OP.logical_shift_right)
    fill(("XT", NULL, WX), 0.0)
    cp(QF, ci(1))
    cp(GF, ci(2))
    cp(PF, ci(0))
    fill(("ZER", 0, 64), 0.0)
    ts(N15, QF, 15.0, OP.is_lt)
    ts(I15, QF, 15.0, OP.is_equal)
    ts(I0, QF, 0.0, OP.is_equal)
    ts(CEN, N15, -127.5, OP.mult)
    ts(UNC, N15, 127.5, OP.mult)
    ts(EPS, N15, -0.0625, OP.mult)
    ts(M15, I15, -1.0, OP.mult)
    ts(HLF, N15, 0.5, OP.mult)
    ts(SB0, N15, 1.0625, OP.mult, -1.0, OP.add)
    ts(SB3, N15, 128.5625, OP.mult, -1.0, OP.add)
    for t in range(RO):
        ts(NVB[t], I15, 192.0 + t, OP.mult, CEN if t + 1 < RO else 0.0, OP.add)
    ts(GM, ("TMF", 0, 128), GF, OP.is_equal)
    ts(("GGK", 0, 128), ("GGK", 0, 128), GF, OP.is_equal)
    cp(GG, ("GGK", 0, 8))
    for x in "AB":
        zero(("ZS" + x, 0, 640))
        zero(("R" + x, 0, 136))
    fill(("STL", 0, 16), 0.0)
    for e in far_first:
        send(("SND", (e - 1) * 24, e * 24), "s", e, 0)
    iota(("NBI", S, S + 448), [[1, 448]], S)
    calls[-1][5] = last_of("send", "G")
    cp(("SNU", 0, 72), ("SND", 0, 72))
    ts(("RD", 0, 8), GG, N15, OP.mult, 16384.0, OP.mult)
    ts(("RD", 8, 16), GG, I15, OP.mult, 4.25, OP.mult)
    ts(("RS", 0, 128), GM, N15, OP.mult, -16384.0, OP.mult)
    ts(("RS", 128, 256), GM, I15, OP.mult, -4.25, OP.mult)
    ts(("M", 0, 128), ("NN", 0, 128), -0.25, OP.mult, MID / 16384.0 - 0.25, OP.add)
    ts(EMP, I15, -1024.0, OP.mult)
    ts(("TV", 0, 128), ("M", 0, 128), I0, OP.mult, EMP, OP.add)
    tt(("RE", 0, 128), ("TV", 0, 128), GM, OP.mult)
    ts(("IDK", 0, 128), ("IDB", 0, 128), 1.0 / 16384.0, OP.mult)
    ts(("REP", 0, 128), ("NN", 0, 128), QF, OP.is_equal, 16384.0, OP.mult)
    mm(("PM", 0, 64), ("IDB", 0, 128), ("ZER", 0, 64), True, True)
    ts(("MSK", 0, 128), ("NN", 0, 128), 0.5, OP.is_gt)
    for lo, hi in ((128, 256), (256, 512), (512, 640)):
        cp(("MSK", lo, hi), ("MSK", 0, hi - lo))
    ts(("DQ", 0, 32), ("NN", 0, 32), QF, OP.is_equal)

    def ghosts(t):
        at = t * 1152
        for e in far_first:
            a, b, c = (e - 1) * GH, (e - 1) * GH + GH // 2, e * GH
            if t:
                act(("GS", at + a, at + b), ("I", OWN, ("SNU", a // 16, b // 16)))
                cp(("GS", at + b, at + c), ("I", OWN, ("SNU", b // 16, c // 16)))
            else:
                act(("GS", a, b), ("I", ("XR", 0, S), ("SNU", a // 16, b // 16)), AF.Identity, bias=CEN)
                ts(("GS", b, c), ("I", ("XR", 0, S), ("SNU", b // 16, c // 16)), CEN, OP.add)
            if e in far:
                mark[:] = last_of("do", "V")
            send(("GS", at + a, at + c), "g", e, t)

    ghosts(0)
    calls.append(["G", 0.0, 0.0, [], [("go", 0, 1)], last_of("send", "G"), "inc", None])
    dma("Y", "ld6", T["NBI"][:, NB1:S], T.nb[:, NB1:S], [("go", 0, 1)], [("NBI", NB1, S)], LOAD + 1.5 + 2.7 * (S - NB1) / S)
    dma("Y", "ld4", T["WTI"][:, 0:1], T.wt[:, :], [], [("WTI", 0, 1)], LOAD + 3.0)
    dma("Y", "ld5", T["PUL"][:, :], T.pull[:, :], [], [("PUL", 0, 512)], LOAD + 3.5)
    late = len(calls)
    iota(("NBI", S + 448, WX), [[1, WX - S - 448]], S + 448)
    for k in range(4):
        pick(("EXP", 512 * k, 512 * k + 512), ("ONE", 0, 512), [[-1, 32], [0, 16]], -32 * k)
    for k in (0, 1):
        pick(("PRB", 512 * k, 512 * k + 512), ("ONE", 0, 512), [[-16, 4], [0, 8], [-1, 16]], -64 * k)
    for k in range(4):
        iota(("IOT", 448 * k, 448 * k + 448), [[1, 448]], 448 * k)
    iota(("IOT", NULL, WX), [[1, WX - NULL]], NULL)
    for k in range(8):
        iota(("EQ", 512 * k, 512 * k + 512), [[0, 512]])
    for c in calls[late:]:
        c[5] = last_of("send", "G")
    for k in range(4):
        ts(("XT", 448 * k, 448 * k + 448), ("XR", 448 * k, 448 * k + 448), CEN, OP.add)
    for k in range(8):
        cp(("WK", k, 320, 8), ("WAN", 0, 40))
    for k, (nc, at) in enumerate(DGA.items()):
        ts(col(64 + k), QF, float(nc - 1), OP.min, 8.0, OP.mult)
        for j in (0, 1):
            ts(("DG", at + j, at + j + 1), col(64 + k), GF, OP.add)
    ts(Q8, QF, 8.0, OP.is_ge)
    ts(col(56), Q8, -8.0, OP.mult, QF, OP.add)
    ts(col(57), col(56), 16.0, OP.mult, 15.0 - 128.0, OP.add)
    tt(col(58), GF, Q8, OP.subtract)
    for k in range(4):
        ts(("RL", k, k + 1), Q8, 2.0 * k, OP.add)
        ts(col(59 + k), col(58), 2.0 * k, OP.is_equal, col(57), OP.mult)
        ts(("XL", k, k + 1), col(59 + k), 128.0, OP.add)
    cp(WTF, ("WTI", 0, 1))
    ts(("WZ", 0, 8), GG, WTF, OP.mult, N15, OP.mult)
    ts(("WZ", 8, 16), GG, I15, OP.mult)
    ts(("WY", 0, 8), ("WZ", 0, 8), 128.0, OP.mult)
    ts(("WY", 8, 16), ("WZ", 0, 8), -0.4375, OP.mult)
    fill(QR, TOP)
    fill(("WC", 16, 32), RATIO ** -16)
    for k in range(4):
        ts(ci(8 + k), ci(1), k, OP.logical_shift_right, 1, OP.bitwise_and)
        ts(col(52 + k), ci(8 + k), RATIO ** -(2 ** k) - 1.0, OP.mult, 1.0, OP.add)
    for k in (0, 2):
        ts(QR, QR, col(52 + k), OP.mult, col(53 + k), OP.mult)
    ts(QR, QR, RATIO ** 16, OP.mult)
    scan(("WC", 0, 16), ("WC", 16, 32), ("ZER", 0, 16), OP.mult, OP.add, QR)
    ts(("THE", 0, 16), ("NN", 0, 16), GF, OP.is_equal)
    tt(("THE", 16, 32), ("THE", 0, 16), ("WC", 0, 16), OP.mult)
    do("V", 64 * CYC, lambda v: v.tensor_reduce(ap(TH), ap(("THE", 16, 32)), AxisListType.X, OP.add), [("THE", 16, 32)], [TH])
    for c0, k in THR.items():
        ts(k, TH, RATIO ** (-8 * c0), OP.mult, -2.54 * RATIO ** (-8 * c0), OP.mult)
    for b in range(2):
        ts(col(32 + b), PF, 2.0, OP.mult, TRASH + 256.0 * b, OP.add)
        for k in range(0, 1024, 256):
            act(("PRW", 1024 * b + k, 1024 * b + k + 256), ("PRB", k, k + 256), AF.Identity, scale=col(32 + b))
    ts(QW, QF, 1.0, OP.add, float(ROOM), OP.mult)
    for k in range(4):
        zero(("GQ", 512 * k, 512 * k + 512))
    for q in range(16):
        cp(("GQ", 129 * q, 128 * q + 128, 16), GG)
    for k in range(0, WX, 512):
        w = min(512, WX - k)
        ts(("PUT", k, k + w), ("PUL", 0, w), -1.0, OP.add)
    for e in (1, 2, 3, 4):
        ts(col(35 + e), QF, float(e - 1), OP.is_equal)
        for lo, hi in [(S + (e - 1) * GH, S + e * GH)] if e < 4 else [(448 * k, 448 * k + 448) for k in range(4)] + [(NULL, WX)]:
            act(("EIN", lo, hi), ("XR", 0, hi - lo), AF.Identity, scale=0.0, bias=col(35 + e))
    for e in (1, 2, 3):
        cp(("SLU", (e - 1) * 24, e * 24), ("SNL", (e - 1) * 24, e * 24))
        for k in (0, 1):
            lo = (e - 1) * GH + 192 * k
            act(("IOT", S + lo, S + lo + 192), ("I", ("IOT", 0, S), ("SLU", lo // 16, lo // 16 + 12)))

    def geo(t, x):
        c0, nc = BLOCKS[t][x]
        return "AB".index(x), c0, nc, 16 * nc

    def own(t, x, h, win):
        b, c0, nc, L = geo(t, x)
        ps, of, zs = "P" + x, ("OF" + x, 0, nc), ("ZS" + x, 0, 16 * L, 16)
        act(zs, ("I", win, of), AF.Identity, bias=EPS)
        cp(("ON" + x, 0, L), ("I", NBW, of))
        act(("BS" + x, 0, L), ("ON" + x, 0, L), AF.Identity, bias=-MID)
        mm((ps, 256, 384, 1, L), zs, ("IDB", 0, 128), True, True)
        act(("ST" + x, 0, 128, 1, L), (ps, 256, 384, 1, L))
        if h == 0:
            act(("E" + x, 0, L), zs, AF.Relu, scale=M15, bias=N15)
        mm((ps, 0, 256, 1, L), zs, ("RS", 0, 256), True, False)
        mm((ps, 128, 256, 1, L), ("E" + x, 0, L), ("RE", 0, 128), False, False)
        mm((ps, 128, 256, 1, L), ("BS" + x, 0, L), ("IDK", 0, 128), False, False)

    def start(t, x):
        b, c0, nc, L = geo(t, x)
        k = 6 if t and x == "A" else 0
        w = 10 * t + c0 + k - (6 if t else 0)
        if k:
            cp(("OFA", 0, k), ("RIN", 8 * t, 8 * t + k))
            calls[-1][5] = mark[:]
            cp(("OL", 0, 8 * k), ("I", ("RIN", 8 * t, 8 * t + k), ("RL", 0, k // 2)))
            calls[-1][5] = mark[:]
            cp(("OL", 8 * k, 8 * nc), ("WK", 8 * w, 8 * (w + nc - k)))
        cp(("OF" + x, k, nc), ("WAN", w, w + nc - k))
        own(t, x, 0, WIN if k else OWN)

    def look(t, x, par):
        b, c0, nc, L = geo(t, x)
        ps, a, sb = "P" + x, FUSED[L], 640 * b
        wi, fi, mi = [(k, 128 * b, 128 * b + 128, 1, L) for k in ("WI", "FI", "M")]
        scan(("SB", sb, sb + 16 * a), ("MSK", 0, 16 * a), ("ZS" + x, 0, 16 * a), OP.mult, OP.add)
        for l in range(0, a, PIECE[0]):
            m = min(l + PIECE[0], a)
            tt(("D" + x, 16 * l, 16 * m), ("I", WIN, ("ON" + x, l, m)), ("SB", sb + 16 * l, sb + 16 * m), OP.max)
        for k, l0 in enumerate(range(a, L, 32)):
            l1, at, bank = min(l0 + 32, L), 1536 * par + 512 * k, "X%d" % k
            for l in range(0, l1 - l0, PIECE[2]):
                m = min(l + PIECE[2], l1 - l0)
                act(("RAW", at + 16 * l, at + 16 * m), ("I", WIN, ("ON" + x, l0 + l, l0 + m)))
            mm((bank, 0, 16 * (l1 - l0)), ("ST" + x, 0, 128, 1, L), ("EXP", 16 * l0, 16 * l1, 1, L), True, True)
            for l in range(0, l1 - l0, PIECE[1]):
                m = min(l + PIECE[1], l1 - l0)
                tt(("D" + x, 16 * (l0 + l), 16 * (l0 + m)), ("RAW", at + 16 * l, at + 16 * m), (bank, 16 * l, 16 * m), OP.max)
        for l0, l1 in ((0, CUT[L]), (CUT[L], L)):
            for i in range(16):
                mm((ps, i, 256, 16, l1, l0), ("D" + x, 16 * l0 + i, 16 * l1, 16), ("RD", 0, 16), False, i == 15)
        ts(wi, (ps, 0, 128, 1, L), -15360.0, OP.add, 0.0, OP.max)
        ts(fi, wi, 15 * 1024, OP.bitwise_and)
        tt(mi, fi, (ps, 128, 256, 1, L), OP.min)
        scan(("R" + x, 0, 128, 1, L), ("MSK", 0, 128, 1, L), mi, OP.mult, OP.max)

    def step(t, x, h):
        b, c0, nc, L = geo(t, x)
        k, o = (nc + 1) // 2, 64 * b
        act(("KQ", o, o + 16 * k), ("I", ("R" + x, 0, 136), ("XL", 0, k)))
        mm(("PT", 0, 8 * nc), ("REP", 0, 128), ("KQ", o, o + 8 * nc), True, True)
        ol = ("OL", 8 * c0, 8 * (c0 + nc))
        w = 8 * (10 * t + c0 - (6 if t else 0))
        tt(("KI", o, o + 8 * nc), ("PT", 0, 8 * nc), ol if h or (t and x == "A") else ("WK", w, w + 8 * nc), OP.max)
        ts(ol, ("KI", o, o + 8 * nc), 4095, OP.bitwise_and)
        if h < 2:
            cp(("OF" + x, 0, 16), ("I", ol, ("DG", DGA[nc], DGA[nc] + 1)))
            own(t, x, h + 1, WIN)

    def each(t):
        return [(x,) + geo(t, x) for x in "AB"]

    def turn(t, mat, stride, src):
        for x, b, c0, nc, L in each(t):
            for c in range(nc):
                at = stride * b + 128 * c
                mm(("PM2", 8 * (c0 + c), 8 * (c0 + c) + 8), (mat, at, at + 128), (src, 8 * b, 8 * b + 8), True, True)

    def places(t):
        nt, last = sum(BLOCKS[t]["B"]), t + 1 == RO
        NL, dg, dof = 16 * nt, ("DG", DGA[nt], DGA[nt] + 1), ("DOF", 0, nt)
        for x, b, c0, nc, L in each(t):
            zs = ("ZS" + x, 0, 16 * L, 16)
            mm(("PM", 8 * b, 8 * b + 8, 1, L), zs, ("WZ", 0, 8), True, False)
            mm(("PM", 8 * b, 8 * b + 8, 1, L), ("E" + x, 0, L), ("WY", 0, 8), False, False)
            mm(("PM", 8 * b, 8 * b + 8, 1, L), ("E" + x, 0, L), ("WY", 8, 16), False, True)
            mm(("PM", 16 + 8 * b, 24 + 8 * b, 1, L), zs, ("WZ", 8, 16), True, True)
            act(("VAL", 256 + 16 * c0, 256 + 16 * c0 + L), zs, AF.Identity, scale=N15, bias=SB3 if last else SB0)
            if last:
                act(("VC", 16 * c0, 16 * c0 + L), zs, AF.Identity, scale=N15, bias=SB0)
        z = [("ZI", 16 * i, 16 * i + 16) for i in range(7)]
        cp(("SD", 16, 32), ("I", ("OL", 0, 8 * nt), dg))
        cp(z[0], ("PM", 0, 16))
        ts(z[1], z[0], 2047, OP.bitwise_and)
        act(("DN", 0, 16), ("PM", 16, 32), AF.Relu, scale=-float(NULL))
        tt(z[2], z[1], z[1], OP.mult)
        if t:
            ts(z[3], z[2], float(97 * t * 32), OP.add)
        ts(z[4], z[3 if t else 2], 5, OP.logical_shift_right, 2047, OP.bitwise_and)
        ts(z[5], z[4], float(S), OP.is_ge, -float(S), OP.mult)
        tt(z[6], z[4], z[5], OP.add)
        tt(("DL", 0, 16), z[6], ("DN", 0, 16), OP.max)
        turn(t, "PRB", 0, "DL")
        act(("KD", 0, 8 * nt), ("PM2", 0, 8 * nt))
        ts(("INV", 0, 16), ("SD", 16, 32), float(S), OP.is_ge, float(NULL), OP.mult)
        tt(("SD", 0, 16), ("I", ("KD", 0, 8 * nt), dg), ("INV", 0, 16), OP.max)
        cp(("DOF", 0, 16), ("SD", 0, 16))
        act(("DBC", 0, NL), ("I", ("IOT", 0, WX), dof))
        for c in range(nt):
            ts(("EQ", c * 272, c * 256 + NL), ("DBC", 16 * c, NL), ("SD", c, c + 1), OP.is_equal, ("WC", c, c + 1), OP.mult)
        act(("XD", 0, NL), ("I", WIN, dof))
        for x, b, c0, nc, L in each(t):
            mm(("PM", 32 + 8 * b, 40 + 8 * b, 1, L), ("XD", 16 * c0, 16 * c0 + L), ("WZ", 8, 16), True, True)
        for x, b, c0, nc, L in each(t):
            act(("THE", 8 * b, 8 * b + 8), ("PM", 32 + 8 * b, 40 + 8 * b), AF.Relu, scale=THR[c0])
        tt(("TV", 0, NL), ("I", ("PUT", 0, WX), dof), ("VC", 0, NL) if last else ("VAL", 256, 256 + NL), OP.add)
        ts(("TV2", 0, NL), ("TV", 0, NL), MAGIC + 128.0, OP.add, -MAGIC, OP.add)
        act(("VAL", 0, NL), ("TV2", 0, NL), AF.Identity, scale=HLF, bias=NVB[t])

    def moves(t):
        nt = sum(BLOCKS[t]["B"])
        to = ("XT" if t + 1 < RO else "YO", 0, 3584)
        act(("STL", 8, 16, 1, geo(t, "B")[3]), ("RB", 15, 128, 16, geo(t, "B")[3]), AF.Relu, scale=-8.0, bias=1.0)
        ts(("STL", 0, 8, 1, geo(t, "A")[3]), ("RA", 15, 128, 16, geo(t, "A")[3]), 0.0, OP.is_equal)
        turn(t, "PRB", 0, "STL")
        tt(("RW", 0, 8 * nt), ("PM2", 0, 8 * nt), ("GGK", 0, 8 * nt), OP.mult)
        tt(("THE", 16, 32), ("THE", 0, 16), ("STL", 0, 16), OP.mult)
        for x, b, c0, nc, L in each(t):
            for c in range(c0 + nc):
                at = c * 256 + 16 * c0
                mm(("PM", 48 + 8 * b, 56 + 8 * b, 1, L), ("EQ", at, at + L), ("RW", 8 * c, 8 * c + 8), c == 0, c == c0 + nc - 1)
        tt(("LB", 0, 16), ("PM", 48, 64), ("THE", 16, 32), OP.is_ge)
        turn(t, "PRW", 1024, "LB")
        act(("KL", 0, 8 * nt), ("PM2", 0, 8 * nt))
        tt(("LW", 0, 32), ("I", ("KL", 0, 8 * nt), ("DG", DGA[nt], DGA[nt] + 2)), ("SD", 0, 32), OP.max)
        cp(("OFS", 0, 32), ("LW", 0, 32))
        for k in (0, 16):
            cp(("I", to, ("OFS", k, k + nt)), ("VAL", 16 * k, 16 * (k + nt)))

    def requests(t):
        nt = sum(BLOCKS[t]["B"])
        NL, of = 16 * nt, ("OFX", 0, nt)
        cp(("OFX", 0, 16), ("I", ("OL", 0, 8 * nt), ("DG", DGA[nt], DGA[nt] + 1)))
        act(("GV", 0, NL), ("I", ("IOT", 0, WX), of))
        for e in (1, 2, 3):
            act(("REQ", ROOM * e + 1, ROOM * e + 33), ("NN", 0, CAP), AF.Identity, scale=0.0, bias=float(NULL))
        act(("IND", 0, NL), ("I", ("EIN", 0, WX), of))
        scan(("PT", 128, 128 + NL), ("ONE", 0, NL), ("IND", 0, NL), OP.mult, OP.add, QW)
        tt(("QC", 0, NL), ("IND", 0, NL), ("PT", 128, 128 + NL), OP.mult)
        for q in range(16):
            mm(("PM2", 256, 256 + nt), ("GQ", 128 * q, 128 * q + 128), ("QC", q, NL, 16), q == 0, q == 15)
        cp(("RQF", 0, nt), ("PM2", 256, 256 + nt))
        cp(("I", ("REQ", 0, 1424), ("RQF", 0, nt)), ("GV", 0, NL))
        calls[-1][5] = mark[:]
        for e in (1, 2, 3):
            tt(("RX", 32 * e - 32, 32 * e), ("REQ", ROOM * e + 1, ROOM * e + 33), ("DQ", 0, CAP), OP.mult)
        scan(("RX", 96, 192), ("MSK", 0, 96), ("RX", 0, 96), OP.mult, OP.add)
        o = (t + 1) * 8
        cp(("RQO", o, o + 6), ("RX", 111, 192, 16))
        for e in far_first:
            send(("RQO", o + 2 * (e - 1), o + 2 * e), "q", e, t + 1)

    par = 0
    for t in range(RO):
        last = t + 1 == RO
        for e in (1, 2, 3):
            lo = (e - 1) * GH
            cp(("XT", S + lo, S + lo + GH), ("LG", t * 1152 + lo, t * 1152 + lo + GH))
        mark[:] = last_of("do", "V", 3)
        for x in "BA":
            start(t, x)
        for h in range(3):
            if h == 2:
                places(t)
            for x in "BA":
                look(t, x, par)
                par = 1 - par
                if h < 2 or not last:
                    step(t, x, h)
        if last:
            for k in range(4):
                act(("YO", 448 * k, 448 * k + 448), ("XT", 448 * k, 448 * k + 448), AF.Identity, bias=UNC)
        moves(t)
        if not last:
            ghosts(t + 1)
            requests(t)
    for k in range(NOUT):
        w = S // NOUT
        dma("YS"[k % 2], "st%d" % k, T.y[:, w * k:w * k + w], T["YO"][:, w * k:w * k + w], [("YO", w * k, w * k + w)], [], LOAD)

    clock = {k: {} for k in queue}
    total, acc = {}, {}
    for i in issue_order(calls):
        q, c1, c2, reads, writes, follows, kind, what = calls[i]
        if kind == "lands":
            total[what[0]] = what[1]
            note(acc, q, [], writes, what, {})
            continue
        for (s, v), ck in sorted(((a[4], a[5]) for a, done in meets(acc, q, reads, writes, kind == "add") if done), key=lambda x: -x[0][1]):
            if clock[q].get(s, 0) < v:
                queue[q].wait_ge(T.sem[s], v)
                clock[q][s] = v
                for a, b in ck.items():
                    clock[q][a] = max(clock[q].get(a, 0), b)
        if kind == "send":
            out, in_, rsem, to = what
            rid, pid = topo.addr(to, core)
            g.remote_dma(out, in_, T.sem[rsem], T.sem["ls"], pid, rid, topo.mask(core, to))
            total["ls"] = total.get("ls", 0) + count(topo.mask(core, to))
            continue
        s, k = (what[0], 16) if kind == "dma" else ("go", 1) if kind == "inc" else ("s" + q, 1)
        total[s] = total.get(s, 0) + k
        if kind == "inc":
            g.sem_inc(T.sem[s], 1)
            note(acc, s, reads, writes, (s, total[s]), {})
            continue
        (queue[q].dma_start(what[1], what[2]) if kind == "dma" else what(queue[q])).then_inc(T.sem[s], k)
        note(acc, s if kind == "dma" else q, reads, writes, (s, total[s]), dict(clock[q]))
    for s in sorted(total):
        if clock["G"].get(s, 0) < total[s]:
            g.wait_ge(T.sem[s], total[s])
